import numpy as np
import ml_dtypes


def mxq(x, axis, fmt="e4m3"):
    dtype, down = {"e4m3": (ml_dtypes.float8_e4m3fn, 7), "e5m2": (ml_dtypes.float8_e5m2, 14)}[fmt]
    v = np.moveaxis(np.asarray(x, np.float32).astype(ml_dtypes.bfloat16).astype(np.float64), axis, -1)
    blocks = v.reshape(v.shape[:-1] + (-1, 32))
    amax = np.abs(blocks).max(-1, keepdims=True)
    byte = np.maximum(np.where(amax > 0, np.frexp(amax)[1] - 1 + 127, 0) - down, 1)
    scale = np.exp2(byte - 127.0)
    codes = (blocks / scale).astype(np.float32).astype(dtype).astype(np.float64)
    return np.moveaxis((codes * scale).reshape(v.shape), -1, axis)


WIDE = False


def mx_kscale(k):
    if not WIDE:
        return np.ones(k)
    levels = np.array([10, -10, 5, -5, 0])
    if k % 512:
        return np.exp2(np.random.permutation(np.resize(levels, k // 32))).repeat(32)
    a = np.empty((k // 512, 16))
    for p in range(k // 512):
        a[p, :8] = np.random.permutation(np.resize(levels, 8))
        for g in range(8):
            far = levels[np.abs(levels - a[p, g]) >= 10]
            a[p, g + 8] = far[np.random.randint(len(far))]
    return np.exp2(a.ravel()).repeat(32)


def f64(x):
    return np.asarray(x).astype(np.float64)


def striped(idx):
    return np.tile(idx.reshape(-1, 16).T, (8, 1)).astype(np.uint16)


def unstriped(offs):
    return offs[:16].T.reshape(-1).astype(np.int64)


E2M1 = np.array([0.0, 0.5, 1.0, 1.5, 2.0, 3.0, 4.0, 6.0, -0.0, -0.5, -1.0, -1.5, -2.0, -3.0, -4.0, -6.0])


def pack_weight(w, fmt):
    k, n = w.shape
    w = f64(np.asarray(w, np.float32).astype(ml_dtypes.bfloat16)).reshape(k // 32, 32, n)
    amax = np.abs(w).max(1)
    if fmt == "e4m3":
        byte = np.frexp(amax)[1] - 1 + 127 - 7
    else:
        mant, ex = np.frexp(amax / 6.0)
        byte = np.where(mant > 0.5, ex, ex - 1) + 127
    byte = np.clip(np.where(amax > 0, byte, 1), 1, 254)
    scaled = (w * np.exp2(127.0 - byte)[:, None, :]).reshape(k, n).astype(np.float32)
    by_word = np.ascontiguousarray(scaled.reshape(k // 512, 128, 4, n).transpose(0, 1, 3, 2))
    if fmt == "e4m3":
        words = by_word.astype(ml_dtypes.float8_e4m3fn).view(np.uint8)
    else:
        c = by_word.astype(ml_dtypes.float4_e2m1fn).view(np.uint8) & 0xF
        words = (c[..., 0::2] | (c[..., 1::2] << 4)).reshape(k // 512, 128, 2 * n)
    return np.ascontiguousarray(words), np.ascontiguousarray(byte.astype(np.uint8).reshape(k // 512, 16, n))


def unpack_weight(words, scales, fmt):
    g, _, n = scales.shape
    words = np.ascontiguousarray(words).reshape(g, 128, n, -1)
    if fmt == "e4m3":
        vals = words.view(ml_dtypes.float8_e4m3fn).astype(np.float64)
    else:
        nib = np.empty((g, 128, n, 4), np.uint8)
        nib[..., 0::2] = words & 0xF
        nib[..., 1::2] = words >> 4
        vals = E2M1[nib]
    vals = vals * np.repeat(np.exp2(scales.astype(np.float64) - 127.0), 8, axis=1)[..., None]
    return vals.transpose(0, 1, 3, 2).reshape(g * 512, n)


def gelu(v):
    return 0.5 * v * (1.0 + np.tanh(np.sqrt(2.0 / np.pi) * (v + 0.044715 * v**3)))


K, H, N, T, S = 1024, 512, 384, 2048, 1024

def setup_inputs():
    n = np.random.standard_normal
    s = mx_kscale(K)[:, None]
    u = mx_kscale(H)[:, None]
    tab_words, tab_scales = pack_weight(n((K, T)) * s, "e4m3")
    w2_words, w2_scales = pack_weight(-0.7 * n((K, H)) / np.sqrt(K) / s, "e2m1")
    w3_words, w3_scales = pack_weight(1.2 * n((K, H)) / np.sqrt(K) / s * u.T, "e4m3")
    return {
        "tab_words": tab_words, "tab_scales": tab_scales,
        "offs": striped(np.random.permutation(T)[:S]),
        "offs2": striped(np.random.permutation(T)[:S]),
        "offs3": striped(np.random.permutation(T)[:S]),
        "w1": (0.7 * n((K, H)) / np.sqrt(K) / s).astype(np.float32),
        "w2_words": w2_words, "w2_scales": w2_scales,
        "w3_words": w3_words, "w3_scales": w3_scales,
        "wo": (1.5 * n((H, N)) / np.sqrt(H) / u).astype(np.float32),
        "b": (0.5 * n(N)).astype(np.float32),
    }

def reference(tab_words, tab_scales, offs, offs2, offs3, w1, w2_words, w2_scales, w3_words, w3_scales, wo, b):
    vi = unpack_weight(tab_words, tab_scales, "e4m3")[:, unstriped(offs)]
    vj = unpack_weight(tab_words, tab_scales, "e4m3")[:, unstriped(offs2)]
    vt = unpack_weight(tab_words, tab_scales, "e4m3")[:, unstriped(offs3)]
    w2 = unpack_weight(w2_words, w2_scales, "e2m1")
    w3 = unpack_weight(w3_words, w3_scales, "e4m3")
    d = mxq(f64(w1), 0, "e4m3").T @ vi + w2.T @ vj
    t = w3.T @ vt
    h = t / (1.0 + np.square(d))
    y = mxq(f64(wo), 0, "e4m3").T @ mxq(h, 0, "e4m3")
    return y + f64(b)[:, None]

@@ -1,0 +1,275 @@
+from contextlib import ExitStack
+
+import concourse.mybir as mybir
+
+K, H, N, T, S = 1024, 512, 384, 2048, 1024
+FLOPS = 2 * (3 * K * H + H * N) * S
+
+F32 = mybir.dt.float32
+BF16 = mybir.dt.bfloat16
+I32 = mybir.dt.int32
+U32 = mybir.dt.uint32
+U16 = mybir.dt.uint16
+U8 = mybir.dt.uint8
+FP8X4 = mybir.dt.float8_e4m3fn_x4
+FP4X4 = mybir.dt.float4_e2m1fn_x4
+ACT = mybir.ActivationFunctionType
+MULT = mybir.AluOpType.mult
+
+P = 128
+PASSES = K // 512
+SLICE = 256
+HALF = 128
+SLICES = S // SLICE
+N_TILES = N // P
+
+
+def tile_list_template_contact_readout_kernel(
+    tc, tab_words, tab_scales, offs, offs2, offs3, w1, w2_words, w2_scales, w3_words, w3_scales, wo, b, out
+):
+    nc = tc.nc
+    with ExitStack() as ctx:
+        keep = ctx.enter_context(tc.tile_pool(name="keep", bufs=1))
+        ring = ctx.enter_context(tc.tile_pool(name="ring", bufs=3))
+        acc_pool = ctx.enter_context(tc.psum_pool(name="acc_psum", bufs=5))
+        y_pool = ctx.enter_context(tc.psum_pool(name="y_psum", bufs=3))
+
+        lists = [keep.tile([P, S // 16], U16, name=f"list{u}") for u in range(3)]
+        tab_sc = keep.tile([P, T // 4], I32, name="tab_sc", align_bytes=64)
+        tab_w = keep.tile([P, PASSES, T], U32, name="tab_w", align_bytes=64)
+        w1_raw = [keep.tile([P, 4, H], F32, name=f"w1_raw{a}") for a in range(PASSES)]
+        w2_raw = keep.tile([P, PASSES, H // 2], I32, name="w2_raw")
+        w3_raw = keep.tile([P, PASSES, H], I32, name="w3_raw")
+        wsc_raw = keep.tile([P, PASSES, H // 4], I32, name="wsc_raw")
+        wo_raw = keep.tile([P, 4, N], F32, name="wo_raw")
+        bias = keep.tile([P, N_TILES], F32, name="bias")
+        v_sc = [keep.tile([P, S], U8, name=f"v_sc{u}", align_bytes=64) for u in range(3)]
+        v2_sc_pass1 = keep.tile([P, S // 4], I32, name="v2_sc_pass1", align_bytes=64)
+        warm_in = keep.tile([P, 1], F32, name="warm_in")
+        warm_out = keep.tile([P, 1], F32, name="warm_out")
+
+        nc.vector.memset(tab_sc[:], 0)
+        nc.gpsimd.memset(warm_in[:], 1.0)
+        nc.scalar.activation(warm_out[:], warm_in[:], ACT.Abs_reciprocal_sqrt)
+        nc.gpsimd.memset(wsc_raw[:], 0)
+        nc.gpsimd.memset(v2_sc_pass1[:], 0)
+
+        nc.sync.dma_start(lists[1][:], offs2)
+        for q in range(4):
+            nc.sync.dma_start(tab_sc[32 * q : 32 * q + 8, :], tab_scales[:, 4 * q : 4 * q + 4, :].bitcast(I32))
+        nc.sync.dma_start(lists[0][:], offs)
+        nc.sync.dma_start(lists[2][:], offs3)
+
+        def load_w1(a):
+            nc.sync.dma_start(w1_raw[a][:], w1[512 * a : 512 * (a + 1), :].rearrange("(p j) c -> p j c", j=4))
+
+        def load_weight_scales(row, scales):
+            for q in range(4):
+                nc.sync.dma_start(
+                    wsc_raw[32 * q + row : 32 * q + row + 4, :, :],
+                    scales[:, 4 * q : 4 * q + 4, :].rearrange("a r c -> r a c").bitcast(I32),
+                )
+
+        load_w1(0)
+        load_weight_scales(0, w2_scales)
+        nc.sync.dma_start(w2_raw[:], w2_words.rearrange("a p c -> p a c").bitcast(I32))
+        load_w1(1)
+        load_weight_scales(4, w3_scales)
+        nc.sync.dma_start(tab_w[:].bitcast(I32), tab_words.rearrange("a p t i -> p a (t i)").bitcast(I32))
+
+        def gather_scales(u):
+            nc.vector.tensor_copy(v_sc[u][:], tab_sc[:].bitcast(U8).indirect(lists[u][:]))
+
+        v_words = {}
+
+        def gather_words(u, a, first, count):
+            tile = keep.tile([P, count * SLICE], U32, name=f"v{u}_{a}_{first}", align_bytes=64)
+            cols = SLICE // 16
+            nc.vector.tensor_copy(tile[:], tab_w[:, a, :].indirect(lists[u][:, first * cols : (first + count) * cols]))
+            for s in range(count):
+                v_words[u, a, first + s] = tile[:, s * SLICE : (s + 1) * SLICE]
+
+        w1_codes = keep.tile([P, PASSES, H], U32, name="w1_codes", align_bytes=64)
+        w1_sc = keep.tile([P, PASSES, H], U8, name="w1_sc", align_bytes=64)
+        w1_bf = [keep.tile([P, 4 * H], BF16, name=f"w1_bf{a}", align_bytes=64) for a in range(PASSES)]
+
+        def round_w1(a):
+            src = w1_raw[a][:].rearrange("p j (g t i) -> p t g i j", t=4, i=8)
+            dst = w1_bf[a][:].rearrange("p (t g i j) -> p t g i j", t=4, i=8, j=4)
+            for t in range(4):
+                nc.scalar.copy(dst[:, t], src[:, t])
+
+        def quantise_w1(a):
+            nc.vector.quantize_mx(w1_codes[:, a, :].bitcast(FP8X4), w1_sc[:, a, :], w1_bf[a][:])
+
+        w2_codes = keep.tile([P, 4, PASSES, 2 * P], U8, name="w2_codes", align_bytes=64)
+        w3_codes = keep.tile([P, 4, PASSES, P], U32, name="w3_codes", align_bytes=64)
+        w_sc = keep.tile([P, 4, PASSES, P], U8, name="w_sc", align_bytes=64)
+
+        def reorder(dst, src, run):
+            nc.vector.tensor_copy(
+                dst[:].bitcast(I32).rearrange("p t a (g e) -> p t (a g) e", e=run),
+                src[:].rearrange("p a (g t e) -> p t (a g) e", t=4, e=run),
+            )
+
+        gather_scales(1)
+        nc.sync.dma_start(v2_sc_pass1[0:112, :], v_sc[1][4:116, :].bitcast(I32))
+        wo_rows = wo.rearrange("(g t i) n -> t g i n", t=4, i=8)
+        for t in range(4):
+            nc.sync.dma_start(wo_raw[:, t, :], wo_rows[t])
+        nc.sync.dma_start(w3_raw[:], w3_words.rearrange("a p c i -> p a (c i)").bitcast(I32))
+        with nc.allow_non_contiguous_dma(reason="one bias value a partition and output tile"):
+            nc.sync.dma_start(bias[:], b.rearrange("(c p) -> p c", p=P))
+
+        gather_scales(0)
+        round_w1(0)
+        round_w1(1)
+        gather_scales(2)
+        quantise_w1(0)
+        reorder(w2_codes, w2_raw, 4)
+        reorder(w_sc, wsc_raw, 2)
+
+        def moving_scale(u, a, cols):
+            if u == 1 and a == 1:
+                return v2_sc_pass1[:].bitcast(U8)[:, cols]
+            return v_sc[u][4 * a : P, cols]
+
+        damp = {}
+
+        def d_stage(s):
+            squares = []
+            for hf in range(SLICE // HALF):
+                local = slice(hf * HALF, (hf + 1) * HALF)
+                cols = slice(s * SLICE + hf * HALF, s * SLICE + (hf + 1) * HALF)
+                d = acc_pool.tile([P, 4, HALF], F32, name="acc")
+                for t in range(4):
+                    for a in range(PASSES):
+                        nc.tensor.matmul_mx(
+                            d[:, t, :],
+                            lhsT=w1_codes[:, a, t * P : (t + 1) * P].bitcast(FP8X4),
+                            lhsT_scale=w1_sc[:, a, t * P : (t + 1) * P],
+                            rhs=v_words[0, a, s][:, local].bitcast(FP8X4),
+                            rhs_scale=moving_scale(0, a, cols),
+                            start=(a == 0),
+                            stop=False,
+                        )
+                    for a in range(PASSES):
+                        nc.tensor.matmul_mx(
+                            d[:, t, :],
+                            lhsT=w2_codes[:, t, a, :].bitcast(FP4X4),
+                            lhsT_scale=w_sc[:, t, a, :],
+                            rhs=v_words[1, a, s][:, local].bitcast(FP8X4),
+                            rhs_scale=moving_scale(1, a, cols),
+                            start=False,
+                            stop=(a == PASSES - 1),
+                        )
+                sq = ring.tile([P, HALF, 4], F32, name="sq")
+                nc.scalar.activation(sq[:], d[:].rearrange("p t n -> p n t"), ACT.Square)
+                squares.append(sq)
+            roots = []
+            for sq in squares:
+                root = ring.tile([P, HALF, 4], F32, name="root")
+                nc.scalar.activation(root[:], sq[:], ACT.Abs_reciprocal_sqrt, bias=1.0)
+                roots.append(root)
+            for hf, root in enumerate(roots):
+                tile = keep.tile([P, HALF, 4], F32, name=f"damp{s}_{hf}")
+                nc.scalar.activation(tile[:], root[:], ACT.Square)
+                damp[s, hf] = tile
+
+        h_bf = [keep.tile([P, SLICE, 4], BF16, name=f"h_bf{s}", align_bytes=64) for s in range(SLICES)]
+
+        def h_stage(s, hf):
+            local = slice(hf * HALF, (hf + 1) * HALF)
+            cols = slice(s * SLICE + hf * HALF, s * SLICE + (hf + 1) * HALF)
+            tp = acc_pool.tile([P, 4, HALF], F32, name="acc")
+            for t in range(4):
+                for a in range(PASSES):
+                    nc.tensor.matmul_mx(
+                        tp[:, t, :],
+                        lhsT=w3_codes[:, t, a, :].bitcast(FP8X4),
+                        lhsT_scale=w_sc[4:P, t, a, :],
+                        rhs=v_words[2, a, s][:, local].bitcast(FP8X4),
+                        rhs_scale=moving_scale(2, a, cols),
+                        start=(a == 0),
+                        stop=(a == PASSES - 1),
+                    )
+            nc.vector.tensor_tensor(h_bf[s][:, local, :], tp[:].rearrange("p t n -> p n t"), damp[s, hf][:], MULT)
+
+        wo_bf = keep.tile([P, N, 4], BF16, name="wo_bf", align_bytes=64)
+        wo_codes = keep.tile([P, N], U32, name="wo_codes", align_bytes=64)
+        wo_sc = keep.tile([P, N], U8, name="wo_sc", align_bytes=64)
+
+        def round_wo():
+            nc.scalar.copy(wo_bf[:], wo_raw[:].rearrange("p t n -> p n t"))
+
+        def quantise_wo():
+            for cols in (slice(0, 256), slice(256, N)):
+                nc.vector.quantize_mx(
+                    wo_codes[:, cols].bitcast(FP8X4), wo_sc[:, cols], wo_bf[:, cols, :].rearrange("p n t -> p (n t)")
+                )
+
+        out_view = out.rearrange("(c p) j -> p c j", p=P)
+
+        def readout(s, lo, width, last=False):
+            name = f"{s}_{lo}"
+            h_codes = keep.tile([P, width], U32, name="h_codes" + name, align_bytes=64)
+            h_sc = keep.tile([P, width], U8, name="h_sc" + name, align_bytes=64)
+            nc.vector.quantize_mx(
+                h_codes[:].bitcast(FP8X4), h_sc[:], h_bf[s][:, lo : lo + width, :].rearrange("p n t -> p (n t)")
+            )
+            result = keep.tile([P, N_TILES, width], F32, name="result" + name)
+            for group in ((0, 1), (2,)):
+                y = y_pool.tile([P, len(group), width], F32, name="y")
+                for place, c in enumerate(group):
+                    nc.tensor.matmul_mx(
+                        y[:, place, :],
+                        lhsT=wo_codes[:, c * P : (c + 1) * P].bitcast(FP8X4),
+                        lhsT_scale=wo_sc[:, c * P : (c + 1) * P],
+                        rhs=h_codes[:].bitcast(FP8X4),
+                        rhs_scale=h_sc[:],
+                        start=True,
+                        stop=True,
+                    )
+                for place, c in enumerate(group):
+                    if last and c == 2:
+                        nc.vector.tensor_scalar_add(result[:, c, :], y[:, place, :], bias[:, c : c + 1])
+                    else:
+                        nc.scalar.activation(result[:, c, :], y[:, place, :], ACT.Identity, bias=bias[:, c : c + 1])
+            first = s * SLICE + lo
+            nc.sync.dma_start(out_view[:, :, first : first + width], result[:])
+
+        def d_gathers(first, count):
+            for a in range(PASSES):
+                gather_words(0, a, first, count)
+                gather_words(1, a, first, count)
+
+        def t_gathers(first, count):
+            for a in range(PASSES):
+                gather_words(2, a, first, count)
+
+        quantise_w1(1)
+        d_gathers(0, 1)
+        round_wo()
+        d_stage(0)
+        d_gathers(1, 1)
+        d_stage(1)
+        d_gathers(2, 2)
+        d_stage(2)
+        d_stage(3)
+        reorder(w3_codes, w3_raw, 8)
+        quantise_wo()
+        t_gathers(0, 1)
+        t_gathers(1, 3)
+        h_stage(0, 0)
+        h_stage(0, 1)
+        h_stage(1, 0)
+        readout(0, 0, SLICE)
+        h_stage(1, 1)
+        h_stage(2, 0)
+        readout(1, 0, SLICE)
+        h_stage(2, 1)
+        h_stage(3, 0)
+        readout(2, 0, SLICE)
+        h_stage(3, 1)
+        readout(3, 0, HALF)
+        readout(3, HALF, HALF, last=True)

@@ -30,7 +30,7 @@ def tile_list_template_contact_readout_kernel(
     nc = tc.nc
     with ExitStack() as ctx:
         keep = ctx.enter_context(tc.tile_pool(name="keep", bufs=1))
-        ring = ctx.enter_context(tc.tile_pool(name="ring", bufs=3))
+        ring = ctx.enter_context(tc.tile_pool(name="ring", bufs=4))
         acc_pool = ctx.enter_context(tc.psum_pool(name="acc_psum", bufs=5))
         y_pool = ctx.enter_context(tc.psum_pool(name="y_psum", bufs=3))
 
@@ -60,8 +60,9 @@ def tile_list_template_contact_readout_kernel(
         nc.sync.dma_start(lists[0][:], offs)
         nc.sync.dma_start(lists[2][:], offs3)
 
-        def load_w1(a):
-            nc.sync.dma_start(w1_raw[a][:], w1[512 * a : 512 * (a + 1), :].rearrange("(p j) c -> p j c", j=4))
+        def load_w1(a, cols):
+            rows = w1[512 * a : 512 * (a + 1), :].rearrange("(p j) c -> p j c", j=4)
+            nc.sync.dma_start(w1_raw[a][:, :, cols], rows[:, :, cols])
 
         def load_weight_scales(row, scales):
             for q in range(4):
@@ -70,12 +71,13 @@ def tile_list_template_contact_readout_kernel(
                     scales[:, 4 * q : 4 * q + 4, :].rearrange("a r c -> r a c").bitcast(I32),
                 )
 
-        load_w1(0)
-        load_weight_scales(0, w2_scales)
-        nc.sync.dma_start(w2_raw[:], w2_words.rearrange("a p c -> p a c").bitcast(I32))
-        load_w1(1)
-        load_weight_scales(4, w3_scales)
+        load_w1(0, slice(0, H))
         nc.sync.dma_start(tab_w[:].bitcast(I32), tab_words.rearrange("a p t i -> p a (t i)").bitcast(I32))
+        nc.sync.dma_start(w2_raw[:], w2_words.rearrange("a p c -> p a c").bitcast(I32))
+        load_w1(1, slice(0, H // 2))
+        load_weight_scales(0, w2_scales)
+        load_weight_scales(4, w3_scales)
+        load_w1(1, slice(H // 2, H))
 
         def gather_scales(u):
             nc.vector.tensor_copy(v_sc[u][:], tab_sc[:].bitcast(U8).indirect(lists[u][:]))
@@ -83,21 +85,22 @@ def tile_list_template_contact_readout_kernel(
         v_words = {}
 
         def gather_words(u, a, first, count):
-            tile = keep.tile([P, count * SLICE], U32, name=f"v{u}_{a}_{first}", align_bytes=64)
+            tile = picked[0 if first < 2 and u < 2 else 1][:, u, a, first * SLICE : (first + count) * SLICE]
             cols = SLICE // 16
-            nc.vector.tensor_copy(tile[:], tab_w[:, a, :].indirect(lists[u][:, first * cols : (first + count) * cols]))
+            nc.vector.tensor_copy(tile, tab_w[:, a, :].indirect(lists[u][:, first * cols : (first + count) * cols]))
             for s in range(count):
                 v_words[u, a, first + s] = tile[:, s * SLICE : (s + 1) * SLICE]
 
         w1_codes = keep.tile([P, PASSES, H], U32, name="w1_codes", align_bytes=64)
         w1_sc = keep.tile([P, PASSES, H], U8, name="w1_sc", align_bytes=64)
-        w1_bf = [keep.tile([P, 4 * H], BF16, name=f"w1_bf{a}", align_bytes=64) for a in range(PASSES)]
+        w1_bf = [keep.tile([P, 4 * H], BF16, name=f"w1_bf{a}", tag=f"w1_bf{a}", align_bytes=64) for a in range(PASSES)]
+        picked = [keep.tile([P, 2, PASSES, 2 * SLICE], U32, name="picked_first", align_bytes=64)]
 
-        def round_w1(a):
+        def round_w1(a, blocks):
             src = w1_raw[a][:].rearrange("p j (g t i) -> p t g i j", t=4, i=8)
             dst = w1_bf[a][:].rearrange("p (t g i j) -> p t g i j", t=4, i=8, j=4)
             for t in range(4):
-                nc.scalar.copy(dst[:, t], src[:, t])
+                nc.scalar.copy(dst[:, t, blocks], src[:, t, blocks])
 
         def quantise_w1(a):
             nc.vector.quantize_mx(w1_codes[:, a, :].bitcast(FP8X4), w1_sc[:, a, :], w1_bf[a][:])
@@ -122,8 +125,9 @@ def tile_list_template_contact_readout_kernel(
             nc.sync.dma_start(bias[:], b.rearrange("(c p) -> p c", p=P))
 
         gather_scales(0)
-        round_w1(0)
-        round_w1(1)
+        round_w1(0, slice(0, 16))
+        round_w1(1, slice(0, 8))
+        round_w1(1, slice(8, 16))
         gather_scales(2)
         quantise_w1(0)
         reorder(w2_codes, w2_raw, 4)
@@ -173,7 +177,7 @@ def tile_list_template_contact_readout_kernel(
                 roots.append(root)
             for hf, root in enumerate(roots):
                 tile = keep.tile([P, HALF, 4], F32, name=f"damp{s}_{hf}")
-                nc.scalar.activation(tile[:], root[:], ACT.Square)
+                nc.gpsimd.tensor_tensor(tile[:], root[:], root[:], MULT)
                 damp[s, hf] = tile
 
         h_bf = [keep.tile([P, SLICE, 4], BF16, name=f"h_bf{s}", align_bytes=64) for s in range(SLICES)]
@@ -247,11 +251,12 @@ def tile_list_template_contact_readout_kernel(
             for a in range(PASSES):
                 gather_words(2, a, first, count)
 
-        quantise_w1(1)
         d_gathers(0, 1)
+        d_gathers(1, 1)
+        quantise_w1(1)
+        picked.append(keep.tile([P, 3, PASSES, S], U32, name="picked_rest", tag="w1_bf1", align_bytes=64))
         round_wo()
         d_stage(0)
-        d_gathers(1, 1)
         d_stage(1)
         d_gathers(2, 2)
         d_stage(2)

@@ -17,11 +17,16 @@ ACT = mybir.ActivationFunctionType
 MULT = mybir.AluOpType.mult
 
 P = 128
-PASSES = K // 512
+PACK = 4
+PASSES = K // (P * PACK)
+BLOCKS = H // 32
 SLICE = 256
 HALF = 128
 SLICES = S // SLICE
+HALVES = SLICE // HALF
 N_TILES = N // P
+LOWER = 4
+FIRST, SECOND, TEMPLATE = 0, 1, 2
 
 
 def tile_list_template_contact_readout_kernel(
@@ -30,191 +35,152 @@ def tile_list_template_contact_readout_kernel(
     nc = tc.nc
     with ExitStack() as ctx:
         keep = ctx.enter_context(tc.tile_pool(name="keep", bufs=1))
-        ring = ctx.enter_context(tc.tile_pool(name="ring", bufs=4))
-        acc_pool = ctx.enter_context(tc.psum_pool(name="acc_psum", bufs=5))
-        y_pool = ctx.enter_context(tc.psum_pool(name="y_psum", bufs=3))
+        ring = ctx.enter_context(tc.tile_pool(name="ring", bufs=2 * HALVES))
+        psum = ctx.enter_context(tc.psum_pool(name="psum", bufs=8))
 
         lists = [keep.tile([P, S // 16], U16, name=f"list{u}") for u in range(3)]
-        tab_sc = keep.tile([P, T // 4], I32, name="tab_sc", align_bytes=64)
         tab_w = keep.tile([P, PASSES, T], U32, name="tab_w", align_bytes=64)
-        w1_raw = [keep.tile([P, 4, H], F32, name=f"w1_raw{a}") for a in range(PASSES)]
+        tab_sc = keep.tile([P, T // 4], I32, name="tab_sc", align_bytes=64)
+        w1_raw = [keep.tile([P, PACK, H], F32, name=f"w1_raw{a}", align_bytes=64) for a in range(PASSES)]
         w2_raw = keep.tile([P, PASSES, H // 2], I32, name="w2_raw")
-        w3_raw = keep.tile([P, PASSES, H], I32, name="w3_raw")
-        wsc_raw = keep.tile([P, PASSES, H // 4], I32, name="wsc_raw")
-        wo_raw = keep.tile([P, 4, N], F32, name="wo_raw")
+        w3_raw = keep.tile([P, PASSES, H], I32, name="w3_raw", tag="w3_raw", align_bytes=64)
+        w_sc_raw = keep.tile([P, PASSES, H // 4], I32, name="w_sc_raw")
+        wo_raw = keep.tile([P, PACK, N], F32, name="wo_raw")
         bias = keep.tile([P, N_TILES], F32, name="bias")
-        v_sc = [keep.tile([P, S], U8, name=f"v_sc{u}", align_bytes=64) for u in range(3)]
-        v2_sc_pass1 = keep.tile([P, S // 4], I32, name="v2_sc_pass1", align_bytes=64)
+        v_sc = {u: keep.tile([P, S], U8, name=f"v_sc{u}", align_bytes=64)[:] for u in (FIRST, SECOND)}
+        second_sc_pass1 = keep.tile([P, S // 4], I32, name="second_sc_pass1", align_bytes=64)
         warm_in = keep.tile([P, 1], F32, name="warm_in")
         warm_out = keep.tile([P, 1], F32, name="warm_out")
 
         nc.vector.memset(tab_sc[:], 0)
         nc.gpsimd.memset(warm_in[:], 1.0)
         nc.scalar.activation(warm_out[:], warm_in[:], ACT.Abs_reciprocal_sqrt)
-        nc.gpsimd.memset(wsc_raw[:], 0)
-        nc.gpsimd.memset(v2_sc_pass1[:], 0)
+        nc.gpsimd.memset(w_sc_raw[:], 0)
+        nc.gpsimd.memset(second_sc_pass1[:], 0)
 
-        nc.sync.dma_start(lists[1][:], offs2)
-        for q in range(4):
-            nc.sync.dma_start(tab_sc[32 * q : 32 * q + 8, :], tab_scales[:, 4 * q : 4 * q + 4, :].bitcast(I32))
-        nc.sync.dma_start(lists[0][:], offs)
-        nc.sync.dma_start(lists[2][:], offs3)
+        def load_table_words(a):
+            nc.sync.dma_start(tab_w[:, a, :].bitcast(I32), tab_words[a].rearrange("p t i -> p (t i)").bitcast(I32))
 
         def load_w1(a, cols):
-            rows = w1[512 * a : 512 * (a + 1), :].rearrange("(p j) c -> p j c", j=4)
+            rows = w1[a * P * PACK : (a + 1) * P * PACK, :].rearrange("(p i) c -> p i c", i=PACK)
             nc.sync.dma_start(w1_raw[a][:, :, cols], rows[:, :, cols])
 
-        def load_weight_scales(row, scales):
+        def load_weight_scales(scales, row):
             for q in range(4):
                 nc.sync.dma_start(
-                    wsc_raw[32 * q + row : 32 * q + row + 4, :, :],
+                    w_sc_raw[32 * q + row : 32 * q + row + 4, :, :],
                     scales[:, 4 * q : 4 * q + 4, :].rearrange("a r c -> r a c").bitcast(I32),
                 )
 
-        load_w1(0, slice(0, H))
-        nc.sync.dma_start(tab_w[:].bitcast(I32), tab_words.rearrange("a p t i -> p a (t i)").bitcast(I32))
-        nc.sync.dma_start(w2_raw[:], w2_words.rearrange("a p c -> p a c").bitcast(I32))
-        load_w1(1, slice(0, H // 2))
-        load_weight_scales(0, w2_scales)
-        load_weight_scales(4, w3_scales)
-        load_w1(1, slice(H // 2, H))
-
         def gather_scales(u):
-            nc.vector.tensor_copy(v_sc[u][:], tab_sc[:].bitcast(U8).indirect(lists[u][:]))
+            nc.vector.tensor_copy(v_sc[u], tab_sc[:].bitcast(U8).indirect(lists[u][:]))
 
         v_words = {}
 
-        def gather_words(u, a, first, count):
-            tile = picked[0 if first < 2 and u < 2 else 1][:, u, a, first * SLICE : (first + count) * SLICE]
+        def gather_words(room, u, a, first, count):
+            piece = room.pop(0)
             cols = SLICE // 16
-            nc.vector.tensor_copy(tile, tab_w[:, a, :].indirect(lists[u][:, first * cols : (first + count) * cols]))
+            nc.vector.tensor_copy(piece, tab_w[:, a, :].indirect(lists[u][:, first * cols : (first + count) * cols]))
             for s in range(count):
-                v_words[u, a, first + s] = tile[:, s * SLICE : (s + 1) * SLICE]
+                v_words[u, a, first + s] = piece[:, s * SLICE : (s + 1) * SLICE]
 
+        def make_room(name, tag, counts):
+            tile = keep.tile([P, sum(counts) * SLICE], U32, name=name, tag=tag, align_bytes=64)
+            ends = [sum(counts[:n]) * SLICE for n in range(len(counts) + 1)]
+            return [tile[:, lo:hi] for lo, hi in zip(ends, ends[1:])]
+
+        def moving_scale(u, a, cols):
+            if u == SECOND and a == 1:
+                return second_sc_pass1[:].bitcast(U8)[:, cols]
+            return v_sc[u][LOWER * a : P, cols]
+
+        w1_bf = [keep.tile([P, PACK * H], BF16, name=f"w1_bf{a}", tag=f"w1_bf{a}", align_bytes=64) for a in range(PASSES)]
         w1_codes = keep.tile([P, PASSES, H], U32, name="w1_codes", align_bytes=64)
         w1_sc = keep.tile([P, PASSES, H], U8, name="w1_sc", align_bytes=64)
-        w1_bf = [keep.tile([P, 4 * H], BF16, name=f"w1_bf{a}", tag=f"w1_bf{a}", align_bytes=64) for a in range(PASSES)]
-        picked = [keep.tile([P, 2, PASSES, 2 * SLICE], U32, name="picked_first", align_bytes=64)]
 
         def round_w1(a, blocks):
-            src = w1_raw[a][:].rearrange("p j (g t i) -> p t g i j", t=4, i=8)
-            dst = w1_bf[a][:].rearrange("p (t g i j) -> p t g i j", t=4, i=8, j=4)
-            for t in range(4):
+            src = w1_raw[a][:].rearrange("p j (g t i) -> p t g i j", t=PACK, i=8)
+            dst = w1_bf[a][:].rearrange("p (t g i j) -> p t g i j", t=PACK, i=8, j=PACK)
+            for t in range(PACK):
                 nc.scalar.copy(dst[:, t, blocks], src[:, t, blocks])
 
         def quantise_w1(a):
             nc.vector.quantize_mx(w1_codes[:, a, :].bitcast(FP8X4), w1_sc[:, a, :], w1_bf[a][:])
 
-        w2_codes = keep.tile([P, 4, PASSES, 2 * P], U8, name="w2_codes", align_bytes=64)
-        w3_codes = keep.tile([P, 4, PASSES, P], U32, name="w3_codes", align_bytes=64)
-        w_sc = keep.tile([P, 4, PASSES, P], U8, name="w_sc", align_bytes=64)
+        w2_codes = keep.tile([P, PACK, PASSES, 2 * P], U8, name="w2_codes", align_bytes=64)
+        w3_codes = keep.tile([P, PACK, PASSES, P], U32, name="w3_codes", align_bytes=64)
+        w_sc = keep.tile([P, PACK, PASSES, P], U8, name="w_sc", align_bytes=64)
 
         def reorder(dst, src, run):
             nc.vector.tensor_copy(
                 dst[:].bitcast(I32).rearrange("p t a (g e) -> p t (a g) e", e=run),
-                src[:].rearrange("p a (g t e) -> p t (a g) e", t=4, e=run),
+                src[:].rearrange("p a (g t e) -> p t (a g) e", t=PACK, e=run),
             )
 
-        gather_scales(1)
-        nc.sync.dma_start(v2_sc_pass1[0:112, :], v_sc[1][4:116, :].bitcast(I32))
-        wo_rows = wo.rearrange("(g t i) n -> t g i n", t=4, i=8)
-        for t in range(4):
-            nc.sync.dma_start(wo_raw[:, t, :], wo_rows[t])
-        nc.sync.dma_start(w3_raw[:], w3_words.rearrange("a p c i -> p a (c i)").bitcast(I32))
-        with nc.allow_non_contiguous_dma(reason="one bias value a partition and output tile"):
-            nc.sync.dma_start(bias[:], b.rearrange("(c p) -> p c", p=P))
-
-        gather_scales(0)
-        round_w1(0, slice(0, 16))
-        round_w1(1, slice(0, 8))
-        round_w1(1, slice(8, 16))
-        gather_scales(2)
-        quantise_w1(0)
-        reorder(w2_codes, w2_raw, 4)
-        reorder(w_sc, wsc_raw, 2)
-
-        def moving_scale(u, a, cols):
-            if u == 1 and a == 1:
-                return v2_sc_pass1[:].bitcast(U8)[:, cols]
-            return v_sc[u][4 * a : P, cols]
+        wo_bf = keep.tile([P, N, PACK], BF16, name="wo_bf", align_bytes=64)
+        wo_codes = keep.tile([P, N], U32, name="wo_codes", align_bytes=64)
+        wo_sc = keep.tile([P, N], U8, name="wo_sc", align_bytes=64)
 
         damp = {}
 
         def d_stage(s):
             squares = []
-            for hf in range(SLICE // HALF):
+            for hf in range(HALVES):
                 local = slice(hf * HALF, (hf + 1) * HALF)
                 cols = slice(s * SLICE + hf * HALF, s * SLICE + (hf + 1) * HALF)
-                d = acc_pool.tile([P, 4, HALF], F32, name="acc")
-                for t in range(4):
-                    for a in range(PASSES):
+                d = psum.tile([P, PACK, HALF], F32, name="bank")
+                order = ((FIRST, 0), (SECOND, 0), (SECOND, 1), (FIRST, 1))
+                for t in range(PACK):
+                    for u, a in order:
+                        if u == FIRST:
+                            codes = w1_codes[:, a, t * P : (t + 1) * P].bitcast(FP8X4)
+                            scale = w1_sc[:, a, t * P : (t + 1) * P]
+                        else:
+                            codes = w2_codes[:, t, a, :].bitcast(FP4X4)
+                            scale = w_sc[:, t, a, :]
                         nc.tensor.matmul_mx(
                             d[:, t, :],
-                            lhsT=w1_codes[:, a, t * P : (t + 1) * P].bitcast(FP8X4),
-                            lhsT_scale=w1_sc[:, a, t * P : (t + 1) * P],
-                            rhs=v_words[0, a, s][:, local].bitcast(FP8X4),
-                            rhs_scale=moving_scale(0, a, cols),
-                            start=(a == 0),
-                            stop=False,
+                            lhsT=codes,
+                            lhsT_scale=scale,
+                            rhs=v_words[u, a, s][:, local].bitcast(FP8X4),
+                            rhs_scale=moving_scale(u, a, cols),
+                            start=((u, a) == order[0]),
+                            stop=((u, a) == order[-1]),
                         )
-                    for a in range(PASSES):
-                        nc.tensor.matmul_mx(
-                            d[:, t, :],
-                            lhsT=w2_codes[:, t, a, :].bitcast(FP4X4),
-                            lhsT_scale=w_sc[:, t, a, :],
-                            rhs=v_words[1, a, s][:, local].bitcast(FP8X4),
-                            rhs_scale=moving_scale(1, a, cols),
-                            start=False,
-                            stop=(a == PASSES - 1),
-                        )
-                sq = ring.tile([P, HALF, 4], F32, name="sq")
-                nc.scalar.activation(sq[:], d[:].rearrange("p t n -> p n t"), ACT.Square)
-                squares.append(sq)
+                square = ring.tile([P, HALF, PACK], F32, name="square")
+                nc.scalar.activation(square[:], d[:].rearrange("p t n -> p n t"), ACT.Square)
+                squares.append(square)
             roots = []
-            for sq in squares:
-                root = ring.tile([P, HALF, 4], F32, name="root")
-                nc.scalar.activation(root[:], sq[:], ACT.Abs_reciprocal_sqrt, bias=1.0)
+            for square in squares:
+                root = ring.tile([P, HALF, PACK], F32, name="root")
+                nc.scalar.activation(root[:], square[:], ACT.Abs_reciprocal_sqrt, bias=1.0)
                 roots.append(root)
             for hf, root in enumerate(roots):
-                tile = keep.tile([P, HALF, 4], F32, name=f"damp{s}_{hf}")
-                nc.gpsimd.tensor_tensor(tile[:], root[:], root[:], MULT)
-                damp[s, hf] = tile
+                damp[s, hf] = keep.tile([P, HALF, PACK], F32, name=f"damp{s}_{hf}", align_bytes=64)
+                nc.scalar.activation(damp[s, hf][:], root[:], ACT.Square)
 
-        h_bf = [keep.tile([P, SLICE, 4], BF16, name=f"h_bf{s}", align_bytes=64) for s in range(SLICES)]
+        h_bf = [keep.tile([P, SLICE, PACK], BF16, name=f"h_bf{s}", align_bytes=64) for s in range(SLICES)]
 
         def h_stage(s, hf):
             local = slice(hf * HALF, (hf + 1) * HALF)
             cols = slice(s * SLICE + hf * HALF, s * SLICE + (hf + 1) * HALF)
-            tp = acc_pool.tile([P, 4, HALF], F32, name="acc")
-            for t in range(4):
+            template = psum.tile([P, PACK, HALF], F32, name="bank")
+            for t in range(PACK):
                 for a in range(PASSES):
                     nc.tensor.matmul_mx(
-                        tp[:, t, :],
+                        template[:, t, :],
                         lhsT=w3_codes[:, t, a, :].bitcast(FP8X4),
-                        lhsT_scale=w_sc[4:P, t, a, :],
-                        rhs=v_words[2, a, s][:, local].bitcast(FP8X4),
-                        rhs_scale=moving_scale(2, a, cols),
+                        lhsT_scale=w_sc[LOWER:P, t, a, :],
+                        rhs=v_words[TEMPLATE, a, s][:, local].bitcast(FP8X4),
+                        rhs_scale=moving_scale(TEMPLATE, a, cols),
                         start=(a == 0),
                         stop=(a == PASSES - 1),
                     )
-            nc.vector.tensor_tensor(h_bf[s][:, local, :], tp[:].rearrange("p t n -> p n t"), damp[s, hf][:], MULT)
-
-        wo_bf = keep.tile([P, N, 4], BF16, name="wo_bf", align_bytes=64)
-        wo_codes = keep.tile([P, N], U32, name="wo_codes", align_bytes=64)
-        wo_sc = keep.tile([P, N], U8, name="wo_sc", align_bytes=64)
-
-        def round_wo():
-            nc.scalar.copy(wo_bf[:], wo_raw[:].rearrange("p t n -> p n t"))
-
-        def quantise_wo():
-            for cols in (slice(0, 256), slice(256, N)):
-                nc.vector.quantize_mx(
-                    wo_codes[:, cols].bitcast(FP8X4), wo_sc[:, cols], wo_bf[:, cols, :].rearrange("p n t -> p (n t)")
-                )
+            nc.vector.tensor_tensor(h_bf[s][:, local, :], template[:].rearrange("p t n -> p n t"), damp[s, hf][:], MULT)
 
         out_view = out.rearrange("(c p) j -> p c j", p=P)
 
-        def readout(s, lo, width, last=False):
+        def readout(s, lo, width, vector_adds_last):
             name = f"{s}_{lo}"
             h_codes = keep.tile([P, width], U32, name="h_codes" + name, align_bytes=64)
             h_sc = keep.tile([P, width], U8, name="h_sc" + name, align_bytes=64)
@@ -223,7 +189,7 @@ def tile_list_template_contact_readout_kernel(
             )
             result = keep.tile([P, N_TILES, width], F32, name="result" + name)
             for group in ((0, 1), (2,)):
-                y = y_pool.tile([P, len(group), width], F32, name="y")
+                y = psum.tile([P, len(group), width], F32, name="bank")
                 for place, c in enumerate(group):
                     nc.tensor.matmul_mx(
                         y[:, place, :],
@@ -235,46 +201,75 @@ def tile_list_template_contact_readout_kernel(
                         stop=True,
                     )
                 for place, c in enumerate(group):
-                    if last and c == 2:
+                    if vector_adds_last and c == N_TILES - 1:
                         nc.vector.tensor_scalar_add(result[:, c, :], y[:, place, :], bias[:, c : c + 1])
                     else:
                         nc.scalar.activation(result[:, c, :], y[:, place, :], ACT.Identity, bias=bias[:, c : c + 1])
             first = s * SLICE + lo
             nc.sync.dma_start(out_view[:, :, first : first + width], result[:])
 
-        def d_gathers(first, count):
-            for a in range(PASSES):
-                gather_words(0, a, first, count)
-                gather_words(1, a, first, count)
+        nc.sync.dma_start(w2_raw[:], w2_words.rearrange("a p c -> p a c").bitcast(I32))
+        nc.sync.dma_start(lists[FIRST][:], offs)
+        nc.sync.dma_start(lists[SECOND][:], offs2)
+        for q in range(4):
+            nc.sync.dma_start(tab_sc[32 * q : 32 * q + 2 * LOWER, :], tab_scales[:, 4 * q : 4 * q + 4, :].bitcast(I32))
+        load_table_words(1)
+        load_weight_scales(w2_scales, 0)
+        load_w1(0, slice(0, H))
+        load_w1(1, slice(0, H // 2))
+        load_weight_scales(w3_scales, LOWER)
+        load_table_words(0)
+        gather_scales(SECOND)
+        nc.sync.dma_start(second_sc_pass1[0:112, :], v_sc[SECOND][LOWER : LOWER + 112, :].bitcast(I32))
+        load_w1(1, slice(H // 2, H))
+        wo_rows = wo.rearrange("(g t i) n -> t g i n", t=PACK, i=8)
+        for t in range(PACK):
+            nc.sync.dma_start(wo_raw[:, t, :], wo_rows[t])
+        nc.sync.dma_start(w3_raw[:], w3_words.rearrange("a p c i -> p a (c i)").bitcast(I32))
+        with nc.allow_non_contiguous_dma(reason="one bias value for each partition and output tile"):
+            nc.sync.dma_start(bias[:], b.rearrange("(c p) -> p c", p=P))
+        nc.sync.dma_start(lists[TEMPLATE][:], offs3)
 
-        def t_gathers(first, count):
-            for a in range(PASSES):
-                gather_words(2, a, first, count)
+        gather_scales(FIRST)
+        round_w1(0, slice(0, BLOCKS))
+        round_w1(1, slice(0, BLOCKS // 2))
+        round_w1(1, slice(BLOCKS // 2, BLOCKS))
+        quantise_w1(0)
+        reorder(w2_codes, w2_raw, 4)
+        reorder(w_sc, w_sc_raw, 2)
 
-        d_gathers(0, 1)
-        d_gathers(1, 1)
+        room = make_room("picked_first", "picked_first", [1] * 8)
+        for s in range(2):
+            for a in range(PASSES):
+                gather_words(room, FIRST, a, s, 1)
+                gather_words(room, SECOND, a, s, 1)
         quantise_w1(1)
-        picked.append(keep.tile([P, 3, PASSES, S], U32, name="picked_rest", tag="w1_bf1", align_bytes=64))
-        round_wo()
-        d_stage(0)
-        d_stage(1)
-        d_gathers(2, 2)
-        d_stage(2)
-        d_stage(3)
+        nc.scalar.copy(wo_bf[:], wo_raw[:].rearrange("p t n -> p n t"))
+
+        room = make_room("picked_second", "w1_bf1", [2, 2, 1, 2, 2])
+        gather_words(room, FIRST, 0, 2, 2)
+        gather_words(room, SECOND, 0, 2, 2)
+        v_sc[TEMPLATE] = room.pop(0).bitcast(U8)
+        gather_scales(TEMPLATE)
+        gather_words(room, FIRST, 1, 2, 2)
+        gather_words(room, SECOND, 1, 2, 2)
+        for s in range(SLICES - 1):
+            d_stage(s)
+        for cols in (slice(0, 2 * P), slice(2 * P, N)):
+            nc.vector.quantize_mx(
+                wo_codes[:, cols].bitcast(FP8X4), wo_sc[:, cols], wo_bf[:, cols, :].rearrange("p n t -> p (n t)")
+            )
         reorder(w3_codes, w3_raw, 8)
-        quantise_wo()
-        t_gathers(0, 1)
-        t_gathers(1, 3)
-        h_stage(0, 0)
-        h_stage(0, 1)
-        h_stage(1, 0)
-        readout(0, 0, SLICE)
-        h_stage(1, 1)
-        h_stage(2, 0)
-        readout(1, 0, SLICE)
-        h_stage(2, 1)
-        h_stage(3, 0)
-        readout(2, 0, SLICE)
-        h_stage(3, 1)
-        readout(3, 0, HALF)
-        readout(3, HALF, HALF, last=True)
+        d_stage(SLICES - 1)
+
+        room = make_room("picked_third", "w3_raw", [2] * 4)
+        for first in (0, 2):
+            for a in range(PASSES):
+                gather_words(room, TEMPLATE, a, first, 2)
+        for s in range(SLICES):
+            for hf in range(HALVES):
+                h_stage(s, hf)
+        for s in range(SLICES - 1):
+            readout(s, 0, SLICE, False)
+        for hf in range(HALVES):
+            readout(SLICES - 1, hf * HALF, HALF, True)

@@ -15,6 +15,7 @@ FP8X4 = mybir.dt.float8_e4m3fn_x4
 FP4X4 = mybir.dt.float4_e2m1fn_x4
 ACT = mybir.ActivationFunctionType
 MULT = mybir.AluOpType.mult
+ADD = mybir.AluOpType.add
 
 P = 128
 PACK = 4
@@ -44,7 +45,8 @@ def tile_list_template_contact_readout_kernel(
         w1_raw = [keep.tile([P, PACK, H], F32, name=f"w1_raw{a}", align_bytes=64) for a in range(PASSES)]
         w2_raw = keep.tile([P, PASSES, H // 2], I32, name="w2_raw")
         w3_raw = keep.tile([P, PASSES, H], I32, name="w3_raw", tag="w3_raw", align_bytes=64)
-        w_sc_raw = keep.tile([P, PASSES, H // 4], I32, name="w_sc_raw")
+        w2_sc_raw = keep.tile([P, PASSES, H // 4], I32, name="w2_sc_raw")
+        w3_sc_raw = keep.tile([P, PASSES, H // 4], I32, name="w3_sc_raw")
         wo_raw = keep.tile([P, PACK, N], F32, name="wo_raw")
         bias = keep.tile([P, N_TILES], F32, name="bias")
         v_sc = {u: keep.tile([P, S], U8, name=f"v_sc{u}", align_bytes=64)[:] for u in (FIRST, SECOND)}
@@ -55,20 +57,21 @@ def tile_list_template_contact_readout_kernel(
         nc.vector.memset(tab_sc[:], 0)
         nc.gpsimd.memset(warm_in[:], 1.0)
         nc.scalar.activation(warm_out[:], warm_in[:], ACT.Abs_reciprocal_sqrt)
-        nc.gpsimd.memset(w_sc_raw[:], 0)
+        nc.gpsimd.memset(w2_sc_raw[:], 0)
         nc.gpsimd.memset(second_sc_pass1[:], 0)
+        nc.gpsimd.memset(w3_sc_raw[:], 0)
 
         def load_table_words(a):
             nc.sync.dma_start(tab_w[:, a, :].bitcast(I32), tab_words[a].rearrange("p t i -> p (t i)").bitcast(I32))
 
-        def load_w1(a, cols):
+        def load_w1(a):
             rows = w1[a * P * PACK : (a + 1) * P * PACK, :].rearrange("(p i) c -> p i c", i=PACK)
-            nc.sync.dma_start(w1_raw[a][:, :, cols], rows[:, :, cols])
+            nc.sync.dma_start(w1_raw[a][:], rows)
 
-        def load_weight_scales(scales, row):
+        def load_weight_scales(scales, raw):
             for q in range(4):
                 nc.sync.dma_start(
-                    w_sc_raw[32 * q + row : 32 * q + row + 4, :, :],
+                    raw[32 * q : 32 * q + 4, :, :],
                     scales[:, 4 * q : 4 * q + 4, :].rearrange("a r c -> r a c").bitcast(I32),
                 )
 
@@ -98,18 +101,19 @@ def tile_list_template_contact_readout_kernel(
         w1_codes = keep.tile([P, PASSES, H], U32, name="w1_codes", align_bytes=64)
         w1_sc = keep.tile([P, PASSES, H], U8, name="w1_sc", align_bytes=64)
 
-        def round_w1(a, blocks):
+        def round_w1(a):
             src = w1_raw[a][:].rearrange("p j (g t i) -> p t g i j", t=PACK, i=8)
             dst = w1_bf[a][:].rearrange("p (t g i j) -> p t g i j", t=PACK, i=8, j=PACK)
             for t in range(PACK):
-                nc.scalar.copy(dst[:, t, blocks], src[:, t, blocks])
+                nc.scalar.copy(dst[:, t], src[:, t])
 
         def quantise_w1(a):
             nc.vector.quantize_mx(w1_codes[:, a, :].bitcast(FP8X4), w1_sc[:, a, :], w1_bf[a][:])
 
         w2_codes = keep.tile([P, PACK, PASSES, 2 * P], U8, name="w2_codes", align_bytes=64)
         w3_codes = keep.tile([P, PACK, PASSES, P], U32, name="w3_codes", align_bytes=64)
-        w_sc = keep.tile([P, PACK, PASSES, P], U8, name="w_sc", align_bytes=64)
+        w2_sc = keep.tile([P, PACK, PASSES, P], U8, name="w2_sc", align_bytes=64)
+        w3_sc = keep.tile([P, PACK, PASSES, P], U8, name="w3_sc", align_bytes=64)
 
         def reorder(dst, src, run):
             nc.vector.tensor_copy(
@@ -130,22 +134,22 @@ def tile_list_template_contact_readout_kernel(
                 cols = slice(s * SLICE + hf * HALF, s * SLICE + (hf + 1) * HALF)
                 d = psum.tile([P, PACK, HALF], F32, name="bank")
                 order = ((FIRST, 0), (SECOND, 0), (SECOND, 1), (FIRST, 1))
-                for t in range(PACK):
-                    for u, a in order:
+                for u, a in order:
+                    for t in range(PACK):
                         if u == FIRST:
                             codes = w1_codes[:, a, t * P : (t + 1) * P].bitcast(FP8X4)
                             scale = w1_sc[:, a, t * P : (t + 1) * P]
                         else:
                             codes = w2_codes[:, t, a, :].bitcast(FP4X4)
-                            scale = w_sc[:, t, a, :]
+                            scale = w2_sc[:, t, a, :]
                         nc.tensor.matmul_mx(
                             d[:, t, :],
                             lhsT=codes,
                             lhsT_scale=scale,
                             rhs=v_words[u, a, s][:, local].bitcast(FP8X4),
                             rhs_scale=moving_scale(u, a, cols),
-                            start=((u, a) == order[0]),
-                            stop=((u, a) == order[-1]),
+                            start=((u, a) == order[0] and t == 0),
+                            stop=((u, a) == order[-1] and t == PACK - 1),
                         )
                 square = ring.tile([P, HALF, PACK], F32, name="square")
                 nc.scalar.activation(square[:], d[:].rearrange("p t n -> p n t"), ACT.Square)
@@ -165,16 +169,16 @@ def tile_list_template_contact_readout_kernel(
             local = slice(hf * HALF, (hf + 1) * HALF)
             cols = slice(s * SLICE + hf * HALF, s * SLICE + (hf + 1) * HALF)
             template = psum.tile([P, PACK, HALF], F32, name="bank")
-            for t in range(PACK):
-                for a in range(PASSES):
+            for a in range(PASSES):
+                for t in range(PACK):
                     nc.tensor.matmul_mx(
                         template[:, t, :],
                         lhsT=w3_codes[:, t, a, :].bitcast(FP8X4),
-                        lhsT_scale=w_sc[LOWER:P, t, a, :],
+                        lhsT_scale=w3_sc[:, t, a, :],
                         rhs=v_words[TEMPLATE, a, s][:, local].bitcast(FP8X4),
                         rhs_scale=moving_scale(TEMPLATE, a, cols),
-                        start=(a == 0),
-                        stop=(a == PASSES - 1),
+                        start=(a == 0 and t == 0),
+                        stop=(a == PASSES - 1 and t == PACK - 1),
                     )
             nc.vector.tensor_tensor(h_bf[s][:, local, :], template[:].rearrange("p t n -> p n t"), damp[s, hf][:], MULT)
 
@@ -209,58 +213,58 @@ def tile_list_template_contact_readout_kernel(
             nc.sync.dma_start(out_view[:, :, first : first + width], result[:])
 
         nc.sync.dma_start(w2_raw[:], w2_words.rearrange("a p c -> p a c").bitcast(I32))
-        nc.sync.dma_start(lists[FIRST][:], offs)
         nc.sync.dma_start(lists[SECOND][:], offs2)
+        nc.sync.dma_start(lists[FIRST][:], offs)
         for q in range(4):
             nc.sync.dma_start(tab_sc[32 * q : 32 * q + 2 * LOWER, :], tab_scales[:, 4 * q : 4 * q + 4, :].bitcast(I32))
-        load_table_words(1)
-        load_weight_scales(w2_scales, 0)
-        load_w1(0, slice(0, H))
-        load_w1(1, slice(0, H // 2))
-        load_weight_scales(w3_scales, LOWER)
+        load_w1(0)
         load_table_words(0)
+        load_weight_scales(w2_scales, w2_sc_raw)
+        load_w1(1)
+        reorder(w2_codes, w2_raw, 4)
         gather_scales(SECOND)
         nc.sync.dma_start(second_sc_pass1[0:112, :], v_sc[SECOND][LOWER : LOWER + 112, :].bitcast(I32))
-        load_w1(1, slice(H // 2, H))
+        load_table_words(1)
+        nc.sync.dma_start(lists[TEMPLATE][:], offs3)
         wo_rows = wo.rearrange("(g t i) n -> t g i n", t=PACK, i=8)
         for t in range(PACK):
             nc.sync.dma_start(wo_raw[:, t, :], wo_rows[t])
+        load_weight_scales(w3_scales, w3_sc_raw)
         nc.sync.dma_start(w3_raw[:], w3_words.rearrange("a p c i -> p a (c i)").bitcast(I32))
         with nc.allow_non_contiguous_dma(reason="one bias value for each partition and output tile"):
             nc.sync.dma_start(bias[:], b.rearrange("(c p) -> p c", p=P))
-        nc.sync.dma_start(lists[TEMPLATE][:], offs3)
 
         gather_scales(FIRST)
-        round_w1(0, slice(0, BLOCKS))
-        round_w1(1, slice(0, BLOCKS // 2))
-        round_w1(1, slice(BLOCKS // 2, BLOCKS))
+        round_w1(0)
+        round_w1(1)
         quantise_w1(0)
-        reorder(w2_codes, w2_raw, 4)
-        reorder(w_sc, w_sc_raw, 2)
+        reorder(w2_sc, w2_sc_raw, 2)
 
-        room = make_room("picked_first", "picked_first", [1] * 8)
-        for s in range(2):
-            for a in range(PASSES):
-                gather_words(room, FIRST, a, s, 1)
-                gather_words(room, SECOND, a, s, 1)
+        room = make_room("picked_first", "picked_first", [3, 3, 1, 1])
+        gather_words(room, FIRST, 0, 0, 3)
+        gather_words(room, SECOND, 0, 0, 3)
+        gather_words(room, SECOND, 1, 0, 1)
+        gather_words(room, FIRST, 1, 0, 1)
         quantise_w1(1)
-        nc.scalar.copy(wo_bf[:], wo_raw[:].rearrange("p t n -> p n t"))
+        nc.gpsimd.tensor_scalar(wo_bf[:], wo_raw[:].rearrange("p t n -> p n t"), 1.0, 0.0, MULT, ADD)
 
-        room = make_room("picked_second", "w1_bf1", [2, 2, 1, 2, 2])
-        gather_words(room, FIRST, 0, 2, 2)
-        gather_words(room, SECOND, 0, 2, 2)
+        room = make_room("picked_second", "w1_bf1", [1, 1, 2, 2, 1, 1, 1])
+        gather_words(room, SECOND, 1, 1, 1)
+        gather_words(room, FIRST, 1, 1, 1)
+        gather_words(room, SECOND, 1, 2, 2)
+        gather_words(room, FIRST, 1, 2, 2)
+        gather_words(room, FIRST, 0, 3, 1)
+        gather_words(room, SECOND, 0, 3, 1)
         v_sc[TEMPLATE] = room.pop(0).bitcast(U8)
         gather_scales(TEMPLATE)
-        gather_words(room, FIRST, 1, 2, 2)
-        gather_words(room, SECOND, 1, 2, 2)
-        for s in range(SLICES - 1):
+        for s in range(SLICES):
             d_stage(s)
         for cols in (slice(0, 2 * P), slice(2 * P, N)):
             nc.vector.quantize_mx(
                 wo_codes[:, cols].bitcast(FP8X4), wo_sc[:, cols], wo_bf[:, cols, :].rearrange("p n t -> p (n t)")
             )
+        reorder(w3_sc, w3_sc_raw, 2)
         reorder(w3_codes, w3_raw, 8)
-        d_stage(SLICES - 1)
 
         room = make_room("picked_third", "w3_raw", [2] * 4)
         for first in (0, 2):

@@ -27,6 +27,7 @@ SLICES = S // SLICE
 HALVES = SLICE // HALF
 N_TILES = N // P
 LOWER = 4
+HELPED = 2
 FIRST, SECOND, TEMPLATE = 0, 1, 2
 
 
@@ -37,7 +38,10 @@ def tile_list_template_contact_readout_kernel(
     with ExitStack() as ctx:
         keep = ctx.enter_context(tc.tile_pool(name="keep", bufs=1))
         ring = ctx.enter_context(tc.tile_pool(name="ring", bufs=2 * HALVES))
-        psum = ctx.enter_context(tc.psum_pool(name="psum", bufs=8))
+        psum = ctx.enter_context(tc.psum_pool(name="psum", bufs=1))
+        d_banks = (0, 2, 4, 0)
+        t_banks = (6, 4, 2, 6)
+        y_banks = {(0, 0): 2, (2, 0): 0, (1, 0): 4, (3, 0): 2, (3, HALF): 6}
 
         lists = [keep.tile([P, S // 16], U16, name=f"list{u}") for u in range(3)]
         tab_w = keep.tile([P, PASSES, T], U32, name="tab_w", align_bytes=64)
@@ -78,6 +82,15 @@ def tile_list_template_contact_readout_kernel(
         def gather_scales(u):
             nc.vector.tensor_copy(v_sc[u], tab_sc[:].bitcast(U8).indirect(lists[u][:]))
 
+        template_sc = {}
+
+        def gather_template_scales(room, half):
+            template_sc[half] = room.pop(0).bitcast(U8)[:, 0 : S // 2]
+            cols = S // 32
+            nc.vector.tensor_copy(
+                template_sc[half], tab_sc[:].bitcast(U8).indirect(lists[TEMPLATE][:, half * cols : (half + 1) * cols])
+            )
+
         v_words = {}
 
         def gather_words(room, u, a, first, count):
@@ -95,6 +108,9 @@ def tile_list_template_contact_readout_kernel(
         def moving_scale(u, a, cols):
             if u == SECOND and a == 1:
                 return second_sc_pass1[:].bitcast(U8)[:, cols]
+            if u == TEMPLATE:
+                half, lo = divmod(cols.start, S // 2)
+                return template_sc[half][LOWER * a : P, lo : lo + HALF]
             return v_sc[u][LOWER * a : P, cols]
 
         w1_bf = [keep.tile([P, PACK * H], BF16, name=f"w1_bf{a}", tag=f"w1_bf{a}", align_bytes=64) for a in range(PASSES)]
@@ -115,24 +131,29 @@ def tile_list_template_contact_readout_kernel(
         w2_sc = keep.tile([P, PACK, PASSES, P], U8, name="w2_sc", align_bytes=64)
         w3_sc = keep.tile([P, PACK, PASSES, P], U8, name="w3_sc", align_bytes=64)
 
-        def reorder(dst, src, run):
-            nc.vector.tensor_copy(
+        def reorder(engine, dst, src, run):
+            engine.tensor_copy(
                 dst[:].bitcast(I32).rearrange("p t a (g e) -> p t (a g) e", e=run),
                 src[:].rearrange("p a (g t e) -> p t (a g) e", t=PACK, e=run),
             )
 
-        wo_bf = keep.tile([P, N, PACK], BF16, name="wo_bf", align_bytes=64)
+        wo_parts = (("wo_bf_wide", slice(P, N)), ("wo_bf_narrow", slice(0, P)))
+        wo_bf = [
+            keep.tile([P, cols.stop - cols.start, PACK], BF16, name=name, tag=name, align_bytes=64)
+            for name, cols in wo_parts
+        ]
         wo_codes = keep.tile([P, N], U32, name="wo_codes", align_bytes=64)
         wo_sc = keep.tile([P, N], U8, name="wo_sc", align_bytes=64)
 
         damp = {}
+        roots = {}
 
         def d_stage(s):
             squares = []
             for hf in range(HALVES):
                 local = slice(hf * HALF, (hf + 1) * HALF)
                 cols = slice(s * SLICE + hf * HALF, s * SLICE + (hf + 1) * HALF)
-                d = psum.tile([P, PACK, HALF], F32, name="bank")
+                d = psum.tile([P, PACK, HALF], F32, name=f"bank{d_banks[s] + hf}")
                 order = ((FIRST, 0), (SECOND, 0), (SECOND, 1), (FIRST, 1))
                 for u, a in order:
                     for t in range(PACK):
@@ -154,21 +175,29 @@ def tile_list_template_contact_readout_kernel(
                 square = ring.tile([P, HALF, PACK], F32, name="square")
                 nc.scalar.activation(square[:], d[:].rearrange("p t n -> p n t"), ACT.Square)
                 squares.append(square)
-            roots = []
-            for square in squares:
-                root = ring.tile([P, HALF, PACK], F32, name="root")
-                nc.scalar.activation(root[:], square[:], ACT.Abs_reciprocal_sqrt, bias=1.0)
-                roots.append(root)
-            for hf, root in enumerate(roots):
-                damp[s, hf] = keep.tile([P, HALF, PACK], F32, name=f"damp{s}_{hf}", align_bytes=64)
-                nc.scalar.activation(damp[s, hf][:], root[:], ACT.Square)
+            for hf, square in enumerate(squares):
+                roots[s, hf] = keep.tile([P, HALF, PACK], F32, name=f"root{s}_{hf}", tag=f"root{s}_{hf}")
+                nc.scalar.activation(roots[s, hf][:], square[:], ACT.Abs_reciprocal_sqrt, bias=1.0)
+            if s >= HELPED:
+                for hf in range(HALVES):
+                    damp[s, hf] = keep.tile(
+                        [P, HALF, PACK], F32, name=f"damp{s}_{hf}", tag=f"damp{s}_{hf}", align_bytes=64
+                    )[:]
+                    nc.scalar.activation(damp[s, hf], roots[s, hf][:], ACT.Square)
 
-        h_bf = [keep.tile([P, SLICE, PACK], BF16, name=f"h_bf{s}", align_bytes=64) for s in range(SLICES)]
+        def square_helped_roots():
+            tile = keep.tile([P, HELPED, HALVES, HALF, PACK], F32, name="damp_helped", tag="wo_bf_wide", align_bytes=64)
+            for s in range(HELPED):
+                for hf in range(HALVES):
+                    damp[s, hf] = tile[:, s, hf]
+                    nc.gpsimd.tensor_tensor(damp[s, hf], roots[s, hf][:], roots[s, hf][:], MULT)
+
+        h_bf = {}
 
         def h_stage(s, hf):
             local = slice(hf * HALF, (hf + 1) * HALF)
             cols = slice(s * SLICE + hf * HALF, s * SLICE + (hf + 1) * HALF)
-            template = psum.tile([P, PACK, HALF], F32, name="bank")
+            template = psum.tile([P, PACK, HALF], F32, name=f"bank{t_banks[s] + hf}")
             for a in range(PASSES):
                 for t in range(PACK):
                     nc.tensor.matmul_mx(
@@ -180,20 +209,39 @@ def tile_list_template_contact_readout_kernel(
                         start=(a == 0 and t == 0),
                         stop=(a == PASSES - 1 and t == PACK - 1),
                     )
-            nc.vector.tensor_tensor(h_bf[s][:, local, :], template[:].rearrange("p t n -> p n t"), damp[s, hf][:], MULT)
+            if s < HELPED:
+                t_sb = keep.tile([P, HALF, PACK], F32, name=f"t_sb{s}_{hf}")
+                nc.scalar.copy(t_sb[:], template[:].rearrange("p t n -> p n t"))
+                nc.gpsimd.tensor_tensor(h_bf[s, hf], t_sb[:], damp[s, hf], MULT)
+            else:
+                nc.vector.tensor_tensor(h_bf[s, hf], template[:].rearrange("p t n -> p n t"), damp[s, hf], MULT)
+
+        def h_room(slices, tag):
+            tile = keep.tile([P, len(slices), SLICE, PACK], BF16, name=f"h_bf{slices[0]}", tag=tag, align_bytes=64)
+            for place, s in enumerate(slices):
+                h_bf[s] = tile[:, place]
+                for hf in range(HALVES):
+                    h_bf[s, hf] = tile[:, place, hf * HALF : (hf + 1) * HALF, :]
 
         out_view = out.rearrange("(c p) j -> p c j", p=P)
 
-        def readout(s, lo, width, vector_adds_last):
+        h_mx = {}
+
+        def quantise_h(s, lo, width, codes_tag=None):
             name = f"{s}_{lo}"
-            h_codes = keep.tile([P, width], U32, name="h_codes" + name, align_bytes=64)
+            h_codes = keep.tile([P, width], U32, name="h_codes" + name, tag=codes_tag or "h_codes" + name, align_bytes=64)
             h_sc = keep.tile([P, width], U8, name="h_sc" + name, align_bytes=64)
             nc.vector.quantize_mx(
                 h_codes[:].bitcast(FP8X4), h_sc[:], h_bf[s][:, lo : lo + width, :].rearrange("p n t -> p (n t)")
             )
-            result = keep.tile([P, N_TILES, width], F32, name="result" + name)
+            h_mx[s, lo] = (h_codes, h_sc)
+
+        def readout(s, lo, width, vector_tiles, result_tag=None):
+            name = f"{s}_{lo}"
+            h_codes, h_sc = h_mx[s, lo]
+            result = keep.tile([P, N_TILES, width], F32, name="result" + name, tag=result_tag or "result" + name)
             for group in ((0, 1), (2,)):
-                y = psum.tile([P, len(group), width], F32, name="bank")
+                y = psum.tile([P, len(group), width], F32, name=f"bank{y_banks[s, lo] + group[0] // 2}")
                 for place, c in enumerate(group):
                     nc.tensor.matmul_mx(
                         y[:, place, :],
@@ -205,7 +253,7 @@ def tile_list_template_contact_readout_kernel(
                         stop=True,
                     )
                 for place, c in enumerate(group):
-                    if vector_adds_last and c == N_TILES - 1:
+                    if c in vector_tiles:
                         nc.vector.tensor_scalar_add(result[:, c, :], y[:, place, :], bias[:, c : c + 1])
                     else:
                         nc.scalar.activation(result[:, c, :], y[:, place, :], ACT.Identity, bias=bias[:, c : c + 1])
@@ -221,16 +269,16 @@ def tile_list_template_contact_readout_kernel(
         load_table_words(0)
         load_weight_scales(w2_scales, w2_sc_raw)
         load_w1(1)
-        reorder(w2_codes, w2_raw, 4)
+        reorder(nc.vector, w2_codes, w2_raw, 4)
         gather_scales(SECOND)
         nc.sync.dma_start(second_sc_pass1[0:112, :], v_sc[SECOND][LOWER : LOWER + 112, :].bitcast(I32))
         load_table_words(1)
         nc.sync.dma_start(lists[TEMPLATE][:], offs3)
+        load_weight_scales(w3_scales, w3_sc_raw)
+        nc.sync.dma_start(w3_raw[:], w3_words.rearrange("a p c i -> p a (c i)").bitcast(I32))
         wo_rows = wo.rearrange("(g t i) n -> t g i n", t=PACK, i=8)
         for t in range(PACK):
             nc.sync.dma_start(wo_raw[:, t, :], wo_rows[t])
-        load_weight_scales(w3_scales, w3_sc_raw)
-        nc.sync.dma_start(w3_raw[:], w3_words.rearrange("a p c i -> p a (c i)").bitcast(I32))
         with nc.allow_non_contiguous_dma(reason="one bias value for each partition and output tile"):
             nc.sync.dma_start(bias[:], b.rearrange("(c p) -> p c", p=P))
 
@@ -238,7 +286,7 @@ def tile_list_template_contact_readout_kernel(
         round_w1(0)
         round_w1(1)
         quantise_w1(0)
-        reorder(w2_sc, w2_sc_raw, 2)
+        reorder(nc.gpsimd, w2_sc, w2_sc_raw, 2)
 
         room = make_room("picked_first", "picked_first", [3, 3, 1, 1])
         gather_words(room, FIRST, 0, 0, 3)
@@ -246,34 +294,49 @@ def tile_list_template_contact_readout_kernel(
         gather_words(room, SECOND, 1, 0, 1)
         gather_words(room, FIRST, 1, 0, 1)
         quantise_w1(1)
-        nc.gpsimd.tensor_scalar(wo_bf[:], wo_raw[:].rearrange("p t n -> p n t"), 1.0, 0.0, MULT, ADD)
+        reorder(nc.gpsimd, w3_sc, w3_sc_raw, 2)
+        reorder(nc.gpsimd, w3_codes, w3_raw, 8)
+        for part, (name, cols) in zip(wo_bf, wo_parts):
+            nc.gpsimd.tensor_scalar(part[:], wo_raw[:, :, cols].rearrange("p t n -> p n t"), 1.0, 0.0, MULT, ADD)
 
-        room = make_room("picked_second", "w1_bf1", [1, 1, 2, 2, 1, 1, 1])
-        gather_words(room, SECOND, 1, 1, 1)
-        gather_words(room, FIRST, 1, 1, 1)
-        gather_words(room, SECOND, 1, 2, 2)
-        gather_words(room, FIRST, 1, 2, 2)
-        gather_words(room, FIRST, 0, 3, 1)
-        gather_words(room, SECOND, 0, 3, 1)
-        v_sc[TEMPLATE] = room.pop(0).bitcast(U8)
-        gather_scales(TEMPLATE)
-        for s in range(SLICES):
+        room = make_room("picked_second", "w1_bf1", [2, 2, 1])
+        gather_words(room, SECOND, 1, 1, 2)
+        gather_words(room, FIRST, 1, 1, 2)
+        gather_template_scales(room, 0)
+        for s in range(SLICES - 1):
             d_stage(s)
-        for cols in (slice(0, 2 * P), slice(2 * P, N)):
+        for part, (name, cols) in zip(wo_bf, wo_parts):
             nc.vector.quantize_mx(
-                wo_codes[:, cols].bitcast(FP8X4), wo_sc[:, cols], wo_bf[:, cols, :].rearrange("p n t -> p (n t)")
+                wo_codes[:, cols].bitcast(FP8X4), wo_sc[:, cols], part[:].rearrange("p n t -> p (n t)")
             )
-        reorder(w3_sc, w3_sc_raw, 2)
-        reorder(w3_codes, w3_raw, 8)
+        square_helped_roots()
 
-        room = make_room("picked_third", "w3_raw", [2] * 4)
-        for first in (0, 2):
-            for a in range(PASSES):
-                gather_words(room, TEMPLATE, a, first, 2)
-        for s in range(SLICES):
+        room = make_room("picked_third", "wo_bf_narrow", [2, 2, 1, 1, 1, 1, 1, 2, 2])
+        for a in range(PASSES):
+            gather_words(room, TEMPLATE, a, 0, 2)
+        for a in range(PASSES):
+            gather_words(room, FIRST, a, 3, 1)
+            gather_words(room, SECOND, a, 3, 1)
+        gather_template_scales(room, 1)
+        for a in range(PASSES):
+            gather_words(room, TEMPLATE, a, 2, 2)
+        for s in range(HELPED):
+            h_room([s], f"h_bf{s}")
             for hf in range(HALVES):
                 h_stage(s, hf)
-        for s in range(SLICES - 1):
-            readout(s, 0, SLICE, False)
+        d_stage(SLICES - 1)
+        quantise_h(0, 0, SLICE)
+        h_room([2, 3], "h_bf0")
         for hf in range(HALVES):
-            readout(SLICES - 1, hf * HALF, HALF, True)
+            h_stage(2, hf)
+        readout(0, 0, SLICE, (), f"root{SLICES - 1}_{HALVES - 1}")
+        quantise_h(2, 0, SLICE)
+        readout(2, 0, SLICE, ())
+        h_stage(3, 0)
+        quantise_h(1, 0, SLICE, "damp3_0")
+        h_stage(3, 1)
+        quantise_h(3, 0, HALF)
+        quantise_h(3, HALF, HALF)
+        readout(1, 0, SLICE, (2,))
+        readout(3, 0, HALF, (0, 1))
+        readout(3, HALF, HALF, (2,))

@@ -27,7 +27,8 @@ SLICES = S // SLICE
 HALVES = SLICE // HALF
 N_TILES = N // P
 LOWER = 4
-HELPED = 2
+SQUARED = 2
+HELPED = 1
 FIRST, SECOND, TEMPLATE = 0, 1, 2
 
 
@@ -39,9 +40,9 @@ def tile_list_template_contact_readout_kernel(
         keep = ctx.enter_context(tc.tile_pool(name="keep", bufs=1))
         ring = ctx.enter_context(tc.tile_pool(name="ring", bufs=2 * HALVES))
         psum = ctx.enter_context(tc.psum_pool(name="psum", bufs=1))
-        d_banks = (0, 2, 4, 0)
-        t_banks = (6, 4, 2, 6)
-        y_banks = {(0, 0): 2, (2, 0): 0, (1, 0): 4, (3, 0): 2, (3, HALF): 6}
+        d_banks = (0, 2, 4, 2)
+        t_banks = (6, 0, 6, 4)
+        y_banks = {(0, 0): 2, (1, 0): 0, (2, 0): 6, (3, 0): 2, (3, HALF): 4}
 
         lists = [keep.tile([P, S // 16], U16, name=f"list{u}") for u in range(3)]
         tab_w = keep.tile([P, PASSES, T], U32, name="tab_w", align_bytes=64)
@@ -51,7 +52,7 @@ def tile_list_template_contact_readout_kernel(
         w3_raw = keep.tile([P, PASSES, H], I32, name="w3_raw", tag="w3_raw", align_bytes=64)
         w2_sc_raw = keep.tile([P, PASSES, H // 4], I32, name="w2_sc_raw")
         w3_sc_raw = keep.tile([P, PASSES, H // 4], I32, name="w3_sc_raw")
-        wo_raw = keep.tile([P, PACK, N], F32, name="wo_raw")
+        wo_raw = keep.tile([P, PACK, N], F32, name="wo_raw", tag="wo_raw", align_bytes=64)
         bias = keep.tile([P, N_TILES], F32, name="bias")
         v_sc = {u: keep.tile([P, S], U8, name=f"v_sc{u}", align_bytes=64)[:] for u in (FIRST, SECOND)}
         second_sc_pass1 = keep.tile([P, S // 4], I32, name="second_sc_pass1", align_bytes=64)
@@ -142,7 +143,6 @@ def tile_list_template_contact_readout_kernel(
             keep.tile([P, cols.stop - cols.start, PACK], BF16, name=name, tag=name, align_bytes=64)
             for name, cols in wo_parts
         ]
-        wo_codes = keep.tile([P, N], U32, name="wo_codes", align_bytes=64)
         wo_sc = keep.tile([P, N], U8, name="wo_sc", align_bytes=64)
 
         damp = {}
@@ -155,6 +155,8 @@ def tile_list_template_contact_readout_kernel(
                 cols = slice(s * SLICE + hf * HALF, s * SLICE + (hf + 1) * HALF)
                 d = psum.tile([P, PACK, HALF], F32, name=f"bank{d_banks[s] + hf}")
                 order = ((FIRST, 0), (SECOND, 0), (SECOND, 1), (FIRST, 1))
+                if s == SLICES - 1:
+                    order = order[2:] + order[:2]
                 for u, a in order:
                     for t in range(PACK):
                         if u == FIRST:
@@ -178,7 +180,7 @@ def tile_list_template_contact_readout_kernel(
             for hf, square in enumerate(squares):
                 roots[s, hf] = keep.tile([P, HALF, PACK], F32, name=f"root{s}_{hf}", tag=f"root{s}_{hf}")
                 nc.scalar.activation(roots[s, hf][:], square[:], ACT.Abs_reciprocal_sqrt, bias=1.0)
-            if s >= HELPED:
+            if s >= SQUARED:
                 for hf in range(HALVES):
                     damp[s, hf] = keep.tile(
                         [P, HALF, PACK], F32, name=f"damp{s}_{hf}", tag=f"damp{s}_{hf}", align_bytes=64
@@ -186,15 +188,17 @@ def tile_list_template_contact_readout_kernel(
                     nc.scalar.activation(damp[s, hf], roots[s, hf][:], ACT.Square)
 
         def square_helped_roots():
-            tile = keep.tile([P, HELPED, HALVES, HALF, PACK], F32, name="damp_helped", tag="wo_bf_wide", align_bytes=64)
-            for s in range(HELPED):
+            tile = keep.tile([P, SQUARED, HALVES, HALF, PACK], F32, name="damp_helped", tag="wo_raw", align_bytes=64)
+            for s in range(SQUARED):
                 for hf in range(HALVES):
                     damp[s, hf] = tile[:, s, hf]
                     nc.gpsimd.tensor_tensor(damp[s, hf], roots[s, hf][:], roots[s, hf][:], MULT)
 
         h_bf = {}
 
-        def h_stage(s, hf):
+        templates = {}
+
+        def t_stage(s, hf):
             local = slice(hf * HALF, (hf + 1) * HALF)
             cols = slice(s * SLICE + hf * HALF, s * SLICE + (hf + 1) * HALF)
             template = psum.tile([P, PACK, HALF], F32, name=f"bank{t_banks[s] + hf}")
@@ -209,6 +213,10 @@ def tile_list_template_contact_readout_kernel(
                         start=(a == 0 and t == 0),
                         stop=(a == PASSES - 1 and t == PACK - 1),
                     )
+            templates[s, hf] = template
+
+        def h_stage(s, hf):
+            template = templates[s, hf]
             if s < HELPED:
                 t_sb = keep.tile([P, HALF, PACK], F32, name=f"t_sb{s}_{hf}")
                 nc.scalar.copy(t_sb[:], template[:].rearrange("p t n -> p n t"))
@@ -299,44 +307,56 @@ def tile_list_template_contact_readout_kernel(
         for part, (name, cols) in zip(wo_bf, wo_parts):
             nc.gpsimd.tensor_scalar(part[:], wo_raw[:, :, cols].rearrange("p t n -> p n t"), 1.0, 0.0, MULT, ADD)
 
-        room = make_room("picked_second", "w1_bf1", [2, 2, 1])
-        gather_words(room, SECOND, 1, 1, 2)
-        gather_words(room, FIRST, 1, 1, 2)
+        room = make_room("picked_second", "w1_bf1", [1, 1, 1])
+        gather_words(room, SECOND, 1, 1, 1)
+        gather_words(room, FIRST, 1, 1, 1)
         gather_template_scales(room, 0)
-        for s in range(SLICES - 1):
+        room = make_room("picked_third", "w3_raw", [2, 2, 2, 2, 1, 1, 1, 2, 2])
+        for a in range(PASSES):
+            gather_words(room, TEMPLATE, a, 0, 2)
+        gather_words(room, SECOND, 1, 2, 2)
+        gather_words(room, FIRST, 1, 2, 2)
+        gather_words(room, FIRST, 0, 3, 1)
+        gather_words(room, SECOND, 0, 3, 1)
+        gather_template_scales(room, 1)
+        for a in range(PASSES):
+            gather_words(room, TEMPLATE, a, 2, 2)
+
+        for s in range(2):
+            h_room([s], f"h_bf{s}")
+        for s in range(2):
             d_stage(s)
+        square_helped_roots()
+        for s in range(2):
+            for hf in range(HALVES):
+                t_stage(s, hf)
+        for hf in range(HALVES):
+            h_stage(0, hf)
+        for s in range(2, SLICES):
+            d_stage(s)
+        for hf in range(HALVES):
+            t_stage(2, hf)
+        for hf in range(HALVES):
+            h_stage(1, hf)
+        wo_codes = keep.tile([P, N], U32, name="wo_codes", tag="wo_raw", align_bytes=64)
         for part, (name, cols) in zip(wo_bf, wo_parts):
             nc.vector.quantize_mx(
                 wo_codes[:, cols].bitcast(FP8X4), wo_sc[:, cols], part[:].rearrange("p n t -> p (n t)")
             )
-        square_helped_roots()
-
-        room = make_room("picked_third", "wo_bf_narrow", [2, 2, 1, 1, 1, 1, 1, 2, 2])
-        for a in range(PASSES):
-            gather_words(room, TEMPLATE, a, 0, 2)
-        for a in range(PASSES):
-            gather_words(room, FIRST, a, 3, 1)
-            gather_words(room, SECOND, a, 3, 1)
-        gather_template_scales(room, 1)
-        for a in range(PASSES):
-            gather_words(room, TEMPLATE, a, 2, 2)
-        for s in range(HELPED):
-            h_room([s], f"h_bf{s}")
-            for hf in range(HALVES):
-                h_stage(s, hf)
-        d_stage(SLICES - 1)
         quantise_h(0, 0, SLICE)
-        h_room([2, 3], "h_bf0")
-        for hf in range(HALVES):
-            h_stage(2, hf)
         readout(0, 0, SLICE, (), f"root{SLICES - 1}_{HALVES - 1}")
-        quantise_h(2, 0, SLICE)
-        readout(2, 0, SLICE, ())
+        for hf in range(HALVES):
+            t_stage(3, hf)
+        h_room([2, 3], "h_bf0")
+        h_stage(2, 0)
+        quantise_h(1, 0, SLICE)
+        readout(1, 0, SLICE, ())
+        h_stage(2, 1)
         h_stage(3, 0)
-        quantise_h(1, 0, SLICE, "damp3_0")
+        quantise_h(2, 0, SLICE)
         h_stage(3, 1)
-        quantise_h(3, 0, HALF)
-        quantise_h(3, HALF, HALF)
-        readout(1, 0, SLICE, (2,))
-        readout(3, 0, HALF, (0, 1))
-        readout(3, HALF, HALF, (2,))
+        for hf in range(HALVES):
+            quantise_h(3, hf * HALF, HALF)
+        readout(2, 0, SLICE, (2,))
+        for hf in range(HALVES):
+            readout(3, hf * HALF, HALF, (2,))

@@ -20,15 +20,13 @@ ADD = mybir.AluOpType.add
 P = 128
 PACK = 4
 PASSES = K // (P * PACK)
-BLOCKS = H // 32
 SLICE = 256
 HALF = 128
 SLICES = S // SLICE
 HALVES = SLICE // HALF
 N_TILES = N // P
+QUADRANTS = 4
 LOWER = 4
-SQUARED = 2
-HELPED = 1
 FIRST, SECOND, TEMPLATE = 0, 1, 2
 
 
@@ -38,85 +36,76 @@ def tile_list_template_contact_readout_kernel(
     nc = tc.nc
     with ExitStack() as ctx:
         keep = ctx.enter_context(tc.tile_pool(name="keep", bufs=1))
-        ring = ctx.enter_context(tc.tile_pool(name="ring", bufs=2 * HALVES))
         psum = ctx.enter_context(tc.psum_pool(name="psum", bufs=1))
-        d_banks = (0, 2, 4, 2)
-        t_banks = (6, 0, 6, 4)
-        y_banks = {(0, 0): 2, (1, 0): 0, (2, 0): 6, (3, 0): 2, (3, HALF): 4}
+        bank_pairs = []
+
+        def next_pair():
+            bank_pairs.append(len(bank_pairs) % 4)
+            return 2 * bank_pairs[-1]
+
+        def sbuf(shape, dtype, name, tag=None):
+            return keep.tile(shape, dtype, name=name, tag=tag or name, align_bytes=64)
 
         lists = [keep.tile([P, S // 16], U16, name=f"list{u}") for u in range(3)]
-        tab_w = keep.tile([P, PASSES, T], U32, name="tab_w", align_bytes=64)
-        tab_sc = keep.tile([P, T // 4], I32, name="tab_sc", align_bytes=64)
-        w1_raw = [keep.tile([P, PACK, H], F32, name=f"w1_raw{a}", align_bytes=64) for a in range(PASSES)]
-        w2_raw = keep.tile([P, PASSES, H // 2], I32, name="w2_raw")
-        w3_raw = keep.tile([P, PASSES, H], I32, name="w3_raw", tag="w3_raw", align_bytes=64)
-        w2_sc_raw = keep.tile([P, PASSES, H // 4], I32, name="w2_sc_raw")
-        w3_sc_raw = keep.tile([P, PASSES, H // 4], I32, name="w3_sc_raw")
-        wo_raw = keep.tile([P, PACK, N], F32, name="wo_raw", tag="wo_raw", align_bytes=64)
-        bias = keep.tile([P, N_TILES], F32, name="bias")
-        v_sc = {u: keep.tile([P, S], U8, name=f"v_sc{u}", align_bytes=64)[:] for u in (FIRST, SECOND)}
-        second_sc_pass1 = keep.tile([P, S // 4], I32, name="second_sc_pass1", align_bytes=64)
-        warm_in = keep.tile([P, 1], F32, name="warm_in")
-        warm_out = keep.tile([P, 1], F32, name="warm_out")
+        tab_w = [sbuf([P, T], U32, f"tab_w{a}") for a in range(PASSES)]
+        tab_sc = sbuf([P, T // 4], I32, "tab_sc")
+        w1_raw = [sbuf([P, PACK, H], F32, f"w1_raw{a}") for a in range(PASSES)]
+        w2_raw = sbuf([P, PASSES, H // 2], I32, "w2_raw")
+        w3_raw = sbuf([P, PASSES, H], I32, "w3_raw")
+        w2_sc_raw = sbuf([P, PASSES, H // 4], I32, "w2_sc_raw")
+        w3_sc_raw = sbuf([P, PASSES, H // 4], I32, "w3_sc_raw")
+        wo_raw = sbuf([P, PACK, N], F32, "wo_raw")
+        bias = sbuf([P, N_TILES], F32, "bias")
+        v_sc = [sbuf([P, S], U8, f"v_sc{u}") for u in range(3)]
+        second_sc_pass1 = sbuf([P, S // 4], I32, "second_sc_pass1")
+        warm_in = sbuf([P, 1], F32, "warm_in")
+        warm_out = sbuf([P, 1], F32, "warm_out")
 
         nc.vector.memset(tab_sc[:], 0)
         nc.gpsimd.memset(warm_in[:], 1.0)
         nc.scalar.activation(warm_out[:], warm_in[:], ACT.Abs_reciprocal_sqrt)
         nc.gpsimd.memset(w2_sc_raw[:], 0)
-        nc.gpsimd.memset(second_sc_pass1[:], 0)
         nc.gpsimd.memset(w3_sc_raw[:], 0)
+        nc.gpsimd.memset(second_sc_pass1[:], 0)
 
         def load_table_words(a):
-            nc.sync.dma_start(tab_w[:, a, :].bitcast(I32), tab_words[a].rearrange("p t i -> p (t i)").bitcast(I32))
+            nc.sync.dma_start(tab_w[a][:].bitcast(I32), tab_words[a].rearrange("p t i -> p (t i)").bitcast(I32))
 
         def load_w1(a):
             rows = w1[a * P * PACK : (a + 1) * P * PACK, :].rearrange("(p i) c -> p i c", i=PACK)
             nc.sync.dma_start(w1_raw[a][:], rows)
 
         def load_weight_scales(scales, raw):
-            for q in range(4):
+            for q in range(QUADRANTS):
                 nc.sync.dma_start(
                     raw[32 * q : 32 * q + 4, :, :],
                     scales[:, 4 * q : 4 * q + 4, :].rearrange("a r c -> r a c").bitcast(I32),
                 )
 
         def gather_scales(u):
-            nc.vector.tensor_copy(v_sc[u], tab_sc[:].bitcast(U8).indirect(lists[u][:]))
-
-        template_sc = {}
-
-        def gather_template_scales(room, half):
-            template_sc[half] = room.pop(0).bitcast(U8)[:, 0 : S // 2]
-            cols = S // 32
-            nc.vector.tensor_copy(
-                template_sc[half], tab_sc[:].bitcast(U8).indirect(lists[TEMPLATE][:, half * cols : (half + 1) * cols])
-            )
+            nc.vector.tensor_copy(v_sc[u][:], tab_sc[:].bitcast(U8).indirect(lists[u][:]))
 
         v_words = {}
 
-        def gather_words(room, u, a, first, count):
-            piece = room.pop(0)
+        def gather_words(name, tag, wanted):
+            tile = sbuf([P, sum(len(slices) for u, a, slices in wanted) * SLICE], U32, name, tag)
             cols = SLICE // 16
-            nc.vector.tensor_copy(piece, tab_w[:, a, :].indirect(lists[u][:, first * cols : (first + count) * cols]))
-            for s in range(count):
-                v_words[u, a, first + s] = piece[:, s * SLICE : (s + 1) * SLICE]
-
-        def make_room(name, tag, counts):
-            tile = keep.tile([P, sum(counts) * SLICE], U32, name=name, tag=tag, align_bytes=64)
-            ends = [sum(counts[:n]) * SLICE for n in range(len(counts) + 1)]
-            return [tile[:, lo:hi] for lo, hi in zip(ends, ends[1:])]
+            place = 0
+            for u, a, slices in wanted:
+                offsets = lists[u][:, slices[0] * cols : (slices[-1] + 1) * cols]
+                nc.vector.tensor_copy(tile[:, place : place + len(slices) * SLICE], tab_w[a][:].indirect(offsets))
+                for s in slices:
+                    v_words[u, a, s] = tile[:, place : place + SLICE]
+                    place += SLICE
 
         def moving_scale(u, a, cols):
             if u == SECOND and a == 1:
                 return second_sc_pass1[:].bitcast(U8)[:, cols]
-            if u == TEMPLATE:
-                half, lo = divmod(cols.start, S // 2)
-                return template_sc[half][LOWER * a : P, lo : lo + HALF]
             return v_sc[u][LOWER * a : P, cols]
 
-        w1_bf = [keep.tile([P, PACK * H], BF16, name=f"w1_bf{a}", tag=f"w1_bf{a}", align_bytes=64) for a in range(PASSES)]
-        w1_codes = keep.tile([P, PASSES, H], U32, name="w1_codes", align_bytes=64)
-        w1_sc = keep.tile([P, PASSES, H], U8, name="w1_sc", align_bytes=64)
+        w1_bf = [sbuf([P, PACK * H], BF16, f"w1_bf{a}") for a in range(PASSES)]
+        w1_codes = sbuf([P, PASSES, H], U32, "w1_codes")
+        w1_sc = sbuf([P, PASSES, H], U8, "w1_sc")
 
         def round_w1(a):
             src = w1_raw[a][:].rearrange("p j (g t i) -> p t g i j", t=PACK, i=8)
@@ -127,10 +116,10 @@ def tile_list_template_contact_readout_kernel(
         def quantise_w1(a):
             nc.vector.quantize_mx(w1_codes[:, a, :].bitcast(FP8X4), w1_sc[:, a, :], w1_bf[a][:])
 
-        w2_codes = keep.tile([P, PACK, PASSES, 2 * P], U8, name="w2_codes", align_bytes=64)
-        w3_codes = keep.tile([P, PACK, PASSES, P], U32, name="w3_codes", align_bytes=64)
-        w2_sc = keep.tile([P, PACK, PASSES, P], U8, name="w2_sc", align_bytes=64)
-        w3_sc = keep.tile([P, PACK, PASSES, P], U8, name="w3_sc", align_bytes=64)
+        w2_codes = sbuf([P, PACK, PASSES, 2 * P], U8, "w2_codes")
+        w3_codes = sbuf([P, PACK, PASSES, P], U32, "w3_codes")
+        w2_sc = sbuf([P, PACK, PASSES, P], U8, "w2_sc")
+        w3_sc = sbuf([P, PACK, PASSES, P], U8, "w3_sc")
 
         def reorder(engine, dst, src, run):
             engine.tensor_copy(
@@ -138,35 +127,25 @@ def tile_list_template_contact_readout_kernel(
                 src[:].rearrange("p a (g t e) -> p t (a g) e", t=PACK, e=run),
             )
 
-        wo_parts = (("wo_bf_wide", slice(P, N)), ("wo_bf_narrow", slice(0, P)))
-        wo_bf = [
-            keep.tile([P, cols.stop - cols.start, PACK], BF16, name=name, tag=name, align_bytes=64)
-            for name, cols in wo_parts
-        ]
-        wo_sc = keep.tile([P, N], U8, name="wo_sc", align_bytes=64)
+        def weight(u, a, t):
+            if u == FIRST:
+                cols = slice(t * P, (t + 1) * P)
+                return w1_codes[:, a, cols].bitcast(FP8X4), w1_sc[:, a, cols]
+            if u == SECOND:
+                return w2_codes[:, t, a, :].bitcast(FP4X4), w2_sc[:, t, a, :]
+            return w3_codes[:, t, a, :].bitcast(FP8X4), w3_sc[:, t, a, :]
 
-        damp = {}
-        roots = {}
-
-        def d_stage(s):
-            squares = []
-            for hf in range(HALVES):
-                local = slice(hf * HALF, (hf + 1) * HALF)
-                cols = slice(s * SLICE + hf * HALF, s * SLICE + (hf + 1) * HALF)
-                d = psum.tile([P, PACK, HALF], F32, name=f"bank{d_banks[s] + hf}")
-                order = ((FIRST, 0), (SECOND, 0), (SECOND, 1), (FIRST, 1))
-                if s == SLICES - 1:
-                    order = order[2:] + order[:2]
-                for u, a in order:
+        def project(s, order):
+            pair = next_pair()
+            banks = [psum.tile([P, PACK, HALF], F32, name=f"bank{pair + hf}") for hf in range(HALVES)]
+            for u, a in order:
+                for hf in range(HALVES):
+                    local = slice(hf * HALF, (hf + 1) * HALF)
+                    cols = slice(s * SLICE + hf * HALF, s * SLICE + (hf + 1) * HALF)
                     for t in range(PACK):
-                        if u == FIRST:
-                            codes = w1_codes[:, a, t * P : (t + 1) * P].bitcast(FP8X4)
-                            scale = w1_sc[:, a, t * P : (t + 1) * P]
-                        else:
-                            codes = w2_codes[:, t, a, :].bitcast(FP4X4)
-                            scale = w2_sc[:, t, a, :]
+                        codes, scale = weight(u, a, t)
                         nc.tensor.matmul_mx(
-                            d[:, t, :],
+                            banks[hf][:, t, :],
                             lhsT=codes,
                             lhsT_scale=scale,
                             rhs=v_words[u, a, s][:, local].bitcast(FP8X4),
@@ -174,112 +153,70 @@ def tile_list_template_contact_readout_kernel(
                             start=((u, a) == order[0] and t == 0),
                             stop=((u, a) == order[-1] and t == PACK - 1),
                         )
-                square = ring.tile([P, HALF, PACK], F32, name="square")
-                nc.scalar.activation(square[:], d[:].rearrange("p t n -> p n t"), ACT.Square)
-                squares.append(square)
-            for hf, square in enumerate(squares):
-                roots[s, hf] = keep.tile([P, HALF, PACK], F32, name=f"root{s}_{hf}", tag=f"root{s}_{hf}")
-                nc.scalar.activation(roots[s, hf][:], square[:], ACT.Abs_reciprocal_sqrt, bias=1.0)
-            if s >= SQUARED:
-                for hf in range(HALVES):
-                    damp[s, hf] = keep.tile(
-                        [P, HALF, PACK], F32, name=f"damp{s}_{hf}", tag=f"damp{s}_{hf}", align_bytes=64
-                    )[:]
-                    nc.scalar.activation(damp[s, hf], roots[s, hf][:], ACT.Square)
+            return [bank[:].rearrange("p t n -> p n t") for bank in banks]
 
-        def square_helped_roots():
-            tile = keep.tile([P, SQUARED, HALVES, HALF, PACK], F32, name="damp_helped", tag="wo_raw", align_bytes=64)
-            for s in range(SQUARED):
-                for hf in range(HALVES):
-                    damp[s, hf] = tile[:, s, hf]
-                    nc.gpsimd.tensor_tensor(damp[s, hf], roots[s, hf][:], roots[s, hf][:], MULT)
+        def root_of(s, d):
+            square = sbuf([P, HALVES, HALF, PACK], F32, f"square{s}", f"square{s % 2}")
+            root = sbuf([P, HALVES, HALF, PACK], F32, f"root{s}")
+            for hf in range(HALVES):
+                nc.scalar.activation(square[:, hf], d[hf], ACT.Square)
+            for hf in range(HALVES):
+                nc.scalar.activation(root[:, hf], square[:, hf], ACT.Abs_reciprocal_sqrt, bias=1.0)
+            return root
 
-        h_bf = {}
+        def damping_on_scalar(s, root):
+            damp = sbuf([P, HALVES, HALF, PACK], F32, f"damp{s}")
+            for hf in range(HALVES):
+                nc.scalar.activation(damp[:, hf], root[:, hf], ACT.Square)
+            return damp
 
-        templates = {}
+        def product_on_vector(h, template, damp):
+            for hf in range(HALVES):
+                nc.vector.tensor_tensor(h[:, hf], template[hf], damp[:, hf], MULT)
 
-        def t_stage(s, hf):
-            local = slice(hf * HALF, (hf + 1) * HALF)
-            cols = slice(s * SLICE + hf * HALF, s * SLICE + (hf + 1) * HALF)
-            template = psum.tile([P, PACK, HALF], F32, name=f"bank{t_banks[s] + hf}")
-            for a in range(PASSES):
-                for t in range(PACK):
-                    nc.tensor.matmul_mx(
-                        template[:, t, :],
-                        lhsT=w3_codes[:, t, a, :].bitcast(FP8X4),
-                        lhsT_scale=w3_sc[:, t, a, :],
-                        rhs=v_words[TEMPLATE, a, s][:, local].bitcast(FP8X4),
-                        rhs_scale=moving_scale(TEMPLATE, a, cols),
-                        start=(a == 0 and t == 0),
-                        stop=(a == PASSES - 1 and t == PACK - 1),
-                    )
-            templates[s, hf] = template
-
-        def h_stage(s, hf):
-            template = templates[s, hf]
-            if s < HELPED:
-                t_sb = keep.tile([P, HALF, PACK], F32, name=f"t_sb{s}_{hf}")
-                nc.scalar.copy(t_sb[:], template[:].rearrange("p t n -> p n t"))
-                nc.gpsimd.tensor_tensor(h_bf[s, hf], t_sb[:], damp[s, hf], MULT)
-            else:
-                nc.vector.tensor_tensor(h_bf[s, hf], template[:].rearrange("p t n -> p n t"), damp[s, hf], MULT)
-
-        def h_room(slices, tag):
-            tile = keep.tile([P, len(slices), SLICE, PACK], BF16, name=f"h_bf{slices[0]}", tag=tag, align_bytes=64)
-            for place, s in enumerate(slices):
-                h_bf[s] = tile[:, place]
-                for hf in range(HALVES):
-                    h_bf[s, hf] = tile[:, place, hf * HALF : (hf + 1) * HALF, :]
+        def quantise(codes, scale, values):
+            nc.vector.quantize_mx(codes.bitcast(FP8X4), scale, values)
 
         out_view = out.rearrange("(c p) j -> p c j", p=P)
 
-        h_mx = {}
-
-        def quantise_h(s, lo, width, codes_tag=None):
-            name = f"{s}_{lo}"
-            h_codes = keep.tile([P, width], U32, name="h_codes" + name, tag=codes_tag or "h_codes" + name, align_bytes=64)
-            h_sc = keep.tile([P, width], U8, name="h_sc" + name, align_bytes=64)
-            nc.vector.quantize_mx(
-                h_codes[:].bitcast(FP8X4), h_sc[:], h_bf[s][:, lo : lo + width, :].rearrange("p n t -> p (n t)")
-            )
-            h_mx[s, lo] = (h_codes, h_sc)
-
-        def readout(s, lo, width, vector_tiles, result_tag=None):
-            name = f"{s}_{lo}"
-            h_codes, h_sc = h_mx[s, lo]
-            result = keep.tile([P, N_TILES, width], F32, name="result" + name, tag=result_tag or "result" + name)
-            for group in ((0, 1), (2,)):
-                y = psum.tile([P, len(group), width], F32, name=f"bank{y_banks[s, lo] + group[0] // 2}")
-                for place, c in enumerate(group):
+        def readout(first, width, codes, scale, vector_tiles):
+            pair = next_pair()
+            result = sbuf([P, N_TILES, width], F32, f"result{first}")
+            for place, group in enumerate(((0, 1), (2,))):
+                y = psum.tile([P, len(group), width], F32, name=f"bank{pair + place}")
+                for slot, c in enumerate(group):
                     nc.tensor.matmul_mx(
-                        y[:, place, :],
+                        y[:, slot, :],
                         lhsT=wo_codes[:, c * P : (c + 1) * P].bitcast(FP8X4),
                         lhsT_scale=wo_sc[:, c * P : (c + 1) * P],
-                        rhs=h_codes[:].bitcast(FP8X4),
-                        rhs_scale=h_sc[:],
+                        rhs=codes.bitcast(FP8X4),
+                        rhs_scale=scale,
                         start=True,
                         stop=True,
                     )
-                for place, c in enumerate(group):
+                for slot, c in enumerate(group):
                     if c in vector_tiles:
-                        nc.vector.tensor_scalar_add(result[:, c, :], y[:, place, :], bias[:, c : c + 1])
+                        nc.vector.tensor_scalar_add(result[:, c, :], y[:, slot, :], bias[:, c : c + 1])
                     else:
-                        nc.scalar.activation(result[:, c, :], y[:, place, :], ACT.Identity, bias=bias[:, c : c + 1])
-            first = s * SLICE + lo
+                        nc.scalar.activation(result[:, c, :], y[:, slot, :], ACT.Identity, bias=bias[:, c : c + 1])
             nc.sync.dma_start(out_view[:, :, first : first + width], result[:])
 
         nc.sync.dma_start(w2_raw[:], w2_words.rearrange("a p c -> p a c").bitcast(I32))
         nc.sync.dma_start(lists[SECOND][:], offs2)
         nc.sync.dma_start(lists[FIRST][:], offs)
-        for q in range(4):
+        for q in range(QUADRANTS):
             nc.sync.dma_start(tab_sc[32 * q : 32 * q + 2 * LOWER, :], tab_scales[:, 4 * q : 4 * q + 4, :].bitcast(I32))
         load_w1(0)
-        load_table_words(0)
         load_weight_scales(w2_scales, w2_sc_raw)
+        load_table_words(0)
         load_w1(1)
         reorder(nc.vector, w2_codes, w2_raw, 4)
         gather_scales(SECOND)
-        nc.sync.dma_start(second_sc_pass1[0:112, :], v_sc[SECOND][LOWER : LOWER + 112, :].bitcast(I32))
+        for q in range(QUADRANTS):
+            nc.sync.dma_start(
+                second_sc_pass1[32 * q : 32 * q + 4, :],
+                v_sc[SECOND][32 * q + LOWER : 32 * q + LOWER + 4, :].bitcast(I32),
+            )
         load_table_words(1)
         nc.sync.dma_start(lists[TEMPLATE][:], offs3)
         load_weight_scales(w3_scales, w3_sc_raw)
@@ -293,70 +230,78 @@ def tile_list_template_contact_readout_kernel(
         gather_scales(FIRST)
         round_w1(0)
         round_w1(1)
-        quantise_w1(0)
         reorder(nc.gpsimd, w2_sc, w2_sc_raw, 2)
-
-        room = make_room("picked_first", "picked_first", [3, 3, 1, 1])
-        gather_words(room, FIRST, 0, 0, 3)
-        gather_words(room, SECOND, 0, 0, 3)
-        gather_words(room, SECOND, 1, 0, 1)
-        gather_words(room, FIRST, 1, 0, 1)
-        quantise_w1(1)
         reorder(nc.gpsimd, w3_sc, w3_sc_raw, 2)
         reorder(nc.gpsimd, w3_codes, w3_raw, 8)
-        for part, (name, cols) in zip(wo_bf, wo_parts):
-            nc.gpsimd.tensor_scalar(part[:], wo_raw[:, :, cols].rearrange("p t n -> p n t"), 1.0, 0.0, MULT, ADD)
+        wo_bf = sbuf([P, N, PACK], BF16, "wo_bf")
+        nc.gpsimd.tensor_scalar(wo_bf[:], wo_raw[:].rearrange("p t n -> p n t"), 1.0, 0.0, MULT, ADD)
 
-        room = make_room("picked_second", "w1_bf1", [1, 1, 1])
-        gather_words(room, SECOND, 1, 1, 1)
-        gather_words(room, FIRST, 1, 1, 1)
-        gather_template_scales(room, 0)
-        room = make_room("picked_third", "w3_raw", [2, 2, 2, 2, 1, 1, 1, 2, 2])
-        for a in range(PASSES):
-            gather_words(room, TEMPLATE, a, 0, 2)
-        gather_words(room, SECOND, 1, 2, 2)
-        gather_words(room, FIRST, 1, 2, 2)
-        gather_words(room, FIRST, 0, 3, 1)
-        gather_words(room, SECOND, 0, 3, 1)
-        gather_template_scales(room, 1)
-        for a in range(PASSES):
-            gather_words(room, TEMPLATE, a, 2, 2)
+        early = ((FIRST, 0), (SECOND, 0))
+        late = ((SECOND, 1), (FIRST, 1))
+        both = ((TEMPLATE, 0), (TEMPLATE, 1))
 
+        def of_slice(pairs, *slices):
+            return [(u, a, slices) for u, a in pairs]
+
+        quantise_w1(0)
+        gather_words("picked0", None, of_slice(early, 0, 1, 2))
+        quantise_w1(1)
+        gather_words("picked1", None, of_slice(late, 0) + of_slice(late, 1))
+        gather_scales(TEMPLATE)
+        d0 = project(0, early + late)
+        d1 = project(1, early + late)
+        gather_words(
+            "picked4",
+            "w3_raw",
+            of_slice(both, 0) + of_slice(late, 2) + of_slice(both, 1) + of_slice(early + late, 3),
+        )
+        root0 = root_of(0, d0)
+        root1 = root_of(1, d1)
+        damp01 = sbuf([P, 2, HALVES, HALF, PACK], F32, "damp01", "wo_raw")
+        nc.gpsimd.tensor_tensor(damp01[:, 0], root0[:], root0[:], MULT)
+        nc.gpsimd.tensor_tensor(damp01[:, 1], root1[:], root1[:], MULT)
+
+        t0 = project(0, both)
+        t0_sb = sbuf([P, HALVES, HALF, PACK], F32, "t0_sb")
+        for hf in range(HALVES):
+            nc.scalar.copy(t0_sb[:, hf], t0[hf])
+        h01 = sbuf([P, 2, HALVES, HALF, PACK], BF16, "h01")
+        nc.gpsimd.tensor_tensor(h01[:, 0], t0_sb[:], damp01[:, 0], MULT)
+
+        d2 = project(2, early + late)
+        damp2 = damping_on_scalar(2, root_of(2, d2))
+        t1 = project(1, both)
+        d3 = project(3, early + late)
+        damp3 = damping_on_scalar(3, root_of(3, d3))
+        product_on_vector(h01[:, 1], t1, damp01[:, 1])
+        gather_words("picked5", "root1", of_slice(both, 2))
+        t2 = project(2, both)
+
+        planes = sbuf([P, N + 2 * SLICE], U8, "planes", "wo_raw")
+        wo_sc = planes[:, 0:N]
+        wo_codes = sbuf([P, N], U32, "wo_codes")
+        for cols in (slice(0, 2 * P), slice(2 * P, N)):
+            quantise(wo_codes[:, cols], wo_sc[:, cols], wo_bf[:, cols, :].rearrange("p n t -> p (n t)"))
+        h_codes = sbuf([P, S], U32, "h_codes")
         for s in range(2):
-            h_room([s], f"h_bf{s}")
-        for s in range(2):
-            d_stage(s)
-        square_helped_roots()
-        for s in range(2):
-            for hf in range(HALVES):
-                t_stage(s, hf)
+            scale = planes[:, N + s * SLICE : N + (s + 1) * SLICE]
+            cols = slice(s * SLICE, (s + 1) * SLICE)
+            quantise(h_codes[:, cols], scale, h01[:, s].rearrange("p f n t -> p (f n t)"))
+            readout(s * SLICE, SLICE, h_codes[:, cols], scale, ())
+
+        h2 = sbuf([P, HALVES, HALF, PACK], BF16, "h2", "t0_sb")
+        product_on_vector(h2, t2, damp2)
+        gather_words("picked6", "damp2", of_slice(both, 3))
+        t3 = project(3, both)
+        h_sc = sbuf([P, 2 * SLICE], U8, "h_sc")
+        cols = slice(2 * SLICE, 3 * SLICE)
+        quantise(h_codes[:, cols], h_sc[:, 0:SLICE], h2[:].rearrange("p f n t -> p (f n t)"))
+        readout(2 * SLICE, SLICE, h_codes[:, cols], h_sc[:, 0:SLICE], ())
+        h3 = sbuf([P, HALVES, HALF, PACK], BF16, "h3")
+        product_on_vector(h3, t3, damp3)
+        last = [slice(3 * SLICE + hf * HALF, 3 * SLICE + (hf + 1) * HALF) for hf in range(HALVES)]
+        scales = [h_sc[:, SLICE + hf * HALF : SLICE + (hf + 1) * HALF] for hf in range(HALVES)]
         for hf in range(HALVES):
-            h_stage(0, hf)
-        for s in range(2, SLICES):
-            d_stage(s)
+            quantise(h_codes[:, last[hf]], scales[hf], h3[:, hf].rearrange("p n t -> p (n t)"))
         for hf in range(HALVES):
-            t_stage(2, hf)
-        for hf in range(HALVES):
-            h_stage(1, hf)
-        wo_codes = keep.tile([P, N], U32, name="wo_codes", tag="wo_raw", align_bytes=64)
-        for part, (name, cols) in zip(wo_bf, wo_parts):
-            nc.vector.quantize_mx(
-                wo_codes[:, cols].bitcast(FP8X4), wo_sc[:, cols], part[:].rearrange("p n t -> p (n t)")
-            )
-        quantise_h(0, 0, SLICE)
-        readout(0, 0, SLICE, (), f"root{SLICES - 1}_{HALVES - 1}")
-        for hf in range(HALVES):
-            t_stage(3, hf)
-        h_room([2, 3], "h_bf0")
-        h_stage(2, 0)
-        quantise_h(1, 0, SLICE)
-        readout(1, 0, SLICE, ())
-        h_stage(2, 1)
-        h_stage(3, 0)
-        quantise_h(2, 0, SLICE)
-        h_stage(3, 1)
-        for hf in range(HALVES):
-            quantise_h(3, hf * HALF, HALF)
-        readout(2, 0, SLICE, (2,))
-        for hf in range(HALVES):
-            readout(3, hf * HALF, HALF, (2,))
+            readout(last[hf].start, HALF, h_codes[:, last[hf]], scales[hf], (2,))

@@ -37,11 +37,6 @@ def tile_list_template_contact_readout_kernel(
     with ExitStack() as ctx:
         keep = ctx.enter_context(tc.tile_pool(name="keep", bufs=1))
         psum = ctx.enter_context(tc.psum_pool(name="psum", bufs=1))
-        bank_pairs = []
-
-        def next_pair():
-            bank_pairs.append(len(bank_pairs) % 4)
-            return 2 * bank_pairs[-1]
 
         def sbuf(shape, dtype, name, tag=None):
             return keep.tile(shape, dtype, name=name, tag=tag or name, align_bytes=64)
@@ -56,7 +51,7 @@ def tile_list_template_contact_readout_kernel(
         w3_sc_raw = sbuf([P, PASSES, H // 4], I32, "w3_sc_raw")
         wo_raw = sbuf([P, PACK, N], F32, "wo_raw")
         bias = sbuf([P, N_TILES], F32, "bias")
-        v_sc = [sbuf([P, S], U8, f"v_sc{u}") for u in range(3)]
+        v_sc = {u: sbuf([P, S], U8, f"v_sc{u}") for u in (FIRST, SECOND)}
         second_sc_pass1 = sbuf([P, S // 4], I32, "second_sc_pass1")
         warm_in = sbuf([P, 1], F32, "warm_in")
         warm_out = sbuf([P, 1], F32, "warm_out")
@@ -85,33 +80,45 @@ def tile_list_template_contact_readout_kernel(
         def gather_scales(u):
             nc.vector.tensor_copy(v_sc[u][:], tab_sc[:].bitcast(U8).indirect(lists[u][:]))
 
+        template_sc = {}
+
+        def gather_template_scales(half, room):
+            template_sc[half] = room
+            cols = S // 32
+            offsets = lists[TEMPLATE][:, half * cols : (half + 1) * cols]
+            nc.vector.tensor_copy(room, tab_sc[:].bitcast(U8).indirect(offsets))
+
         v_words = {}
 
-        def gather_words(name, tag, wanted):
-            tile = sbuf([P, sum(len(slices) for u, a, slices in wanted) * SLICE], U32, name, tag)
+        def gather_words(tile, place, wanted):
             cols = SLICE // 16
-            place = 0
             for u, a, slices in wanted:
                 offsets = lists[u][:, slices[0] * cols : (slices[-1] + 1) * cols]
                 nc.vector.tensor_copy(tile[:, place : place + len(slices) * SLICE], tab_w[a][:].indirect(offsets))
                 for s in slices:
                     v_words[u, a, s] = tile[:, place : place + SLICE]
                     place += SLICE
+            return place
 
         def moving_scale(u, a, cols):
             if u == SECOND and a == 1:
                 return second_sc_pass1[:].bitcast(U8)[:, cols]
+            if u == TEMPLATE:
+                half, lo = divmod(cols.start, S // 2)
+                return template_sc[half][LOWER * a : P, lo : lo + HALF]
             return v_sc[u][LOWER * a : P, cols]
 
         w1_bf = [sbuf([P, PACK * H], BF16, f"w1_bf{a}") for a in range(PASSES)]
         w1_codes = sbuf([P, PASSES, H], U32, "w1_codes")
         w1_sc = sbuf([P, PASSES, H], U8, "w1_sc")
 
-        def round_w1(a):
+        def round_w1(a, helped):
             src = w1_raw[a][:].rearrange("p j (g t i) -> p t g i j", t=PACK, i=8)
             dst = w1_bf[a][:].rearrange("p (t g i j) -> p t g i j", t=PACK, i=8, j=PACK)
-            for t in range(PACK):
+            for t in range(PACK - helped):
                 nc.scalar.copy(dst[:, t], src[:, t])
+            for t in range(PACK - helped, PACK):
+                nc.gpsimd.tensor_scalar(dst[:, t], src[:, t], 1.0, 0.0, MULT, ADD)
 
         def quantise_w1(a):
             nc.vector.quantize_mx(w1_codes[:, a, :].bitcast(FP8X4), w1_sc[:, a, :], w1_bf[a][:])
@@ -135,8 +142,7 @@ def tile_list_template_contact_readout_kernel(
                 return w2_codes[:, t, a, :].bitcast(FP4X4), w2_sc[:, t, a, :]
             return w3_codes[:, t, a, :].bitcast(FP8X4), w3_sc[:, t, a, :]
 
-        def project(s, order):
-            pair = next_pair()
+        def project(s, order, pair):
             banks = [psum.tile([P, PACK, HALF], F32, name=f"bank{pair + hf}") for hf in range(HALVES)]
             for u, a in order:
                 for hf in range(HALVES):
@@ -164,8 +170,8 @@ def tile_list_template_contact_readout_kernel(
                 nc.scalar.activation(root[:, hf], square[:, hf], ACT.Abs_reciprocal_sqrt, bias=1.0)
             return root
 
-        def damping_on_scalar(s, root):
-            damp = sbuf([P, HALVES, HALF, PACK], F32, f"damp{s}")
+        def damping_on_scalar(s, root, tag=None):
+            damp = sbuf([P, HALVES, HALF, PACK], F32, f"damp{s}", tag)
             for hf in range(HALVES):
                 nc.scalar.activation(damp[:, hf], root[:, hf], ACT.Square)
             return damp
@@ -179,11 +185,12 @@ def tile_list_template_contact_readout_kernel(
 
         out_view = out.rearrange("(c p) j -> p c j", p=P)
 
-        def readout(first, width, codes, scale, vector_tiles):
-            pair = next_pair()
+        def readout(first, width, codes, scale, banks, vector_tiles):
             result = sbuf([P, N_TILES, width], F32, f"result{first}")
-            for place, group in enumerate(((0, 1), (2,))):
-                y = psum.tile([P, len(group), width], F32, name=f"bank{pair + place}")
+            whole_banks = len(set(banks)) == N_TILES
+            for bank in sorted(set(banks), key=banks.index):
+                group = [c for c in range(N_TILES) if banks[c] == bank]
+                y = psum.tile([P, len(group), width], F32, name=f"bank{bank}")
                 for slot, c in enumerate(group):
                     nc.tensor.matmul_mx(
                         y[:, slot, :],
@@ -199,7 +206,10 @@ def tile_list_template_contact_readout_kernel(
                         nc.vector.tensor_scalar_add(result[:, c, :], y[:, slot, :], bias[:, c : c + 1])
                     else:
                         nc.scalar.activation(result[:, c, :], y[:, slot, :], ACT.Identity, bias=bias[:, c : c + 1])
-            nc.sync.dma_start(out_view[:, :, first : first + width], result[:])
+                    if whole_banks:
+                        nc.sync.dma_start(out_view[:, c, first : first + width], result[:, c, :])
+            if not whole_banks:
+                nc.sync.dma_start(out_view[:, :, first : first + width], result[:])
 
         nc.sync.dma_start(w2_raw[:], w2_words.rearrange("a p c -> p a c").bitcast(I32))
         nc.sync.dma_start(lists[SECOND][:], offs2)
@@ -228,9 +238,9 @@ def tile_list_template_contact_readout_kernel(
             nc.sync.dma_start(bias[:], b.rearrange("(c p) -> p c", p=P))
 
         gather_scales(FIRST)
-        round_w1(0)
-        round_w1(1)
         reorder(nc.gpsimd, w2_sc, w2_sc_raw, 2)
+        round_w1(0, 0)
+        round_w1(1, 1)
         reorder(nc.gpsimd, w3_sc, w3_sc_raw, 2)
         reorder(nc.gpsimd, w3_codes, w3_raw, 8)
         wo_bf = sbuf([P, N, PACK], BF16, "wo_bf")
@@ -244,64 +254,60 @@ def tile_list_template_contact_readout_kernel(
             return [(u, a, slices) for u, a in pairs]
 
         quantise_w1(0)
-        gather_words("picked0", None, of_slice(early, 0, 1, 2))
+        room = sbuf([P, 8 * SLICE], U32, "picked_first")
+        place = gather_words(room, 0, of_slice(early, 0, 1))
         quantise_w1(1)
-        gather_words("picked1", None, of_slice(late, 0) + of_slice(late, 1))
-        gather_scales(TEMPLATE)
-        d0 = project(0, early + late)
-        d1 = project(1, early + late)
-        gather_words(
-            "picked4",
-            "w3_raw",
-            of_slice(both, 0) + of_slice(late, 2) + of_slice(both, 1) + of_slice(early + late, 3),
-        )
+        gather_words(room, place, of_slice(late, 0) + of_slice(late, 1))
+        gather_template_scales(0, sbuf([P, S // 2], U8, "template_sc0")[:])
+        d0 = project(0, early + late, 0)
+        d1 = project(1, early + late, 2)
+        room = sbuf([P, 16 * SLICE], U32, "picked_second", "w3_raw")
+        place = gather_words(room, 0, of_slice(both, 0, 1) + of_slice(early, 2, 3) + of_slice(late, 2) + of_slice(late, 3))
+        gather_template_scales(1, room[:, place : place + SLICE].bitcast(U8)[:, 0 : S // 2])
+        gather_words(room, place + SLICE, of_slice(both[:1], 2, 3) + of_slice(both[1:], 2))
         root0 = root_of(0, d0)
         root1 = root_of(1, d1)
-        damp01 = sbuf([P, 2, HALVES, HALF, PACK], F32, "damp01", "wo_raw")
-        nc.gpsimd.tensor_tensor(damp01[:, 0], root0[:], root0[:], MULT)
-        nc.gpsimd.tensor_tensor(damp01[:, 1], root1[:], root1[:], MULT)
+        damp0 = sbuf([P, HALVES, HALF, PACK], F32, "damp0", "wo_raw")
+        nc.gpsimd.tensor_tensor(damp0[:], root0[:], root0[:], MULT)
 
-        t0 = project(0, both)
-        t0_sb = sbuf([P, HALVES, HALF, PACK], F32, "t0_sb")
-        for hf in range(HALVES):
-            nc.scalar.copy(t0_sb[:, hf], t0[hf])
+        t01 = sbuf([P, 2, HALVES, HALF, PACK], F32, "t01")
         h01 = sbuf([P, 2, HALVES, HALF, PACK], BF16, "h01")
-        nc.gpsimd.tensor_tensor(h01[:, 0], t0_sb[:], damp01[:, 0], MULT)
 
-        d2 = project(2, early + late)
-        damp2 = damping_on_scalar(2, root_of(2, d2))
-        t1 = project(1, both)
-        d3 = project(3, early + late)
-        damp3 = damping_on_scalar(3, root_of(3, d3))
-        product_on_vector(h01[:, 1], t1, damp01[:, 1])
-        gather_words("picked5", "root1", of_slice(both, 2))
-        t2 = project(2, both)
+        def product_on_gpsimd(s, damp):
+            template = project(s, both, 4 + 2 * s)
+            for hf in range(HALVES):
+                nc.scalar.copy(t01[:, s, hf], template[hf])
+            nc.gpsimd.tensor_tensor(h01[:, s], t01[:, s], damp[:], MULT)
 
-        planes = sbuf([P, N + 2 * SLICE], U8, "planes", "wo_raw")
+        product_on_gpsimd(0, damp0)
+        product_on_gpsimd(1, damping_on_scalar(1, root1, "root0"))
+
+        damp2 = damping_on_scalar(2, root_of(2, project(2, early + late, 0)))
+        damp3 = damping_on_scalar(3, root_of(3, project(3, early + late, 2)))
+
+        planes = sbuf([P, N + 2 * SLICE], U8, "planes", "root0")
         wo_sc = planes[:, 0:N]
         wo_codes = sbuf([P, N], U32, "wo_codes")
         for cols in (slice(0, 2 * P), slice(2 * P, N)):
             quantise(wo_codes[:, cols], wo_sc[:, cols], wo_bf[:, cols, :].rearrange("p n t -> p (n t)"))
         h_codes = sbuf([P, S], U32, "h_codes")
-        for s in range(2):
-            scale = planes[:, N + s * SLICE : N + (s + 1) * SLICE]
-            cols = slice(s * SLICE, (s + 1) * SLICE)
-            quantise(h_codes[:, cols], scale, h01[:, s].rearrange("p f n t -> p (f n t)"))
-            readout(s * SLICE, SLICE, h_codes[:, cols], scale, ())
+        quantise(h_codes[:, 0 : 2 * SLICE], planes[:, N : N + 2 * SLICE], h01[:].rearrange("p s f n t -> p (s f n t)"))
+        t2 = project(2, both, 4)
+        readout(0, 2 * SLICE, h_codes[:, 0 : 2 * SLICE], planes[:, N : N + 2 * SLICE], (6, 7, 0), ())
 
-        h2 = sbuf([P, HALVES, HALF, PACK], BF16, "h2", "t0_sb")
+        h2 = sbuf([P, HALVES, HALF, PACK], BF16, "h2", "t01")
         product_on_vector(h2, t2, damp2)
-        gather_words("picked6", "damp2", of_slice(both, 3))
-        t3 = project(3, both)
+        gather_words(sbuf([P, SLICE], U32, "picked_last", "damp2"), 0, of_slice(both[1:], 3))
+        t3 = project(3, both, 2)
         h_sc = sbuf([P, 2 * SLICE], U8, "h_sc")
         cols = slice(2 * SLICE, 3 * SLICE)
         quantise(h_codes[:, cols], h_sc[:, 0:SLICE], h2[:].rearrange("p f n t -> p (f n t)"))
-        readout(2 * SLICE, SLICE, h_codes[:, cols], h_sc[:, 0:SLICE], ())
+        readout(2 * SLICE, SLICE, h_codes[:, cols], h_sc[:, 0:SLICE], (1, 1, 4), ())
         h3 = sbuf([P, HALVES, HALF, PACK], BF16, "h3")
         product_on_vector(h3, t3, damp3)
         last = [slice(3 * SLICE + hf * HALF, 3 * SLICE + (hf + 1) * HALF) for hf in range(HALVES)]
         scales = [h_sc[:, SLICE + hf * HALF : SLICE + (hf + 1) * HALF] for hf in range(HALVES)]
         for hf in range(HALVES):
             quantise(h_codes[:, last[hf]], scales[hf], h3[:, hf].rearrange("p n t -> p (n t)"))
-        for hf in range(HALVES):
-            readout(last[hf].start, HALF, h_codes[:, last[hf]], scales[hf], (2,))
+        for hf, banks in enumerate(((5, 5, 6), (7, 7, 0))):
+            readout(last[hf].start, HALF, h_codes[:, last[hf]], scales[hf], banks, (2,))

@@ -177,8 +177,7 @@ def tile_list_template_contact_readout_kernel(
             return damp
 
         def product_on_vector(h, template, damp):
-            for hf in range(HALVES):
-                nc.vector.tensor_tensor(h[:, hf], template[hf], damp[:, hf], MULT)
+            nc.vector.tensor_tensor(h, template, damp, MULT)
 
         def quantise(codes, scale, values):
             nc.vector.quantize_mx(codes.bitcast(FP8X4), scale, values)
@@ -261,10 +260,10 @@ def tile_list_template_contact_readout_kernel(
         gather_template_scales(0, sbuf([P, S // 2], U8, "template_sc0")[:])
         d0 = project(0, early + late, 0)
         d1 = project(1, early + late, 2)
-        room = sbuf([P, 16 * SLICE], U32, "picked_second", "w3_raw")
+        room = sbuf([P, 17 * SLICE], U32, "picked_second", "w3_raw")
         place = gather_words(room, 0, of_slice(both, 0, 1) + of_slice(early, 2, 3) + of_slice(late, 2) + of_slice(late, 3))
         gather_template_scales(1, room[:, place : place + SLICE].bitcast(U8)[:, 0 : S // 2])
-        gather_words(room, place + SLICE, of_slice(both[:1], 2, 3) + of_slice(both[1:], 2))
+        gather_words(room, place + SLICE, of_slice(both, 2, 3))
         root0 = root_of(0, d0)
         root1 = root_of(1, d1)
         damp0 = sbuf([P, HALVES, HALF, PACK], F32, "damp0", "wo_raw")
@@ -282,32 +281,35 @@ def tile_list_template_contact_readout_kernel(
         product_on_gpsimd(0, damp0)
         product_on_gpsimd(1, damping_on_scalar(1, root1, "root0"))
 
-        damp2 = damping_on_scalar(2, root_of(2, project(2, early + late, 0)))
+        root2 = root_of(2, project(2, early + late, 0))
+        damp2 = sbuf([P, HALVES, HALF, PACK], F32, "damp2")
+        nc.scalar.activation(damp2[:, 0], root2[:, 0], ACT.Square)
+        nc.gpsimd.tensor_tensor(damp2[:, 1], root2[:, 1], root2[:, 1], MULT)
         damp3 = damping_on_scalar(3, root_of(3, project(3, early + late, 2)))
+        t2 = project(2, both, 4)
+        t3 = project(3, both, 2)
 
-        planes = sbuf([P, N + 2 * SLICE], U8, "planes", "root0")
+        planes = sbuf([P, N + 2 * SLICE], U8, "planes", "root2")
         wo_sc = planes[:, 0:N]
         wo_codes = sbuf([P, N], U32, "wo_codes")
         for cols in (slice(0, 2 * P), slice(2 * P, N)):
             quantise(wo_codes[:, cols], wo_sc[:, cols], wo_bf[:, cols, :].rearrange("p n t -> p (n t)"))
         h_codes = sbuf([P, S], U32, "h_codes")
         quantise(h_codes[:, 0 : 2 * SLICE], planes[:, N : N + 2 * SLICE], h01[:].rearrange("p s f n t -> p (s f n t)"))
-        t2 = project(2, both, 4)
         readout(0, 2 * SLICE, h_codes[:, 0 : 2 * SLICE], planes[:, N : N + 2 * SLICE], (6, 7, 0), ())
 
-        h2 = sbuf([P, HALVES, HALF, PACK], BF16, "h2", "t01")
-        product_on_vector(h2, t2, damp2)
-        gather_words(sbuf([P, SLICE], U32, "picked_last", "damp2"), 0, of_slice(both[1:], 3))
-        t3 = project(3, both, 2)
+        h23 = sbuf([P, 2, HALVES, HALF, PACK], BF16, "h23", "h01")
         h_sc = sbuf([P, 2 * SLICE], U8, "h_sc")
+        product_on_vector(h23[:, 0, 0], t2[0], damp2[:, 0])
+        product_on_vector(h23[:, 0, 1], t2[1], damp2[:, 1])
+        product_on_vector(h23[:, 1, 0], t3[0], damp3[:, 0])
         cols = slice(2 * SLICE, 3 * SLICE)
-        quantise(h_codes[:, cols], h_sc[:, 0:SLICE], h2[:].rearrange("p f n t -> p (f n t)"))
-        readout(2 * SLICE, SLICE, h_codes[:, cols], h_sc[:, 0:SLICE], (1, 1, 4), ())
-        h3 = sbuf([P, HALVES, HALF, PACK], BF16, "h3")
-        product_on_vector(h3, t3, damp3)
+        quantise(h_codes[:, cols], h_sc[:, 0:SLICE], h23[:, 0].rearrange("p f n t -> p (f n t)"))
+        product_on_vector(h23[:, 1, 1], t3[1], damp3[:, 1])
         last = [slice(3 * SLICE + hf * HALF, 3 * SLICE + (hf + 1) * HALF) for hf in range(HALVES)]
         scales = [h_sc[:, SLICE + hf * HALF : SLICE + (hf + 1) * HALF] for hf in range(HALVES)]
         for hf in range(HALVES):
-            quantise(h_codes[:, last[hf]], scales[hf], h3[:, hf].rearrange("p n t -> p (n t)"))
+            quantise(h_codes[:, last[hf]], scales[hf], h23[:, 1, hf].rearrange("p n t -> p (n t)"))
+        readout(2 * SLICE, SLICE, h_codes[:, cols], h_sc[:, 0:SLICE], (1, 1, 4), (2,))
         for hf, banks in enumerate(((5, 5, 6), (7, 7, 0))):
             readout(last[hf].start, HALF, h_codes[:, last[hf]], scales[hf], banks, (2,))

@@ -126,7 +126,6 @@ def tile_list_template_contact_readout_kernel(
         w2_codes = sbuf([P, PACK, PASSES, 2 * P], U8, "w2_codes")
         w3_codes = sbuf([P, PACK, PASSES, P], U32, "w3_codes")
         w2_sc = sbuf([P, PACK, PASSES, P], U8, "w2_sc")
-        w3_sc = sbuf([P, PACK, PASSES, P], U8, "w3_sc")
 
         def reorder(engine, dst, src, run):
             engine.tensor_copy(
@@ -184,9 +183,8 @@ def tile_list_template_contact_readout_kernel(
 
         out_view = out.rearrange("(c p) j -> p c j", p=P)
 
-        def readout(first, width, codes, scale, banks, vector_tiles):
+        def readout(first, width, codes, scale, banks, vector_tiles, by_tile):
             result = sbuf([P, N_TILES, width], F32, f"result{first}")
-            whole_banks = len(set(banks)) == N_TILES
             for bank in sorted(set(banks), key=banks.index):
                 group = [c for c in range(N_TILES) if banks[c] == bank]
                 y = psum.tile([P, len(group), width], F32, name=f"bank{bank}")
@@ -205,9 +203,9 @@ def tile_list_template_contact_readout_kernel(
                         nc.vector.tensor_scalar_add(result[:, c, :], y[:, slot, :], bias[:, c : c + 1])
                     else:
                         nc.scalar.activation(result[:, c, :], y[:, slot, :], ACT.Identity, bias=bias[:, c : c + 1])
-                    if whole_banks:
+                    if by_tile:
                         nc.sync.dma_start(out_view[:, c, first : first + width], result[:, c, :])
-            if not whole_banks:
+            if not by_tile:
                 nc.sync.dma_start(out_view[:, :, first : first + width], result[:])
 
         nc.sync.dma_start(w2_raw[:], w2_words.rearrange("a p c -> p a c").bitcast(I32))
@@ -215,10 +213,13 @@ def tile_list_template_contact_readout_kernel(
         nc.sync.dma_start(lists[FIRST][:], offs)
         for q in range(QUADRANTS):
             nc.sync.dma_start(tab_sc[32 * q : 32 * q + 2 * LOWER, :], tab_scales[:, 4 * q : 4 * q + 4, :].bitcast(I32))
-        load_w1(0)
-        load_weight_scales(w2_scales, w2_sc_raw)
         load_table_words(0)
+        load_weight_scales(w2_scales, w2_sc_raw)
+        load_w1(0)
+        nc.sync.dma_start(lists[TEMPLATE][:], offs3)
         load_w1(1)
+        load_weight_scales(w3_scales, w3_sc_raw)
+        load_table_words(1)
         reorder(nc.vector, w2_codes, w2_raw, 4)
         gather_scales(SECOND)
         for q in range(QUADRANTS):
@@ -226,9 +227,6 @@ def tile_list_template_contact_readout_kernel(
                 second_sc_pass1[32 * q : 32 * q + 4, :],
                 v_sc[SECOND][32 * q + LOWER : 32 * q + LOWER + 4, :].bitcast(I32),
             )
-        load_table_words(1)
-        nc.sync.dma_start(lists[TEMPLATE][:], offs3)
-        load_weight_scales(w3_scales, w3_sc_raw)
         nc.sync.dma_start(w3_raw[:], w3_words.rearrange("a p c i -> p a (c i)").bitcast(I32))
         wo_rows = wo.rearrange("(g t i) n -> t g i n", t=PACK, i=8)
         for t in range(PACK):
@@ -238,78 +236,79 @@ def tile_list_template_contact_readout_kernel(
 
         gather_scales(FIRST)
         reorder(nc.gpsimd, w2_sc, w2_sc_raw, 2)
-        round_w1(0, 0)
+        round_w1(0, 1)
         round_w1(1, 1)
-        reorder(nc.gpsimd, w3_sc, w3_sc_raw, 2)
-        reorder(nc.gpsimd, w3_codes, w3_raw, 8)
-        wo_bf = sbuf([P, N, PACK], BF16, "wo_bf")
-        nc.gpsimd.tensor_scalar(wo_bf[:], wo_raw[:].rearrange("p t n -> p n t"), 1.0, 0.0, MULT, ADD)
 
-        early = ((FIRST, 0), (SECOND, 0))
+        early = ((SECOND, 0), (FIRST, 0))
         late = ((SECOND, 1), (FIRST, 1))
         both = ((TEMPLATE, 0), (TEMPLATE, 1))
 
         def of_slice(pairs, *slices):
             return [(u, a, slices) for u, a in pairs]
 
-        quantise_w1(0)
-        room = sbuf([P, 8 * SLICE], U32, "picked_first")
-        place = gather_words(room, 0, of_slice(early, 0, 1))
-        quantise_w1(1)
-        gather_words(room, place, of_slice(late, 0) + of_slice(late, 1))
+        room = sbuf([P, 10 * SLICE], U32, "picked_first")
+        place = gather_words(room, 0, of_slice(early, 0, 1, 2))
         gather_template_scales(0, sbuf([P, S // 2], U8, "template_sc0")[:])
+        quantise_w1(0)
+        quantise_w1(1)
+        w3_sc = sbuf([P, PACK, PASSES, P], U8, "w3_sc", "w1_bf1")
+        reorder(nc.gpsimd, w3_sc, w3_sc_raw, 2)
+        reorder(nc.gpsimd, w3_codes, w3_raw, 8)
+        wo_bf = sbuf([P, N, PACK], BF16, "wo_bf")
+        nc.gpsimd.tensor_scalar(wo_bf[:], wo_raw[:].rearrange("p t n -> p n t"), 1.0, 0.0, MULT, ADD)
+        gather_words(room, place, of_slice(late, 0) + of_slice(late, 1))
         d0 = project(0, early + late, 0)
         d1 = project(1, early + late, 2)
-        room = sbuf([P, 17 * SLICE], U32, "picked_second", "w3_raw")
-        place = gather_words(room, 0, of_slice(both, 0, 1) + of_slice(early, 2, 3) + of_slice(late, 2) + of_slice(late, 3))
+        room = sbuf([P, 13 * SLICE], U32, "picked_second", "w3_raw")
+        place = gather_words(
+            room, 0, of_slice(both, 0, 1) + of_slice(late, 2) + of_slice(early + late, 3)
+        )
         gather_template_scales(1, room[:, place : place + SLICE].bitcast(U8)[:, 0 : S // 2])
-        gather_words(room, place + SLICE, of_slice(both, 2, 3))
+        gather_words(room, place + SLICE, of_slice(both[:1], 2, 3))
         root0 = root_of(0, d0)
         root1 = root_of(1, d1)
-        damp0 = sbuf([P, HALVES, HALF, PACK], F32, "damp0", "wo_raw")
-        nc.gpsimd.tensor_tensor(damp0[:], root0[:], root0[:], MULT)
-
-        t01 = sbuf([P, 2, HALVES, HALF, PACK], F32, "t01")
+        damp01 = sbuf([P, 2, HALVES, HALF, PACK], F32, "damp01", "wo_raw")
+        nc.gpsimd.tensor_tensor(damp01[:, 0], root0[:], root0[:], MULT)
+        nc.gpsimd.tensor_tensor(damp01[:, 1], root1[:], root1[:], MULT)
+        t0 = project(0, both, 4)
+        t0_sb = sbuf([P, HALVES, HALF, PACK], F32, "t0_sb")
+        for hf in range(HALVES):
+            nc.scalar.copy(t0_sb[:, hf], t0[hf])
         h01 = sbuf([P, 2, HALVES, HALF, PACK], BF16, "h01")
+        nc.gpsimd.tensor_tensor(h01[:, 0], t0_sb[:], damp01[:, 0], MULT)
 
-        def product_on_gpsimd(s, damp):
-            template = project(s, both, 4 + 2 * s)
-            for hf in range(HALVES):
-                nc.scalar.copy(t01[:, s, hf], template[hf])
-            nc.gpsimd.tensor_tensor(h01[:, s], t01[:, s], damp[:], MULT)
-
-        product_on_gpsimd(0, damp0)
-        product_on_gpsimd(1, damping_on_scalar(1, root1, "root0"))
-
-        root2 = root_of(2, project(2, early + late, 0))
-        damp2 = sbuf([P, HALVES, HALF, PACK], F32, "damp2")
-        nc.scalar.activation(damp2[:, 0], root2[:, 0], ACT.Square)
-        nc.gpsimd.tensor_tensor(damp2[:, 1], root2[:, 1], root2[:, 1], MULT)
+        damp2 = damping_on_scalar(2, root_of(2, project(2, early + late, 0)))
+        t1 = project(1, both, 6)
         damp3 = damping_on_scalar(3, root_of(3, project(3, early + late, 2)))
+        for hf in range(HALVES):
+            product_on_vector(h01[:, 1, hf], t1[hf], damp01[:, 1, hf])
+        gather_words(sbuf([P, SLICE], U32, "picked_third", "root1"), 0, of_slice(both[1:], 2))
         t2 = project(2, both, 4)
-        t3 = project(3, both, 2)
 
-        planes = sbuf([P, N + 2 * SLICE], U8, "planes", "root2")
+        planes = sbuf([P, N + 2 * SLICE], U8, "planes", "wo_raw")
         wo_sc = planes[:, 0:N]
         wo_codes = sbuf([P, N], U32, "wo_codes")
         for cols in (slice(0, 2 * P), slice(2 * P, N)):
             quantise(wo_codes[:, cols], wo_sc[:, cols], wo_bf[:, cols, :].rearrange("p n t -> p (n t)"))
         h_codes = sbuf([P, S], U32, "h_codes")
         quantise(h_codes[:, 0 : 2 * SLICE], planes[:, N : N + 2 * SLICE], h01[:].rearrange("p s f n t -> p (s f n t)"))
-        readout(0, 2 * SLICE, h_codes[:, 0 : 2 * SLICE], planes[:, N : N + 2 * SLICE], (6, 7, 0), ())
+        readout(0, 2 * SLICE, h_codes[:, 0 : 2 * SLICE], planes[:, N : N + 2 * SLICE], (0, 1, 2), (), True)
 
-        h23 = sbuf([P, 2, HALVES, HALF, PACK], BF16, "h23", "h01")
+        h2 = sbuf([P, HALVES, HALF, PACK], BF16, "h2", "t0_sb")
+        h3 = sbuf([P, HALVES, HALF, PACK], BF16, "h3")
         h_sc = sbuf([P, 2 * SLICE], U8, "h_sc")
-        product_on_vector(h23[:, 0, 0], t2[0], damp2[:, 0])
-        product_on_vector(h23[:, 0, 1], t2[1], damp2[:, 1])
-        product_on_vector(h23[:, 1, 0], t3[0], damp3[:, 0])
+        product_on_vector(h2[:, 0], t2[0], damp2[:, 0])
+        gather_words(sbuf([P, SLICE], U32, "picked_last", "h01"), 0, of_slice(both[1:], 3))
+        t3 = project(3, both, 6)
+        product_on_vector(h2[:, 1], t2[1], damp2[:, 1])
         cols = slice(2 * SLICE, 3 * SLICE)
-        quantise(h_codes[:, cols], h_sc[:, 0:SLICE], h23[:, 0].rearrange("p f n t -> p (f n t)"))
-        product_on_vector(h23[:, 1, 1], t3[1], damp3[:, 1])
+        quantise(h_codes[:, cols], h_sc[:, 0:SLICE], h2[:].rearrange("p f n t -> p (f n t)"))
+        readout(2 * SLICE, SLICE, h_codes[:, cols], h_sc[:, 0:SLICE], (3, 3, 4), (), True)
+        for hf in range(HALVES):
+            product_on_vector(h3[:, hf], t3[hf], damp3[:, hf])
         last = [slice(3 * SLICE + hf * HALF, 3 * SLICE + (hf + 1) * HALF) for hf in range(HALVES)]
         scales = [h_sc[:, SLICE + hf * HALF : SLICE + (hf + 1) * HALF] for hf in range(HALVES)]
         for hf in range(HALVES):
-            quantise(h_codes[:, last[hf]], scales[hf], h23[:, 1, hf].rearrange("p n t -> p (n t)"))
-        readout(2 * SLICE, SLICE, h_codes[:, cols], h_sc[:, 0:SLICE], (1, 1, 4), (2,))
-        for hf, banks in enumerate(((5, 5, 6), (7, 7, 0))):
-            readout(last[hf].start, HALF, h_codes[:, last[hf]], scales[hf], banks, (2,))
+            quantise(h_codes[:, last[hf]], scales[hf], h3[:, hf].rearrange("p n t -> p (n t)"))
+        for hf, banks in enumerate(((5, 5, 0), (1, 1, 2))):
+            readout(last[hf].start, HALF, h_codes[:, last[hf]], scales[hf], banks, (2,), False)

@@ -26,6 +26,7 @@ SLICES = S // SLICE
 HALVES = SLICE // HALF
 N_TILES = N // P
 QUADRANTS = 4
+ROWS = 4
 LOWER = 4
 FIRST, SECOND, TEMPLATE = 0, 1, 2
 
@@ -44,6 +45,9 @@ def tile_list_template_contact_readout_kernel(
         lists = [keep.tile([P, S // 16], U16, name=f"list{u}") for u in range(3)]
         tab_w = [sbuf([P, T], U32, f"tab_w{a}") for a in range(PASSES)]
         tab_sc = sbuf([P, T // 4], I32, "tab_sc")
+        tab_rows = sbuf([P, T // 4], I32, "tab_rows")
+        template_rows = sbuf([P, S // 2], U8, "template_rows")
+        template_sc = sbuf([P, PASSES, S // 8], I32, "template_sc")
         w1_raw = [sbuf([P, PACK, H], F32, f"w1_raw{a}") for a in range(PASSES)]
         w2_raw = sbuf([P, PASSES, H // 2], I32, "w2_raw")
         w3_raw = sbuf([P, PASSES, H], I32, "w3_raw")
@@ -56,12 +60,15 @@ def tile_list_template_contact_readout_kernel(
         warm_in = sbuf([P, 1], F32, "warm_in")
         warm_out = sbuf([P, 1], F32, "warm_out")
 
-        nc.vector.memset(tab_sc[:], 0)
+        nc.gpsimd.memset(tab_sc[:], 0)
+        nc.vector.memset(tab_rows[32:64, :], 0)
+        nc.vector.memset(tab_rows[64:P, :], 0)
         nc.gpsimd.memset(warm_in[:], 1.0)
         nc.scalar.activation(warm_out[:], warm_in[:], ACT.Abs_reciprocal_sqrt)
         nc.gpsimd.memset(w2_sc_raw[:], 0)
         nc.gpsimd.memset(w3_sc_raw[:], 0)
         nc.gpsimd.memset(second_sc_pass1[:], 0)
+        nc.gpsimd.memset(template_sc[:], 0)
 
         def load_table_words(a):
             nc.sync.dma_start(tab_w[a][:].bitcast(I32), tab_words[a].rearrange("p t i -> p (t i)").bitcast(I32))
@@ -71,22 +78,11 @@ def tile_list_template_contact_readout_kernel(
             nc.sync.dma_start(w1_raw[a][:], rows)
 
         def load_weight_scales(scales, raw):
-            for q in range(QUADRANTS):
-                nc.sync.dma_start(
-                    raw[32 * q : 32 * q + 4, :, :],
-                    scales[:, 4 * q : 4 * q + 4, :].rearrange("a r c -> r a c").bitcast(I32),
-                )
+            for r in range(ROWS):
+                nc.sync.dma_start(raw[r:P:32, :, :], scales[:, r:16:ROWS, :].rearrange("a q c -> q a c").bitcast(I32))
 
         def gather_scales(u):
             nc.vector.tensor_copy(v_sc[u][:], tab_sc[:].bitcast(U8).indirect(lists[u][:]))
-
-        template_sc = {}
-
-        def gather_template_scales(half, room):
-            template_sc[half] = room
-            cols = S // 32
-            offsets = lists[TEMPLATE][:, half * cols : (half + 1) * cols]
-            nc.vector.tensor_copy(room, tab_sc[:].bitcast(U8).indirect(offsets))
 
         v_words = {}
 
@@ -104,8 +100,9 @@ def tile_list_template_contact_readout_kernel(
             if u == SECOND and a == 1:
                 return second_sc_pass1[:].bitcast(U8)[:, cols]
             if u == TEMPLATE:
-                half, lo = divmod(cols.start, S // 2)
-                return template_sc[half][LOWER * a : P, lo : lo + HALF]
+                if cols.start < S // 2:
+                    return template_first[LOWER * a : P, cols]
+                return template_sc[:, a, :].bitcast(U8)[:, cols.start - S // 2 : cols.stop - S // 2]
             return v_sc[u][LOWER * a : P, cols]
 
         w1_bf = [sbuf([P, PACK * H], BF16, f"w1_bf{a}") for a in range(PASSES)]
@@ -124,13 +121,13 @@ def tile_list_template_contact_readout_kernel(
             nc.vector.quantize_mx(w1_codes[:, a, :].bitcast(FP8X4), w1_sc[:, a, :], w1_bf[a][:])
 
         w2_codes = sbuf([P, PACK, PASSES, 2 * P], U8, "w2_codes")
-        w3_codes = sbuf([P, PACK, PASSES, P], U32, "w3_codes")
+        w3_sc = sbuf([P, PACK, PASSES, P], U8, "w3_sc")
         w2_sc = sbuf([P, PACK, PASSES, P], U8, "w2_sc")
 
-        def reorder(engine, dst, src, run):
-            engine.tensor_copy(
-                dst[:].bitcast(I32).rearrange("p t a (g e) -> p t (a g) e", e=run),
-                src[:].rearrange("p a (g t e) -> p t (a g) e", t=PACK, e=run),
+        def reorder(copy, dst, src, run):
+            copy(
+                dst[:].bitcast(U32).rearrange("p t a (g e) -> p t (a g) e", e=run),
+                src[:].bitcast(U32).rearrange("p a (g t e) -> p t (a g) e", t=PACK, e=run),
             )
 
         def weight(u, a, t):
@@ -208,34 +205,36 @@ def tile_list_template_contact_readout_kernel(
             if not by_tile:
                 nc.sync.dma_start(out_view[:, :, first : first + width], result[:])
 
-        nc.sync.dma_start(w2_raw[:], w2_words.rearrange("a p c -> p a c").bitcast(I32))
-        nc.sync.dma_start(lists[SECOND][:], offs2)
-        nc.sync.dma_start(lists[FIRST][:], offs)
+        nc.sync.dma_start(lists[TEMPLATE][:], offs3)
+        nc.sync.dma_start(tab_rows[0:32, :], tab_scales.rearrange("a q t -> q a t").bitcast(I32))
         for q in range(QUADRANTS):
             nc.sync.dma_start(tab_sc[32 * q : 32 * q + 2 * LOWER, :], tab_scales[:, 4 * q : 4 * q + 4, :].bitcast(I32))
+        nc.sync.dma_start(lists[SECOND][:], offs2)
         load_table_words(0)
-        load_weight_scales(w2_scales, w2_sc_raw)
+        nc.sync.dma_start(lists[FIRST][:], offs)
+        nc.sync.dma_start(w2_raw[:], w2_words.rearrange("a p c -> p a c").bitcast(I32))
         load_w1(0)
-        nc.sync.dma_start(lists[TEMPLATE][:], offs3)
+        load_weight_scales(w2_scales, w2_sc_raw)
         load_w1(1)
-        load_weight_scales(w3_scales, w3_sc_raw)
-        load_table_words(1)
-        reorder(nc.vector, w2_codes, w2_raw, 4)
+        nc.vector.tensor_copy(template_rows[:], tab_rows[:].bitcast(U8).indirect(lists[TEMPLATE][:, S // 32 :]))
+        reorder(nc.scalar.copy, w2_codes, w2_raw, 4)
         gather_scales(SECOND)
-        for q in range(QUADRANTS):
-            nc.sync.dma_start(
-                second_sc_pass1[32 * q : 32 * q + 4, :],
-                v_sc[SECOND][32 * q + LOWER : 32 * q + LOWER + 4, :].bitcast(I32),
-            )
+        for r in range(ROWS):
+            nc.sync.dma_start(second_sc_pass1[r:P:32, :], v_sc[SECOND][LOWER + r : P : 32, :].bitcast(I32))
+        load_table_words(1)
         nc.sync.dma_start(w3_raw[:], w3_words.rearrange("a p c i -> p a (c i)").bitcast(I32))
+        load_weight_scales(w3_scales, w3_sc_raw)
         wo_rows = wo.rearrange("(g t i) n -> t g i n", t=PACK, i=8)
         for t in range(PACK):
             nc.sync.dma_start(wo_raw[:, t, :], wo_rows[t])
+        for q in range(QUADRANTS):
+            nc.sync.dma_start(
+                template_sc[32 * q : 32 * q + ROWS, :, :], template_rows[8 * q : 8 * q + 8, :].bitcast(I32)
+            )
         with nc.allow_non_contiguous_dma(reason="one bias value for each partition and output tile"):
             nc.sync.dma_start(bias[:], b.rearrange("(c p) -> p c", p=P))
 
-        gather_scales(FIRST)
-        reorder(nc.gpsimd, w2_sc, w2_sc_raw, 2)
+        reorder(nc.gpsimd.tensor_copy, w2_sc, w2_sc_raw, 2)
         round_w1(0, 1)
         round_w1(1, 1)
 
@@ -246,25 +245,27 @@ def tile_list_template_contact_readout_kernel(
         def of_slice(pairs, *slices):
             return [(u, a, slices) for u, a in pairs]
 
-        room = sbuf([P, 10 * SLICE], U32, "picked_first")
-        place = gather_words(room, 0, of_slice(early, 0, 1, 2))
-        gather_template_scales(0, sbuf([P, S // 2], U8, "template_sc0")[:])
+        room = sbuf([P, 6 * SLICE], U32, "picked_head")
+        place = gather_words(room, 0, of_slice(early[:1], 0, 1, 2))
+        gather_scales(FIRST)
+        gather_words(room, place, of_slice(early[1:], 0, 1, 2))
         quantise_w1(0)
         quantise_w1(1)
-        w3_sc = sbuf([P, PACK, PASSES, P], U8, "w3_sc", "w1_bf1")
-        reorder(nc.gpsimd, w3_sc, w3_sc_raw, 2)
-        reorder(nc.gpsimd, w3_codes, w3_raw, 8)
+        w3_codes = sbuf([P, PACK, PASSES, P], U32, "w3_codes", "w1_bf1")
+        reorder(nc.gpsimd.tensor_copy, w3_codes, w3_raw, 8)
+        reorder(nc.gpsimd.tensor_copy, w3_sc, w3_sc_raw, 2)
         wo_bf = sbuf([P, N, PACK], BF16, "wo_bf")
         nc.gpsimd.tensor_scalar(wo_bf[:], wo_raw[:].rearrange("p t n -> p n t"), 1.0, 0.0, MULT, ADD)
-        gather_words(room, place, of_slice(late, 0) + of_slice(late, 1))
+        gather_words(sbuf([P, SLICE], U32, "picked_start", "w1_raw0"), 0, of_slice(late[:1], 0))
+        gather_words(sbuf([P, 3 * SLICE], U32, "picked_first", "w1_raw1"), 0, of_slice(late[1:], 0) + of_slice(late, 1))
         d0 = project(0, early + late, 0)
         d1 = project(1, early + late, 2)
-        room = sbuf([P, 13 * SLICE], U32, "picked_second", "w3_raw")
-        place = gather_words(
-            room, 0, of_slice(both, 0, 1) + of_slice(late, 2) + of_slice(early + late, 3)
+        template_first = sbuf([P, S // 2], U8, "template_first", "w1_raw0")
+        nc.vector.tensor_copy(template_first[:], tab_sc[:].bitcast(U8).indirect(lists[TEMPLATE][:, 0 : S // 32]))
+        room = sbuf([P, 12 * SLICE], U32, "picked_second", "w3_sc_raw")
+        gather_words(
+            room, 0, of_slice(both, 0, 1) + of_slice(late, 2) + of_slice(early + late, 3) + of_slice(both[:1], 2, 3)
         )
-        gather_template_scales(1, room[:, place : place + SLICE].bitcast(U8)[:, 0 : S // 2])
-        gather_words(room, place + SLICE, of_slice(both[:1], 2, 3))
         root0 = root_of(0, d0)
         root1 = root_of(1, d1)
         damp01 = sbuf([P, 2, HALVES, HALF, PACK], F32, "damp01", "wo_raw")

@@ -138,16 +138,22 @@ def tile_list_template_contact_readout_kernel(
                 return w2_codes[:, t, a, :].bitcast(FP4X4), w2_sc[:, t, a, :]
             return w3_codes[:, t, a, :].bitcast(FP8X4), w3_sc[:, t, a, :]
 
-        def project(s, order, pair):
-            banks = [psum.tile([P, PACK, HALF], F32, name=f"bank{pair + hf}") for hf in range(HALVES)]
-            for u, a in order:
+        def project(slices, order, first_bank):
+            banks = {
+                (s, hf): psum.tile([P, PACK, HALF], F32, name=f"bank{first_bank + HALVES * place + hf}")
+                for place, s in enumerate(slices)
+                for hf in range(HALVES)
+            }
+            steps = [(pair, s) for pair in order[:-2] for s in slices]
+            steps.extend((pair, s) for s in slices for pair in order[-2:])
+            for (u, a), s in steps:
                 for hf in range(HALVES):
                     local = slice(hf * HALF, (hf + 1) * HALF)
                     cols = slice(s * SLICE + hf * HALF, s * SLICE + (hf + 1) * HALF)
                     for t in range(PACK):
                         codes, scale = weight(u, a, t)
                         nc.tensor.matmul_mx(
-                            banks[hf][:, t, :],
+                            banks[s, hf][:, t, :],
                             lhsT=codes,
                             lhsT_scale=scale,
                             rhs=v_words[u, a, s][:, local].bitcast(FP8X4),
@@ -155,7 +161,7 @@ def tile_list_template_contact_readout_kernel(
                             start=((u, a) == order[0] and t == 0),
                             stop=((u, a) == order[-1] and t == PACK - 1),
                         )
-            return [bank[:].rearrange("p t n -> p n t") for bank in banks]
+            return [[banks[s, hf][:].rearrange("p t n -> p n t") for hf in range(HALVES)] for s in slices]
 
         def root_of(s, d):
             square = sbuf([P, HALVES, HALF, PACK], F32, f"square{s}", f"square{s % 2}")
@@ -258,8 +264,7 @@ def tile_list_template_contact_readout_kernel(
         nc.gpsimd.tensor_scalar(wo_bf[:], wo_raw[:].rearrange("p t n -> p n t"), 1.0, 0.0, MULT, ADD)
         gather_words(sbuf([P, SLICE], U32, "picked_start", "w1_raw0"), 0, of_slice(late[:1], 0))
         gather_words(sbuf([P, 3 * SLICE], U32, "picked_first", "w1_raw1"), 0, of_slice(late[1:], 0) + of_slice(late, 1))
-        d0 = project(0, early + late, 0)
-        d1 = project(1, early + late, 2)
+        d0, d1 = project((0, 1), early + late, 0)
         template_first = sbuf([P, S // 2], U8, "template_first", "w1_raw0")
         nc.vector.tensor_copy(template_first[:], tab_sc[:].bitcast(U8).indirect(lists[TEMPLATE][:, 0 : S // 32]))
         room = sbuf([P, 12 * SLICE], U32, "picked_second", "w3_sc_raw")
@@ -271,20 +276,20 @@ def tile_list_template_contact_readout_kernel(
         damp01 = sbuf([P, 2, HALVES, HALF, PACK], F32, "damp01", "wo_raw")
         nc.gpsimd.tensor_tensor(damp01[:, 0], root0[:], root0[:], MULT)
         nc.gpsimd.tensor_tensor(damp01[:, 1], root1[:], root1[:], MULT)
-        t0 = project(0, both, 4)
+        t0 = project((0,), both, 4)[0]
         t0_sb = sbuf([P, HALVES, HALF, PACK], F32, "t0_sb")
         for hf in range(HALVES):
             nc.scalar.copy(t0_sb[:, hf], t0[hf])
         h01 = sbuf([P, 2, HALVES, HALF, PACK], BF16, "h01")
         nc.gpsimd.tensor_tensor(h01[:, 0], t0_sb[:], damp01[:, 0], MULT)
 
-        damp2 = damping_on_scalar(2, root_of(2, project(2, early + late, 0)))
-        t1 = project(1, both, 6)
-        damp3 = damping_on_scalar(3, root_of(3, project(3, early + late, 2)))
+        damp2 = damping_on_scalar(2, root_of(2, project((2,), early + late, 0)[0]))
+        t1 = project((1,), both, 6)[0]
+        damp3 = damping_on_scalar(3, root_of(3, project((3,), early + late, 2)[0]))
         for hf in range(HALVES):
             product_on_vector(h01[:, 1, hf], t1[hf], damp01[:, 1, hf])
         gather_words(sbuf([P, SLICE], U32, "picked_third", "root1"), 0, of_slice(both[1:], 2))
-        t2 = project(2, both, 4)
+        t2 = project((2,), both, 4)[0]
 
         planes = sbuf([P, N + 2 * SLICE], U8, "planes", "wo_raw")
         wo_sc = planes[:, 0:N]
@@ -300,7 +305,7 @@ def tile_list_template_contact_readout_kernel(
         h_sc = sbuf([P, 2 * SLICE], U8, "h_sc")
         product_on_vector(h2[:, 0], t2[0], damp2[:, 0])
         gather_words(sbuf([P, SLICE], U32, "picked_last", "h01"), 0, of_slice(both[1:], 3))
-        t3 = project(3, both, 6)
+        t3 = project((3,), both, 6)[0]
         product_on_vector(h2[:, 1], t2[1], damp2[:, 1])
         cols = slice(2 * SLICE, 3 * SLICE)
         quantise(h_codes[:, cols], h_sc[:, 0:SLICE], h2[:].rearrange("p f n t -> p (f n t)"))

@@ -37,17 +37,21 @@ def tile_list_template_contact_readout_kernel(
     nc = tc.nc
     with ExitStack() as ctx:
         keep = ctx.enter_context(tc.tile_pool(name="keep", bufs=1))
+        over = ctx.enter_context(tc.tile_pool(name="over", bufs=1))
         psum = ctx.enter_context(tc.psum_pool(name="psum", bufs=1))
 
         def sbuf(shape, dtype, name, tag=None):
             return keep.tile(shape, dtype, name=name, tag=tag or name, align_bytes=64)
 
+        def placed(shape, dtype, name, offset):
+            return over.tile(shape, dtype, name=name, align_bytes=64, offset=offset)
+
         lists = [keep.tile([P, S // 16], U16, name=f"list{u}") for u in range(3)]
         tab_w = [sbuf([P, T], U32, f"tab_w{a}") for a in range(PASSES)]
         tab_sc = sbuf([P, T // 4], I32, "tab_sc")
         tab_rows = sbuf([P, T // 4], I32, "tab_rows")
-        template_rows = sbuf([P, S // 2], U8, "template_rows")
-        template_sc = sbuf([P, PASSES, S // 8], I32, "template_sc")
+        template_rows = sbuf([P, S], U8, "template_rows")
+        template_sc = sbuf([P, PASSES, S // 4], I32, "template_sc")
         w1_raw = [sbuf([P, PACK, H], F32, f"w1_raw{a}") for a in range(PASSES)]
         w2_raw = sbuf([P, PASSES, H // 2], I32, "w2_raw")
         w3_raw = sbuf([P, PASSES, H], I32, "w3_raw")
@@ -60,15 +64,11 @@ def tile_list_template_contact_readout_kernel(
         warm_in = sbuf([P, 1], F32, "warm_in")
         warm_out = sbuf([P, 1], F32, "warm_out")
 
+        nc.gpsimd.memset(warm_in[:], 1.0)
+        nc.scalar.activation(warm_out[:], warm_in[:], ACT.Abs_reciprocal_sqrt)
         nc.gpsimd.memset(tab_sc[:], 0)
         nc.vector.memset(tab_rows[32:64, :], 0)
         nc.vector.memset(tab_rows[64:P, :], 0)
-        nc.gpsimd.memset(warm_in[:], 1.0)
-        nc.scalar.activation(warm_out[:], warm_in[:], ACT.Abs_reciprocal_sqrt)
-        nc.gpsimd.memset(w2_sc_raw[:], 0)
-        nc.gpsimd.memset(w3_sc_raw[:], 0)
-        nc.gpsimd.memset(second_sc_pass1[:], 0)
-        nc.gpsimd.memset(template_sc[:], 0)
 
         def load_table_words(a):
             nc.sync.dma_start(tab_w[a][:].bitcast(I32), tab_words[a].rearrange("p t i -> p (t i)").bitcast(I32))
@@ -77,50 +77,49 @@ def tile_list_template_contact_readout_kernel(
             rows = w1[a * P * PACK : (a + 1) * P * PACK, :].rearrange("(p i) c -> p i c", i=PACK)
             nc.sync.dma_start(w1_raw[a][:], rows)
 
-        def load_weight_scales(scales, raw):
+        def load_weight_scales(queue, scales, raw):
             for r in range(ROWS):
-                nc.sync.dma_start(raw[r:P:32, :, :], scales[:, r:16:ROWS, :].rearrange("a q c -> q a c").bitcast(I32))
+                queue.dma_start(raw[r:P:32, :, :], scales[:, r:16:ROWS, :].rearrange("a q c -> q a c").bitcast(I32))
 
         def gather_scales(u):
             nc.vector.tensor_copy(v_sc[u][:], tab_sc[:].bitcast(U8).indirect(lists[u][:]))
 
         v_words = {}
 
-        def gather_words(tile, place, wanted):
+        def gather_words(name, tag, wanted, offset=None):
             cols = SLICE // 16
+            shape = [P, SLICE * sum(len(slices) for u, a, slices in wanted)]
+            tile = sbuf(shape, U32, name, tag) if offset is None else placed(shape, U32, name, offset)
+            place = 0
             for u, a, slices in wanted:
                 offsets = lists[u][:, slices[0] * cols : (slices[-1] + 1) * cols]
                 nc.vector.tensor_copy(tile[:, place : place + len(slices) * SLICE], tab_w[a][:].indirect(offsets))
                 for s in slices:
                     v_words[u, a, s] = tile[:, place : place + SLICE]
                     place += SLICE
-            return place
 
         def moving_scale(u, a, cols):
             if u == SECOND and a == 1:
                 return second_sc_pass1[:].bitcast(U8)[:, cols]
             if u == TEMPLATE:
-                if cols.start < S // 2:
-                    return template_first[LOWER * a : P, cols]
-                return template_sc[:, a, :].bitcast(U8)[:, cols.start - S // 2 : cols.stop - S // 2]
+                return template_sc[:, a, :].bitcast(U8)[:, cols]
             return v_sc[u][LOWER * a : P, cols]
 
         w1_bf = [sbuf([P, PACK * H], BF16, f"w1_bf{a}") for a in range(PASSES)]
         w1_codes = sbuf([P, PASSES, H], U32, "w1_codes")
         w1_sc = sbuf([P, PASSES, H], U8, "w1_sc")
 
-        def round_w1(a, helped):
-            src = w1_raw[a][:].rearrange("p j (g t i) -> p t g i j", t=PACK, i=8)
-            dst = w1_bf[a][:].rearrange("p (t g i j) -> p t g i j", t=PACK, i=8, j=PACK)
-            for t in range(PACK - helped):
+        def round_w1(a):
+            src = w1_raw[a][:].rearrange("p j (g t c i) -> p t g c j i", t=PACK, c=2, i=4)
+            dst = w1_bf[a][:].rearrange("p (t g c i j) -> p t g c j i", t=PACK, c=2, i=4, j=PACK)
+            for t in range(PACK):
                 nc.scalar.copy(dst[:, t], src[:, t])
-            for t in range(PACK - helped, PACK):
-                nc.gpsimd.tensor_scalar(dst[:, t], src[:, t], 1.0, 0.0, MULT, ADD)
 
-        def quantise_w1(a):
-            nc.vector.quantize_mx(w1_codes[:, a, :].bitcast(FP8X4), w1_sc[:, a, :], w1_bf[a][:])
+        def quantise(codes, scale, values):
+            nc.vector.quantize_mx(codes.bitcast(FP8X4), scale, values)
 
         w2_codes = sbuf([P, PACK, PASSES, 2 * P], U8, "w2_codes")
+        w3_codes = sbuf([P, PACK, PASSES, P], U32, "w3_codes")
         w3_sc = sbuf([P, PACK, PASSES, P], U8, "w3_sc")
         w2_sc = sbuf([P, PACK, PASSES, P], U8, "w2_sc")
 
@@ -138,55 +137,64 @@ def tile_list_template_contact_readout_kernel(
                 return w2_codes[:, t, a, :].bitcast(FP4X4), w2_sc[:, t, a, :]
             return w3_codes[:, t, a, :].bitcast(FP8X4), w3_sc[:, t, a, :]
 
-        def project(slices, order, first_bank):
-            banks = {
-                (s, hf): psum.tile([P, PACK, HALF], F32, name=f"bank{first_bank + HALVES * place + hf}")
-                for place, s in enumerate(slices)
-                for hf in range(HALVES)
-            }
-            steps = [(pair, s) for pair in order[:-2] for s in slices]
-            steps.extend((pair, s) for s in slices for pair in order[-2:])
-            for (u, a), s in steps:
-                for hf in range(HALVES):
-                    local = slice(hf * HALF, (hf + 1) * HALF)
-                    cols = slice(s * SLICE + hf * HALF, s * SLICE + (hf + 1) * HALF)
-                    for t in range(PACK):
-                        codes, scale = weight(u, a, t)
-                        nc.tensor.matmul_mx(
-                            banks[s, hf][:, t, :],
-                            lhsT=codes,
-                            lhsT_scale=scale,
-                            rhs=v_words[u, a, s][:, local].bitcast(FP8X4),
-                            rhs_scale=moving_scale(u, a, cols),
-                            start=((u, a) == order[0] and t == 0),
-                            stop=((u, a) == order[-1] and t == PACK - 1),
-                        )
-            return [[banks[s, hf][:].rearrange("p t n -> p n t") for hf in range(HALVES)] for s in slices]
+        def one_pass(dst, u, a, t, s, local, start, stop):
+            codes, scale = weight(u, a, t)
+            nc.tensor.matmul_mx(
+                dst,
+                lhsT=codes,
+                lhsT_scale=scale,
+                rhs=v_words[u, a, s][:, local].bitcast(FP8X4),
+                rhs_scale=moving_scale(u, a, slice(s * SLICE + local.start, s * SLICE + local.stop)),
+                start=start,
+                stop=stop,
+            )
 
-        def root_of(s, d):
-            square = sbuf([P, HALVES, HALF, PACK], F32, f"square{s}", f"square{s % 2}")
-            root = sbuf([P, HALVES, HALF, PACK], F32, f"root{s}")
-            for hf in range(HALVES):
-                nc.scalar.activation(square[:, hf], d[hf], ACT.Square)
-            for hf in range(HALVES):
-                nc.scalar.activation(root[:, hf], square[:, hf], ACT.Abs_reciprocal_sqrt, bias=1.0)
+        d_banks = [[psum.tile([P, 2, SLICE], F32, name=f"bank{2 * s + m}") for m in range(2)] for s in range(SLICES)]
+        d_order = ((SECOND, 0), (FIRST, 0), (FIRST, 1), (SECOND, 1))
+
+        def d_passes(pair, *slices):
+            for s in slices:
+                for t in range(PACK):
+                    m, e = divmod(t, 2)
+                    first = pair == d_order[0] and e == 0
+                    last = pair == d_order[-1] and e == 1
+                    one_pass(d_banks[s][m][:, e, :], *pair, t, s, slice(0, SLICE), first, last)
+
+        def template(s):
+            banks = [psum.tile([P, PACK, HALF], F32, name=f"bank{2 * s + hf}") for hf in range(HALVES)]
+            for a in range(PASSES):
+                for hf in range(HALVES):
+                    for t in range(PACK):
+                        local = slice(hf * HALF, (hf + 1) * HALF)
+                        first = a == 0 and t == 0
+                        last = a == PASSES - 1 and t == PACK - 1
+                        one_pass(banks[hf][:, t, :], TEMPLATE, a, t, s, local, first, last)
+            return banks
+
+        def root_of(s):
+            square = sbuf([P, 2, SLICE, 2], F32, f"square{s}", f"square{s % 2}")
+            root = placed([P, 2, SLICE, 2], F32, f"root{s}", 4096 * s)
+            for m in range(2):
+                nc.scalar.activation(square[:, m], d_banks[s][m][:].rearrange("p e n -> p n e"), ACT.Square)
+            for m in range(2):
+                nc.scalar.activation(root[:, m], square[:, m], ACT.Abs_reciprocal_sqrt, bias=1.0)
             return root
 
-        def damping_on_scalar(s, root, tag=None):
-            damp = sbuf([P, HALVES, HALF, PACK], F32, f"damp{s}", tag)
-            for hf in range(HALVES):
-                nc.scalar.activation(damp[:, hf], root[:, hf], ACT.Square)
-            return damp
+        def by_entry(damp, first, count):
+            return damp[:, :, first : first + count, :].rearrange("p m n e -> p n m e")
 
-        def product_on_vector(h, template, damp):
-            nc.vector.tensor_tensor(h, template, damp, MULT)
-
-        def quantise(codes, scale, values):
-            nc.vector.quantize_mx(codes.bitcast(FP8X4), scale, values)
+        def product(h, banks, damp, hf):
+            nc.vector.tensor_tensor(
+                h[:, hf].rearrange("p n (m e) -> p n m e", e=2),
+                banks[hf][:].rearrange("p (m e) n -> p n m e", e=2),
+                by_entry(damp, hf * HALF, HALF),
+                MULT,
+            )
 
         out_view = out.rearrange("(c p) j -> p c j", p=P)
+        h_codes = sbuf([P, S], U32, "h_codes")
 
-        def readout(first, width, codes, scale, banks, vector_tiles, by_tile):
+        def readout(first, width, scale, banks, vector_tiles, by_tile):
             result = sbuf([P, N_TILES, width], F32, f"result{first}")
             for bank in sorted(set(banks), key=banks.index):
                 group = [c for c in range(N_TILES) if banks[c] == bank]
@@ -196,7 +204,7 @@ def tile_list_template_contact_readout_kernel(
                         y[:, slot, :],
                         lhsT=wo_codes[:, c * P : (c + 1) * P].bitcast(FP8X4),
                         lhsT_scale=wo_sc[:, c * P : (c + 1) * P],
-                        rhs=codes.bitcast(FP8X4),
+                        rhs=h_codes[:, first : first + width].bitcast(FP8X4),
                         rhs_scale=scale,
                         start=True,
                         stop=True,
@@ -211,8 +219,12 @@ def tile_list_template_contact_readout_kernel(
             if not by_tile:
                 nc.sync.dma_start(out_view[:, :, first : first + width], result[:])
 
+        nc.gpsimd.memset(w2_sc_raw[:], 0)
+        nc.gpsimd.memset(second_sc_pass1[:], 0)
+        nc.gpsimd.memset(w3_sc_raw[:], 0)
+        nc.gpsimd.memset(template_sc[:], 0)
         nc.sync.dma_start(lists[TEMPLATE][:], offs3)
-        nc.sync.dma_start(tab_rows[0:32, :], tab_scales.rearrange("a q t -> q a t").bitcast(I32))
+        nc.sync.dma_start(tab_rows[0:32, :], tab_scales.rearrange("a q t -> (a q) t").bitcast(I32))
         for q in range(QUADRANTS):
             nc.sync.dma_start(tab_sc[32 * q : 32 * q + 2 * LOWER, :], tab_scales[:, 4 * q : 4 * q + 4, :].bitcast(I32))
         nc.sync.dma_start(lists[SECOND][:], offs2)
@@ -220,101 +232,103 @@ def tile_list_template_contact_readout_kernel(
         nc.sync.dma_start(lists[FIRST][:], offs)
         nc.sync.dma_start(w2_raw[:], w2_words.rearrange("a p c -> p a c").bitcast(I32))
         load_w1(0)
-        load_weight_scales(w2_scales, w2_sc_raw)
+        load_weight_scales(nc.sync, w2_scales, w2_sc_raw)
         load_w1(1)
-        nc.vector.tensor_copy(template_rows[:], tab_rows[:].bitcast(U8).indirect(lists[TEMPLATE][:, S // 32 :]))
         reorder(nc.scalar.copy, w2_codes, w2_raw, 4)
+        reorder(nc.gpsimd.tensor_copy, w2_sc, w2_sc_raw, 2)
+        round_w1(0)
+        round_w1(1)
+
+        nc.vector.tensor_copy(template_rows[:], tab_rows[:].bitcast(U8).indirect(lists[TEMPLATE][:]))
         gather_scales(SECOND)
+        gather_words("early", None, [(SECOND, 0, (0, 1, 2, 3))])
         for r in range(ROWS):
             nc.sync.dma_start(second_sc_pass1[r:P:32, :], v_sc[SECOND][LOWER + r : P : 32, :].bitcast(I32))
         load_table_words(1)
         nc.sync.dma_start(w3_raw[:], w3_words.rearrange("a p c i -> p a (c i)").bitcast(I32))
-        load_weight_scales(w3_scales, w3_sc_raw)
         wo_rows = wo.rearrange("(g t i) n -> t g i n", t=PACK, i=8)
         for t in range(PACK):
             nc.sync.dma_start(wo_raw[:, t, :], wo_rows[t])
-        for q in range(QUADRANTS):
-            nc.sync.dma_start(
-                template_sc[32 * q : 32 * q + ROWS, :, :], template_rows[8 * q : 8 * q + 8, :].bitcast(I32)
-            )
+        load_weight_scales(nc.sync, w3_scales, w3_sc_raw)
+        for a in range(PASSES):
+            for r in range(ROWS):
+                nc.sync.dma_start(template_sc[r:P:32, a, :], template_rows[16 * a + r : 16 * a + 16 : 4, :].bitcast(I32))
         with nc.allow_non_contiguous_dma(reason="one bias value for each partition and output tile"):
             nc.sync.dma_start(bias[:], b.rearrange("(c p) -> p c", p=P))
-
-        reorder(nc.gpsimd.tensor_copy, w2_sc, w2_sc_raw, 2)
-        round_w1(0, 1)
-        round_w1(1, 1)
-
-        early = ((SECOND, 0), (FIRST, 0))
-        late = ((SECOND, 1), (FIRST, 1))
-        both = ((TEMPLATE, 0), (TEMPLATE, 1))
-
-        def of_slice(pairs, *slices):
-            return [(u, a, slices) for u, a in pairs]
-
-        room = sbuf([P, 6 * SLICE], U32, "picked_head")
-        place = gather_words(room, 0, of_slice(early[:1], 0, 1, 2))
+        d_passes((SECOND, 0), 0, 1, 2, 3)
         gather_scales(FIRST)
-        gather_words(room, place, of_slice(early[1:], 0, 1, 2))
-        quantise_w1(0)
-        quantise_w1(1)
-        w3_codes = sbuf([P, PACK, PASSES, P], U32, "w3_codes", "w1_bf1")
-        reorder(nc.gpsimd.tensor_copy, w3_codes, w3_raw, 8)
-        reorder(nc.gpsimd.tensor_copy, w3_sc, w3_sc_raw, 2)
+        quantise(w1_codes[:, 0, :], w1_sc[:, 0, :], w1_bf[0][:])
+        gather_words("early_first", "w1_raw0", [(FIRST, 0, (0, 1)), (FIRST, 0, (2, 3))])
+        quantise(w1_codes[:, 1, :], w1_sc[:, 1, :], w1_bf[1][:])
+        d_passes((FIRST, 0), 0, 1, 2, 3)
+        reorder(nc.scalar.copy, w3_codes, w3_raw, 8)
         wo_bf = sbuf([P, N, PACK], BF16, "wo_bf")
         nc.gpsimd.tensor_scalar(wo_bf[:], wo_raw[:].rearrange("p t n -> p n t"), 1.0, 0.0, MULT, ADD)
-        gather_words(sbuf([P, SLICE], U32, "picked_start", "w1_raw0"), 0, of_slice(late[:1], 0))
-        gather_words(sbuf([P, 3 * SLICE], U32, "picked_first", "w1_raw1"), 0, of_slice(late[1:], 0) + of_slice(late, 1))
-        d0, d1 = project((0, 1), early + late, 0)
-        template_first = sbuf([P, S // 2], U8, "template_first", "w1_raw0")
-        nc.vector.tensor_copy(template_first[:], tab_sc[:].bitcast(U8).indirect(lists[TEMPLATE][:, 0 : S // 32]))
-        room = sbuf([P, 12 * SLICE], U32, "picked_second", "w3_sc_raw")
-        gather_words(
-            room, 0, of_slice(both, 0, 1) + of_slice(late, 2) + of_slice(early + late, 3) + of_slice(both[:1], 2, 3)
-        )
-        root0 = root_of(0, d0)
-        root1 = root_of(1, d1)
-        damp01 = sbuf([P, 2, HALVES, HALF, PACK], F32, "damp01", "wo_raw")
-        nc.gpsimd.tensor_tensor(damp01[:, 0], root0[:], root0[:], MULT)
-        nc.gpsimd.tensor_tensor(damp01[:, 1], root1[:], root1[:], MULT)
-        t0 = project((0,), both, 4)[0]
-        t0_sb = sbuf([P, HALVES, HALF, PACK], F32, "t0_sb")
-        for hf in range(HALVES):
-            nc.scalar.copy(t0_sb[:, hf], t0[hf])
-        h01 = sbuf([P, 2, HALVES, HALF, PACK], BF16, "h01")
-        nc.gpsimd.tensor_tensor(h01[:, 0], t0_sb[:], damp01[:, 0], MULT)
+        reorder(nc.gpsimd.tensor_copy, w3_sc, w3_sc_raw, 2)
 
-        damp2 = damping_on_scalar(2, root_of(2, project((2,), early + late, 0)[0]))
-        t1 = project((1,), both, 6)[0]
-        damp3 = damping_on_scalar(3, root_of(3, project((3,), early + late, 2)[0]))
-        for hf in range(HALVES):
-            product_on_vector(h01[:, 1, hf], t1[hf], damp01[:, 1, hf])
-        gather_words(sbuf([P, SLICE], U32, "picked_third", "root1"), 0, of_slice(both[1:], 2))
-        t2 = project((2,), both, 4)[0]
+        late = d_order[2:]
+        wanted = [(*pair, (s,)) for s in (0, 1) for pair in late] + [(*pair, (2, 3)) for pair in late]
+        gather_words("late", "w1_raw1", wanted)
+        for s in (0, 1):
+            for pair in late:
+                d_passes(pair, s)
+        for pair in late:
+            d_passes(pair, 2, 3)
+        gather_words("template01", "w3_raw", [(TEMPLATE, 0, (0, 1)), (TEMPLATE, 1, (0,)), (TEMPLATE, 1, (1,))])
 
-        planes = sbuf([P, N + 2 * SLICE], U8, "planes", "wo_raw")
-        wo_sc = planes[:, 0:N]
+        roots = [root_of(s) for s in range(SLICES)]
+        damp0 = sbuf([P, 2, SLICE, 2], F32, "damp0")
+        nc.gpsimd.tensor_tensor(damp0[:], roots[0][:], roots[0][:], MULT)
+        wo_sc = placed([P, N], U8, "wo_sc", 0)
         wo_codes = sbuf([P, N], U32, "wo_codes")
         for cols in (slice(0, 2 * P), slice(2 * P, N)):
             quantise(wo_codes[:, cols], wo_sc[:, cols], wo_bf[:, cols, :].rearrange("p n t -> p (n t)"))
-        h_codes = sbuf([P, S], U32, "h_codes")
-        quantise(h_codes[:, 0 : 2 * SLICE], planes[:, N : N + 2 * SLICE], h01[:].rearrange("p s f n t -> p (s f n t)"))
-        readout(0, 2 * SLICE, h_codes[:, 0 : 2 * SLICE], planes[:, N : N + 2 * SLICE], (0, 1, 2), (), True)
+        damp1 = sbuf([P, 2, SLICE, 2], F32, "damp1", "wo_bf")
+        nc.gpsimd.tensor_tensor(damp1[:], roots[1][:], roots[1][:], MULT)
+        damp = [damp0[:], damp1[:]]
 
-        h2 = sbuf([P, HALVES, HALF, PACK], BF16, "h2", "t0_sb")
-        h3 = sbuf([P, HALVES, HALF, PACK], BF16, "h3")
-        h_sc = sbuf([P, 2 * SLICE], U8, "h_sc")
-        product_on_vector(h2[:, 0], t2[0], damp2[:, 0])
-        gather_words(sbuf([P, SLICE], U32, "picked_last", "h01"), 0, of_slice(both[1:], 3))
-        t3 = project((3,), both, 6)[0]
-        product_on_vector(h2[:, 1], t2[1], damp2[:, 1])
-        cols = slice(2 * SLICE, 3 * SLICE)
-        quantise(h_codes[:, cols], h_sc[:, 0:SLICE], h2[:].rearrange("p f n t -> p (f n t)"))
-        readout(2 * SLICE, SLICE, h_codes[:, cols], h_sc[:, 0:SLICE], (3, 3, 4), (), True)
-        for hf in range(HALVES):
-            product_on_vector(h3[:, hf], t3[hf], damp3[:, hf])
-        last = [slice(3 * SLICE + hf * HALF, 3 * SLICE + (hf + 1) * HALF) for hf in range(HALVES)]
-        scales = [h_sc[:, SLICE + hf * HALF : SLICE + (hf + 1) * HALF] for hf in range(HALVES)]
-        for hf in range(HALVES):
-            quantise(h_codes[:, last[hf]], scales[hf], h3[:, hf].rearrange("p n t -> p (n t)"))
-        for hf, banks in enumerate(((5, 5, 0), (1, 1, 2))):
-            readout(last[hf].start, HALF, h_codes[:, last[hf]], scales[hf], banks, (2,), False)
+        def damp_on_scalar(s):
+            tile = sbuf([P, 2, SLICE, 2], F32, f"damp{s}")
+            for m in range(2):
+                nc.scalar.activation(tile[:, m], roots[s][:, m], ACT.Square)
+            damp.append(tile[:])
+
+        h = [sbuf([P, HALVES, HALF, PACK], BF16, f"h{s}") for s in range(SLICES)]
+        h_sc = sbuf([P, S], U8, "h_sc")
+
+        def products(s, banks, *halves):
+            for hf in halves:
+                product(h[s], banks, damp[s], hf)
+
+        def finish(s):
+            cols = slice(s * SLICE, (s + 1) * SLICE)
+            quantise(h_codes[:, cols], h_sc[:, cols], h[s][:].rearrange("p f n t -> p (f n t)"))
+            readout(s * SLICE, SLICE, h_sc[:, cols], (2 * s, 2 * s, 2 * s + 1), (), True)
+
+        t0 = template(0)
+        t1 = template(1)
+        damp_on_scalar(2)
+        products(0, t0, 0, 1)
+        gather_words("template23", None, [(TEMPLATE, 0, (2, 3))], 1024)
+        finish(0)
+        damp_on_scalar(3)
+        products(1, t1, 0, 1)
+        gather_words("template2", None, [(TEMPLATE, 1, (2,))], 4096)
+        t2 = template(2)
+        finish(1)
+        gather_words("template3", "wo_bf", [(TEMPLATE, 1, (3,))])
+        t3 = template(3)
+
+        def finish_half(s, hf, banks, vector_tiles):
+            first = s * SLICE + hf * HALF
+            cols = slice(first, first + HALF)
+            quantise(h_codes[:, cols], h_sc[:, cols], h[s][:, hf].rearrange("p n t -> p (n t)"))
+            readout(first, HALF, h_sc[:, cols], banks, vector_tiles, False)
+
+        products(2, t2, 0, 1)
+        finish_half(2, 0, (4, 4, 4), ())
+        products(3, t3, 0)
+        finish_half(2, 1, (5, 5, 5), ())
+        products(3, t3, 1)
+        finish_half(3, 0, (6, 6, 6), ())
+        finish_half(3, 1, (7, 7, 0), (2,))

@@ -28,6 +28,7 @@ N_TILES = N // P
 QUADRANTS = 4
 ROWS = 4
 LOWER = 4
+FIRST_ROOM, SECOND_ROOM, THIRD_ROOM = 0, 4096, 8192
 FIRST, SECOND, TEMPLATE = 0, 1, 2
 
 
@@ -50,11 +51,11 @@ def tile_list_template_contact_readout_kernel(
         tab_w = [sbuf([P, T], U32, f"tab_w{a}") for a in range(PASSES)]
         tab_sc = sbuf([P, T // 4], I32, "tab_sc")
         tab_rows = sbuf([P, T // 4], I32, "tab_rows")
-        template_rows = sbuf([P, S], U8, "template_rows")
-        template_sc = sbuf([P, PASSES, S // 4], I32, "template_sc")
+        template_rows = sbuf([P, S // 2], U8, "template_rows")
+        template_sc = sbuf([P, PASSES, S // 8], I32, "template_sc")
         w1_raw = [sbuf([P, PACK, H], F32, f"w1_raw{a}") for a in range(PASSES)]
         w2_raw = sbuf([P, PASSES, H // 2], I32, "w2_raw")
-        w3_raw = sbuf([P, PASSES, H], I32, "w3_raw")
+        w3_raw = placed([P, PASSES, H], I32, "w3_raw", THIRD_ROOM)
         w2_sc_raw = sbuf([P, PASSES, H // 4], I32, "w2_sc_raw")
         w3_sc_raw = sbuf([P, PASSES, H // 4], I32, "w3_sc_raw")
         wo_raw = sbuf([P, PACK, N], F32, "wo_raw")
@@ -64,11 +65,11 @@ def tile_list_template_contact_readout_kernel(
         warm_in = sbuf([P, 1], F32, "warm_in")
         warm_out = sbuf([P, 1], F32, "warm_out")
 
-        nc.gpsimd.memset(warm_in[:], 1.0)
-        nc.scalar.activation(warm_out[:], warm_in[:], ACT.Abs_reciprocal_sqrt)
         nc.gpsimd.memset(tab_sc[:], 0)
         nc.vector.memset(tab_rows[32:64, :], 0)
         nc.vector.memset(tab_rows[64:P, :], 0)
+        nc.gpsimd.memset(warm_in[:], 1.0)
+        nc.scalar.activation(warm_out[:], warm_in[:], ACT.Abs_reciprocal_sqrt)
 
         def load_table_words(a):
             nc.sync.dma_start(tab_w[a][:].bitcast(I32), tab_words[a].rearrange("p t i -> p (t i)").bitcast(I32))
@@ -102,7 +103,9 @@ def tile_list_template_contact_readout_kernel(
             if u == SECOND and a == 1:
                 return second_sc_pass1[:].bitcast(U8)[:, cols]
             if u == TEMPLATE:
-                return template_sc[:, a, :].bitcast(U8)[:, cols]
+                if cols.start < S // 2:
+                    return template_first[LOWER * a : P, cols]
+                return template_sc[:, a, :].bitcast(U8)[:, cols.start - S // 2 : cols.stop - S // 2]
             return v_sc[u][LOWER * a : P, cols]
 
         w1_bf = [sbuf([P, PACK * H], BF16, f"w1_bf{a}") for a in range(PASSES)]
@@ -112,8 +115,11 @@ def tile_list_template_contact_readout_kernel(
         def round_w1(a):
             src = w1_raw[a][:].rearrange("p j (g t c i) -> p t g c j i", t=PACK, c=2, i=4)
             dst = w1_bf[a][:].rearrange("p (t g c i j) -> p t g c j i", t=PACK, c=2, i=4, j=PACK)
-            for t in range(PACK):
+            for t in range(PACK - 1):
                 nc.scalar.copy(dst[:, t], src[:, t])
+            src = w1_raw[a][:].rearrange("p j (g t i) -> p t g i j", t=PACK, i=8)
+            dst = w1_bf[a][:].rearrange("p (t g i j) -> p t g i j", t=PACK, i=8, j=PACK)
+            nc.gpsimd.tensor_scalar(dst[:, PACK - 1], src[:, PACK - 1], 1.0, 0.0, MULT, ADD)
 
         def quantise(codes, scale, values):
             nc.vector.quantize_mx(codes.bitcast(FP8X4), scale, values)
@@ -149,19 +155,22 @@ def tile_list_template_contact_readout_kernel(
                 stop=stop,
             )
 
-        d_banks = [[psum.tile([P, 2, SLICE], F32, name=f"bank{2 * s + m}") for m in range(2)] for s in range(SLICES)]
-        d_order = ((SECOND, 0), (FIRST, 0), (FIRST, 1), (SECOND, 1))
+        d_banks = {}
+        d_order = ((SECOND, 0), (FIRST, 0), (SECOND, 1), (FIRST, 1))
 
-        def d_passes(pair, *slices):
+        def open_d(s, bank):
+            d_banks[s] = [psum.tile([P, 2, SLICE], F32, name=f"bank{bank + m}") for m in range(2)]
+
+        def d_passes(pair, *slices, order=(d_order[0], d_order[-1])):
             for s in slices:
                 for t in range(PACK):
                     m, e = divmod(t, 2)
-                    first = pair == d_order[0] and e == 0
-                    last = pair == d_order[-1] and e == 1
+                    first = pair == order[0] and e == 0
+                    last = pair == order[1] and e == 1
                     one_pass(d_banks[s][m][:, e, :], *pair, t, s, slice(0, SLICE), first, last)
 
-        def template(s):
-            banks = [psum.tile([P, PACK, HALF], F32, name=f"bank{2 * s + hf}") for hf in range(HALVES)]
+        def template(s, bank):
+            banks = [psum.tile([P, PACK, HALF], F32, name=f"bank{bank + hf}") for hf in range(HALVES)]
             for a in range(PASSES):
                 for hf in range(HALVES):
                     for t in range(PACK):
@@ -173,7 +182,7 @@ def tile_list_template_contact_readout_kernel(
 
         def root_of(s):
             square = sbuf([P, 2, SLICE, 2], F32, f"square{s}", f"square{s % 2}")
-            root = placed([P, 2, SLICE, 2], F32, f"root{s}", 4096 * s)
+            root = sbuf([P, 2, SLICE, 2], F32, f"root{s}")
             for m in range(2):
                 nc.scalar.activation(square[:, m], d_banks[s][m][:].rearrange("p e n -> p n e"), ACT.Square)
             for m in range(2):
@@ -224,7 +233,7 @@ def tile_list_template_contact_readout_kernel(
         nc.gpsimd.memset(w3_sc_raw[:], 0)
         nc.gpsimd.memset(template_sc[:], 0)
         nc.sync.dma_start(lists[TEMPLATE][:], offs3)
-        nc.sync.dma_start(tab_rows[0:32, :], tab_scales.rearrange("a q t -> (a q) t").bitcast(I32))
+        nc.sync.dma_start(tab_rows[0:32, :], tab_scales.rearrange("a q t -> q a t").bitcast(I32))
         for q in range(QUADRANTS):
             nc.sync.dma_start(tab_sc[32 * q : 32 * q + 2 * LOWER, :], tab_scales[:, 4 * q : 4 * q + 4, :].bitcast(I32))
         nc.sync.dma_start(lists[SECOND][:], offs2)
@@ -239,96 +248,123 @@ def tile_list_template_contact_readout_kernel(
         round_w1(0)
         round_w1(1)
 
-        nc.vector.tensor_copy(template_rows[:], tab_rows[:].bitcast(U8).indirect(lists[TEMPLATE][:]))
+        nc.vector.tensor_copy(template_rows[:], tab_rows[:].bitcast(U8).indirect(lists[TEMPLATE][:, S // 32 :]))
         gather_scales(SECOND)
-        gather_words("early", None, [(SECOND, 0, (0, 1, 2, 3))])
         for r in range(ROWS):
             nc.sync.dma_start(second_sc_pass1[r:P:32, :], v_sc[SECOND][LOWER + r : P : 32, :].bitcast(I32))
         load_table_words(1)
         nc.sync.dma_start(w3_raw[:], w3_words.rearrange("a p c i -> p a (c i)").bitcast(I32))
+        load_weight_scales(nc.sync, w3_scales, w3_sc_raw)
         wo_rows = wo.rearrange("(g t i) n -> t g i n", t=PACK, i=8)
         for t in range(PACK):
             nc.sync.dma_start(wo_raw[:, t, :], wo_rows[t])
-        load_weight_scales(nc.sync, w3_scales, w3_sc_raw)
-        for a in range(PASSES):
-            for r in range(ROWS):
-                nc.sync.dma_start(template_sc[r:P:32, a, :], template_rows[16 * a + r : 16 * a + 16 : 4, :].bitcast(I32))
+        for q in range(QUADRANTS):
+            nc.sync.dma_start(
+                template_sc[32 * q : 32 * q + ROWS, :, :], template_rows[8 * q : 8 * q + 8, :].bitcast(I32)
+            )
         with nc.allow_non_contiguous_dma(reason="one bias value for each partition and output tile"):
             nc.sync.dma_start(bias[:], b.rearrange("(c p) -> p c", p=P))
-        d_passes((SECOND, 0), 0, 1, 2, 3)
-        gather_scales(FIRST)
-        quantise(w1_codes[:, 0, :], w1_sc[:, 0, :], w1_bf[0][:])
-        gather_words("early_first", "w1_raw0", [(FIRST, 0, (0, 1)), (FIRST, 0, (2, 3))])
-        quantise(w1_codes[:, 1, :], w1_sc[:, 1, :], w1_bf[1][:])
-        d_passes((FIRST, 0), 0, 1, 2, 3)
-        reorder(nc.scalar.copy, w3_codes, w3_raw, 8)
-        wo_bf = sbuf([P, N, PACK], BF16, "wo_bf")
-        nc.gpsimd.tensor_scalar(wo_bf[:], wo_raw[:].rearrange("p t n -> p n t"), 1.0, 0.0, MULT, ADD)
-        reorder(nc.gpsimd.tensor_copy, w3_sc, w3_sc_raw, 2)
 
-        late = d_order[2:]
-        wanted = [(*pair, (s,)) for s in (0, 1) for pair in late] + [(*pair, (2, 3)) for pair in late]
-        gather_words("late", "w1_raw1", wanted)
+        wo_codes = sbuf([P, N], U32, "wo_codes")
+        roots = {}
+        damp = {}
+
+        def damp_on_scalar(s):
+            damp[s] = sbuf([P, 2, SLICE, 2], F32, f"damp{s}")
+            for m in range(2):
+                nc.scalar.activation(damp[s][:, m], roots[s][:, m], ACT.Square)
+
+        def damp_on_gpsimd(s, tag=None):
+            damp[s] = sbuf([P, 2, SLICE, 2], F32, f"damp{s}", tag)
+            nc.gpsimd.tensor_tensor(damp[s][:], roots[s][:], roots[s][:], MULT)
+
+        def copy_out(name, banks, halves, offset):
+            tile = placed([P, len(halves), HALF, PACK], F32, name, offset)
+            for place, hf in enumerate(halves):
+                nc.scalar.copy(tile[:, place], banks[hf][:].rearrange("p t n -> p n t"))
+            return tile
+
+        def product_on_gpsimd(dst, copied, s, first, count):
+            entries = "p f n (m e) -> p (f n) m e"
+            nc.gpsimd.tensor_tensor(
+                dst.rearrange(entries, e=2), copied[:].rearrange(entries, e=2), by_entry(damp[s], first, count), MULT
+            )
+
+        def finish(values, first, width, scale, banks, vector_tiles=(), by_tile=True):
+            quantise(h_codes[:, first : first + width], scale, values)
+            readout(first, width, scale, banks, vector_tiles, by_tile)
+
+        flat = "p f n t -> p (f n t)"
+        gather_words("second0", None, [(SECOND, 0, (0, 1, 2, 3))])
+        gather_scales(FIRST)
+        gather_words("first0", None, [(FIRST, 0, (0, 1))])
+        for a in range(PASSES):
+            quantise(w1_codes[:, a, :], w1_sc[:, a, :], w1_bf[a][:])
+        reorder(nc.scalar.copy, w3_codes, w3_raw, 8)
+        reorder(nc.gpsimd.tensor_copy, w3_sc, w3_sc_raw, 2)
+        wo_bf = sbuf([P, N, PACK], BF16, "wo_bf", "w1_bf1")
+        nc.gpsimd.tensor_scalar(wo_bf[:], wo_raw[:].rearrange("p t n -> p n t"), 1.0, 0.0, MULT, ADD)
+        early, late = d_order[:2], d_order[2:]
+        for s in range(3):
+            open_d(s, 2 * s)
+        d_passes(early[0], 0, 1, 2)
+        d_passes(early[1], 0, 1)
+        gather_words("late_start", "w1_raw0", [(*late[0], (0,))])
+        gather_words("late", "w1_raw1", [(*late[1], (0,))] + [(*pair, (s,)) for s in (1, 2) for pair in late])
+        gather_words("first0_rest", None, [(*early[1], (2, 3))], THIRD_ROOM)
         for s in (0, 1):
             for pair in late:
                 d_passes(pair, s)
+        for pair in late + early[1:]:
+            d_passes(pair, 2, order=(early[0], early[1]))
+        template_first = placed([P, S // 2], U8, "template_first", THIRD_ROOM + 2048)
+        nc.vector.tensor_copy(template_first[:], tab_sc[:].bitcast(U8).indirect(lists[TEMPLATE][:, 0 : S // 32]))
+        wanted = [(TEMPLATE, 0, (0,)), (TEMPLATE, 1, (0,))] + [(*pair, (3,)) for pair in late]
+        wanted += [(TEMPLATE, 0, (1, 2, 3)), (TEMPLATE, 1, (1,)), (TEMPLATE, 1, (2, 3))]
+        gather_words("middle", None, wanted, THIRD_ROOM + 2560)
+        for s in range(3):
+            roots[s] = root_of(s)
+        open_d(3, 0)
+        for pair in early:
+            d_passes(pair, 3)
+        damp01 = sbuf([P, 2, 2, SLICE, 2], F32, "damp01", "wo_raw")
+        for s in range(2):
+            damp[s] = damp01[:, s]
+            nc.gpsimd.tensor_tensor(damp[s], roots[s][:], roots[s][:], MULT)
+        t0 = template(0, 6)
+        t0_sb = copy_out("t0_sb", t0, (0, 1), FIRST_ROOM)
+        h0 = sbuf([P, HALVES, HALF, PACK], BF16, "h0")
+        product_on_gpsimd(h0[:], t0_sb, 0, 0, SLICE)
+        damp_on_scalar(2)
         for pair in late:
-            d_passes(pair, 2, 3)
-        gather_words("template01", "w3_raw", [(TEMPLATE, 0, (0, 1)), (TEMPLATE, 1, (0,)), (TEMPLATE, 1, (1,))])
+            d_passes(pair, 3)
+        t1 = template(1, 2)
+        roots[3] = root_of(3)
+        t1_sb = copy_out("t1_sb", t1, (0,), SECOND_ROOM)
+        damp_on_scalar(3)
+        t2 = template(2, 4)
 
-        roots = [root_of(s) for s in range(SLICES)]
-        damp0 = sbuf([P, 2, SLICE, 2], F32, "damp0")
-        nc.gpsimd.tensor_tensor(damp0[:], roots[0][:], roots[0][:], MULT)
-        wo_sc = placed([P, N], U8, "wo_sc", 0)
-        wo_codes = sbuf([P, N], U32, "wo_codes")
+        planes = placed([P, N + 2 * SLICE], U8, "planes", FIRST_ROOM)
+        wo_sc = planes[:, 0:N]
         for cols in (slice(0, 2 * P), slice(2 * P, N)):
             quantise(wo_codes[:, cols], wo_sc[:, cols], wo_bf[:, cols, :].rearrange("p n t -> p (n t)"))
-        damp1 = sbuf([P, 2, SLICE, 2], F32, "damp1", "wo_bf")
-        nc.gpsimd.tensor_tensor(damp1[:], roots[1][:], roots[1][:], MULT)
-        damp = [damp0[:], damp1[:]]
-
-        def damp_on_scalar(s):
-            tile = sbuf([P, 2, SLICE, 2], F32, f"damp{s}")
-            for m in range(2):
-                nc.scalar.activation(tile[:, m], roots[s][:, m], ACT.Square)
-            damp.append(tile[:])
-
-        h = [sbuf([P, HALVES, HALF, PACK], BF16, f"h{s}") for s in range(SLICES)]
-        h_sc = sbuf([P, S], U8, "h_sc")
-
-        def products(s, banks, *halves):
-            for hf in halves:
-                product(h[s], banks, damp[s], hf)
-
-        def finish(s):
-            cols = slice(s * SLICE, (s + 1) * SLICE)
-            quantise(h_codes[:, cols], h_sc[:, cols], h[s][:].rearrange("p f n t -> p (f n t)"))
-            readout(s * SLICE, SLICE, h_sc[:, cols], (2 * s, 2 * s, 2 * s + 1), (), True)
-
-        t0 = template(0)
-        t1 = template(1)
-        damp_on_scalar(2)
-        products(0, t0, 0, 1)
-        gather_words("template23", None, [(TEMPLATE, 0, (2, 3))], 1024)
-        finish(0)
-        damp_on_scalar(3)
-        products(1, t1, 0, 1)
-        gather_words("template2", None, [(TEMPLATE, 1, (2,))], 4096)
-        t2 = template(2)
-        finish(1)
-        gather_words("template3", "wo_bf", [(TEMPLATE, 1, (3,))])
-        t3 = template(3)
-
-        def finish_half(s, hf, banks, vector_tiles):
-            first = s * SLICE + hf * HALF
-            cols = slice(first, first + HALF)
-            quantise(h_codes[:, cols], h_sc[:, cols], h[s][:, hf].rearrange("p n t -> p (n t)"))
-            readout(first, HALF, h_sc[:, cols], banks, vector_tiles, False)
-
-        products(2, t2, 0, 1)
-        finish_half(2, 0, (4, 4, 4), ())
-        products(3, t3, 0)
-        finish_half(2, 1, (5, 5, 5), ())
-        products(3, t3, 1)
-        finish_half(3, 0, (6, 6, 6), ())
-        finish_half(3, 1, (7, 7, 0), (2,))
+        finish(h0[:].rearrange(flat), 0, SLICE, planes[:, N : N + SLICE], (6, 6, 7))
+        h1 = sbuf([P, HALVES, HALF, PACK], BF16, "h1", "h0")
+        product_on_gpsimd(h1[:, 0:1], t1_sb, 1, 0, HALF)
+        h2 = placed([P, HALVES, HALF, PACK], BF16, "h2", FIRST_ROOM + 2048)
+        product(h2, t2, damp[2], 0)
+        product(h1, t1, damp[1], 1)
+        t3 = template(3, 2)
+        product(h2, t2, damp[2], 1)
+        finish(h1[:].rearrange(flat), SLICE, SLICE, planes[:, N + SLICE :], (0, 0, 1))
+        h3 = placed([P, HALVES, HALF, PACK], BF16, "h3_late", SECOND_ROOM + 1024)
+        late_sc = placed([P, 2 * SLICE], U8, "late_sc", SECOND_ROOM)
+        product(h3, t3, damp[3], 0)
+        finish(h2[:].rearrange(flat), 2 * SLICE, SLICE, late_sc[:, 0:SLICE], (6, 6, 7))
+        product(h3, t3, damp[3], 1)
+        scales = [late_sc[:, SLICE + hf * HALF : SLICE + (hf + 1) * HALF] for hf in range(HALVES)]
+        for hf in range(HALVES):
+            first = 3 * SLICE + hf * HALF
+            quantise(h_codes[:, first : first + HALF], scales[hf], h3[:, hf].rearrange("p n t -> p (n t)"))
+        for hf, banks in enumerate(((4, 4, 5), (0, 0, 1))):
+            readout(3 * SLICE + hf * HALF, HALF, scales[hf], banks, (2,), False)

@@ -310,7 +310,7 @@ def tile_list_template_contact_readout_kernel(
         d_passes(early[0], 0, 1, 2)
         d_passes(early[1], 0, 1)
         gather_words("late_start", "w1_raw0", [(*late[0], (0,))])
-        gather_words("late", "w1_raw1", [(*late[1], (0,))] + [(*pair, (s,)) for s in (1, 2) for pair in late])
+        gather_words("late", "w1_raw1", [(*late[1], (0,))] + [(*pair, (1, 2)) for pair in late])
         gather_words("first0_rest", None, [(*early[1], (2, 3))], THIRD_ROOM)
         for s in (0, 1):
             for pair in late:
@@ -333,38 +333,35 @@ def tile_list_template_contact_readout_kernel(
             nc.gpsimd.tensor_tensor(damp[s], roots[s][:], roots[s][:], MULT)
         t0 = template(0, 6)
         t0_sb = copy_out("t0_sb", t0, (0, 1), FIRST_ROOM)
-        h0 = sbuf([P, HALVES, HALF, PACK], BF16, "h0")
-        product_on_gpsimd(h0[:], t0_sb, 0, 0, SLICE)
+        h01 = sbuf([P, 2, HALVES, HALF, PACK], BF16, "h01")
+        product_on_gpsimd(h01[:, 0], t0_sb, 0, 0, SLICE)
         damp_on_scalar(2)
         for pair in late:
             d_passes(pair, 3)
         t1 = template(1, 2)
         roots[3] = root_of(3)
-        t1_sb = copy_out("t1_sb", t1, (0,), SECOND_ROOM)
         damp_on_scalar(3)
         t2 = template(2, 4)
 
+        for hf in range(HALVES):
+            product(h01[:, 1], t1, damp[1], hf)
+        t3 = template(3, 2)
         planes = placed([P, N + 2 * SLICE], U8, "planes", FIRST_ROOM)
         wo_sc = planes[:, 0:N]
         for cols in (slice(0, 2 * P), slice(2 * P, N)):
             quantise(wo_codes[:, cols], wo_sc[:, cols], wo_bf[:, cols, :].rearrange("p n t -> p (n t)"))
-        finish(h0[:].rearrange(flat), 0, SLICE, planes[:, N : N + SLICE], (6, 6, 7))
-        h1 = sbuf([P, HALVES, HALF, PACK], BF16, "h1", "h0")
-        product_on_gpsimd(h1[:, 0:1], t1_sb, 1, 0, HALF)
+        finish(h01[:].rearrange("p s f n t -> p (s f n t)"), 0, 2 * SLICE, planes[:, N:], (6, 7, 0))
         h2 = placed([P, HALVES, HALF, PACK], BF16, "h2", FIRST_ROOM + 2048)
-        product(h2, t2, damp[2], 0)
-        product(h1, t1, damp[1], 1)
-        t3 = template(3, 2)
-        product(h2, t2, damp[2], 1)
-        finish(h1[:].rearrange(flat), SLICE, SLICE, planes[:, N + SLICE :], (0, 0, 1))
-        h3 = placed([P, HALVES, HALF, PACK], BF16, "h3_late", SECOND_ROOM + 1024)
-        late_sc = placed([P, 2 * SLICE], U8, "late_sc", SECOND_ROOM)
+        for hf in range(HALVES):
+            product(h2, t2, damp[2], hf)
+        h3 = sbuf([P, HALVES, HALF, PACK], BF16, "h3")
+        late_sc = sbuf([P, 2 * SLICE], U8, "late_sc")
         product(h3, t3, damp[3], 0)
-        finish(h2[:].rearrange(flat), 2 * SLICE, SLICE, late_sc[:, 0:SLICE], (6, 6, 7))
+        finish(h2[:].rearrange(flat), 2 * SLICE, SLICE, late_sc[:, 0:SLICE], (1, 1, 4))
         product(h3, t3, damp[3], 1)
         scales = [late_sc[:, SLICE + hf * HALF : SLICE + (hf + 1) * HALF] for hf in range(HALVES)]
         for hf in range(HALVES):
             first = 3 * SLICE + hf * HALF
             quantise(h_codes[:, first : first + HALF], scales[hf], h3[:, hf].rearrange("p n t -> p (n t)"))
-        for hf, banks in enumerate(((4, 4, 5), (0, 0, 1))):
+        for hf, banks in enumerate(((5, 5, 6), (7, 7, 0))):
             readout(3 * SLICE + hf * HALF, HALF, scales[hf], banks, (2,), False)

@@ -58,7 +58,8 @@ def tile_list_template_contact_readout_kernel(
         w3_raw = placed([P, PASSES, H], I32, "w3_raw", THIRD_ROOM)
         w2_sc_raw = sbuf([P, PASSES, H // 4], I32, "w2_sc_raw")
         w3_sc_raw = sbuf([P, PASSES, H // 4], I32, "w3_sc_raw")
-        wo_raw = sbuf([P, PACK, N], F32, "wo_raw")
+        wo_raw = sbuf([P, PACK, 2 * P], F32, "wo_raw")
+        wo_raw_last = sbuf([P, PACK, P], F32, "wo_raw_last")
         bias = sbuf([P, N_TILES], F32, "bias")
         v_sc = {u: sbuf([P, S], U8, f"v_sc{u}") for u in (FIRST, SECOND)}
         second_sc_pass1 = sbuf([P, S // 4], I32, "second_sc_pass1")
@@ -257,11 +258,13 @@ def tile_list_template_contact_readout_kernel(
         load_weight_scales(nc.sync, w3_scales, w3_sc_raw)
         wo_rows = wo.rearrange("(g t i) n -> t g i n", t=PACK, i=8)
         for t in range(PACK):
-            nc.sync.dma_start(wo_raw[:, t, :], wo_rows[t])
+            nc.sync.dma_start(wo_raw[:, t, :], wo_rows[t][:, :, 0 : 2 * P])
         for q in range(QUADRANTS):
             nc.sync.dma_start(
                 template_sc[32 * q : 32 * q + ROWS, :, :], template_rows[8 * q : 8 * q + 8, :].bitcast(I32)
             )
+        for t in range(PACK):
+            nc.sync.dma_start(wo_raw_last[:, t, :], wo_rows[t][:, :, 2 * P : N])
         with nc.allow_non_contiguous_dma(reason="one bias value for each partition and output tile"):
             nc.sync.dma_start(bias[:], b.rearrange("(c p) -> p c", p=P))
 
@@ -302,8 +305,9 @@ def tile_list_template_contact_readout_kernel(
             quantise(w1_codes[:, a, :], w1_sc[:, a, :], w1_bf[a][:])
         reorder(nc.scalar.copy, w3_codes, w3_raw, 8)
         reorder(nc.gpsimd.tensor_copy, w3_sc, w3_sc_raw, 2)
-        wo_bf = sbuf([P, N, PACK], BF16, "wo_bf", "w1_bf1")
-        nc.gpsimd.tensor_scalar(wo_bf[:], wo_raw[:].rearrange("p t n -> p n t"), 1.0, 0.0, MULT, ADD)
+        wo_bf = sbuf([P, 2 * P, PACK], BF16, "wo_bf", "w1_bf1")
+        shared = wo_raw[:].rearrange("p t n -> p n t")
+        nc.gpsimd.tensor_scalar(wo_bf[:], shared, 1.0, 0.0, MULT, ADD)
         early, late = d_order[:2], d_order[2:]
         for s in range(3):
             open_d(s, 2 * s)
@@ -322,8 +326,9 @@ def tile_list_template_contact_readout_kernel(
         wanted = [(TEMPLATE, 0, (0,)), (TEMPLATE, 1, (0,))] + [(*pair, (3,)) for pair in late]
         wanted += [(TEMPLATE, 0, (1, 2, 3)), (TEMPLATE, 1, (1,)), (TEMPLATE, 1, (2, 3))]
         gather_words("middle", None, wanted, THIRD_ROOM + 2560)
-        for s in range(3):
-            roots[s] = root_of(s)
+        roots[0] = root_of(0)
+        roots[1] = root_of(1)
+        roots[2] = root_of(2)
         open_d(3, 0)
         for pair in early:
             d_passes(pair, 3)
@@ -335,6 +340,11 @@ def tile_list_template_contact_readout_kernel(
         t0_sb = copy_out("t0_sb", t0, (0, 1), FIRST_ROOM)
         h01 = sbuf([P, 2, HALVES, HALF, PACK], BF16, "h01")
         product_on_gpsimd(h01[:, 0], t0_sb, 0, 0, SLICE)
+        wo_bf_last = sbuf([P, P, PACK], BF16, "wo_bf_last")
+        nc.scalar.copy(
+            wo_bf_last[:].rearrange("p (c i) t -> p c t i", i=4),
+            wo_raw_last[:].rearrange("p t (c i) -> p c t i", i=4),
+        )
         damp_on_scalar(2)
         for pair in late:
             d_passes(pair, 3)
@@ -348,8 +358,8 @@ def tile_list_template_contact_readout_kernel(
         t3 = template(3, 2)
         planes = placed([P, N + 2 * SLICE], U8, "planes", FIRST_ROOM)
         wo_sc = planes[:, 0:N]
-        for cols in (slice(0, 2 * P), slice(2 * P, N)):
-            quantise(wo_codes[:, cols], wo_sc[:, cols], wo_bf[:, cols, :].rearrange("p n t -> p (n t)"))
+        for cols, values in ((slice(0, 2 * P), wo_bf), (slice(2 * P, N), wo_bf_last)):
+            quantise(wo_codes[:, cols], wo_sc[:, cols], values[:].rearrange("p n t -> p (n t)"))
         finish(h01[:].rearrange("p s f n t -> p (s f n t)"), 0, 2 * SLICE, planes[:, N:], (6, 7, 0))
         h2 = placed([P, HALVES, HALF, PACK], BF16, "h2", FIRST_ROOM + 2048)
         for hf in range(HALVES):

from contextlib import ExitStack

import concourse.mybir as mybir

K, H, N, T, S = 1024, 512, 384, 2048, 1024
FLOPS = 2 * (3 * K * H + H * N) * S

F32 = mybir.dt.float32
BF16 = mybir.dt.bfloat16
I32 = mybir.dt.int32
U32 = mybir.dt.uint32
U16 = mybir.dt.uint16
U8 = mybir.dt.uint8
FP8X4 = mybir.dt.float8_e4m3fn_x4
FP4X4 = mybir.dt.float4_e2m1fn_x4
ACT = mybir.ActivationFunctionType
MULT = mybir.AluOpType.mult
ADD = mybir.AluOpType.add

P = 128
PACK = 4
PASSES = K // (P * PACK)
SLICE = 256
HALF = 128
SLICES = S // SLICE
HALVES = SLICE // HALF
N_TILES = N // P
QUADRANTS = 4
ROWS = 4
LOWER = 4
FIRST_ROOM, SECOND_ROOM, THIRD_ROOM = 0, 4096, 8192
FIRST, SECOND, TEMPLATE = 0, 1, 2


def tile_list_template_contact_readout_kernel(
    tc, tab_words, tab_scales, offs, offs2, offs3, w1, w2_words, w2_scales, w3_words, w3_scales, wo, b, out
):
    nc = tc.nc
    with ExitStack() as ctx:
        keep = ctx.enter_context(tc.tile_pool(name="keep", bufs=1))
        over = ctx.enter_context(tc.tile_pool(name="over", bufs=1))
        psum = ctx.enter_context(tc.psum_pool(name="psum", bufs=1))

        def sbuf(shape, dtype, name, tag=None):
            return keep.tile(shape, dtype, name=name, tag=tag or name, align_bytes=64)

        def placed(shape, dtype, name, offset):
            return over.tile(shape, dtype, name=name, align_bytes=64, offset=offset)

        lists = [keep.tile([P, S // 16], U16, name=f"list{u}") for u in range(3)]
        tab_w = [sbuf([P, T], U32, f"tab_w{a}") for a in range(PASSES)]
        tab_sc = sbuf([P, T // 4], I32, "tab_sc")
        tab_rows = sbuf([P, T // 4], I32, "tab_rows")
        template_rows = sbuf([P, S // 2], U8, "template_rows")
        template_sc = sbuf([P, PASSES, S // 8], I32, "template_sc")
        w1_raw = [sbuf([P, PACK, H], F32, f"w1_raw{a}") for a in range(PASSES)]
        w2_raw = sbuf([P, PASSES, H // 2], I32, "w2_raw")
        w3_raw = placed([P, PASSES, H], I32, "w3_raw", THIRD_ROOM)
        w2_sc_raw = sbuf([P, PASSES, H // 4], I32, "w2_sc_raw")
        w3_sc_raw = sbuf([P, PASSES, H // 4], I32, "w3_sc_raw")
        wo_raw = sbuf([P, PACK, 2 * P], F32, "wo_raw")
        wo_raw_last = sbuf([P, PACK, P], F32, "wo_raw_last")
        bias = sbuf([P, N_TILES], F32, "bias")
        v_sc = {u: sbuf([P, S], U8, f"v_sc{u}") for u in (FIRST, SECOND)}
        second_sc_pass1 = sbuf([P, S // 4], I32, "second_sc_pass1")
        warm_in = sbuf([P, 1], F32, "warm_in")
        warm_out = sbuf([P, 1], F32, "warm_out")

        nc.gpsimd.memset(tab_sc[:], 0)
        nc.vector.memset(tab_rows[32:64, :], 0)
        nc.vector.memset(tab_rows[64:P, :], 0)
        nc.gpsimd.memset(warm_in[:], 1.0)
        nc.scalar.activation(warm_out[:], warm_in[:], ACT.Abs_reciprocal_sqrt)

        def load_table_words(a):
            nc.sync.dma_start(tab_w[a][:].bitcast(I32), tab_words[a].rearrange("p t i -> p (t i)").bitcast(I32))

        def load_w1(a):
            rows = w1[a * P * PACK : (a + 1) * P * PACK, :].rearrange("(p i) c -> p i c", i=PACK)
            nc.sync.dma_start(w1_raw[a][:], rows)

        def load_weight_scales(queue, scales, raw):
            for r in range(ROWS):
                queue.dma_start(raw[r:P:32, :, :], scales[:, r:16:ROWS, :].rearrange("a q c -> q a c").bitcast(I32))

        def gather_scales(u):
            nc.vector.tensor_copy(v_sc[u][:], tab_sc[:].bitcast(U8).indirect(lists[u][:]))

        v_words = {}

        def gather_words(name, tag, wanted, offset=None):
            cols = SLICE // 16
            shape = [P, SLICE * sum(len(slices) for u, a, slices in wanted)]
            tile = sbuf(shape, U32, name, tag) if offset is None else placed(shape, U32, name, offset)
            place = 0
            for u, a, slices in wanted:
                offsets = lists[u][:, slices[0] * cols : (slices[-1] + 1) * cols]
                nc.vector.tensor_copy(tile[:, place : place + len(slices) * SLICE], tab_w[a][:].indirect(offsets))
                for s in slices:
                    v_words[u, a, s] = tile[:, place : place + SLICE]
                    place += SLICE

        def moving_scale(u, a, cols):
            if u == SECOND and a == 1:
                return second_sc_pass1[:].bitcast(U8)[:, cols]
            if u == TEMPLATE:
                if cols.start < S // 2:
                    return template_first[LOWER * a : P, cols]
                return template_sc[:, a, :].bitcast(U8)[:, cols.start - S // 2 : cols.stop - S // 2]
            return v_sc[u][LOWER * a : P, cols]

        w1_bf = [sbuf([P, PACK * H], BF16, f"w1_bf{a}") for a in range(PASSES)]
        w1_codes = sbuf([P, PASSES, H], U32, "w1_codes")
        w1_sc = sbuf([P, PASSES, H], U8, "w1_sc")

        def round_w1(a):
            src = w1_raw[a][:].rearrange("p j (g t c i) -> p t g c j i", t=PACK, c=2, i=4)
            dst = w1_bf[a][:].rearrange("p (t g c i j) -> p t g c j i", t=PACK, c=2, i=4, j=PACK)
            for t in range(PACK - 1):
                nc.scalar.copy(dst[:, t], src[:, t])
            src = w1_raw[a][:].rearrange("p j (g t i) -> p t g i j", t=PACK, i=8)
            dst = w1_bf[a][:].rearrange("p (t g i j) -> p t g i j", t=PACK, i=8, j=PACK)
            nc.gpsimd.tensor_scalar(dst[:, PACK - 1], src[:, PACK - 1], 1.0, 0.0, MULT, ADD)

        def quantise(codes, scale, values):
            nc.vector.quantize_mx(codes.bitcast(FP8X4), scale, values)

        w2_codes = sbuf([P, PACK, PASSES, 2 * P], U8, "w2_codes")
        w3_codes = sbuf([P, PACK, PASSES, P], U32, "w3_codes")
        w3_sc = sbuf([P, PACK, PASSES, P], U8, "w3_sc")
        w2_sc = sbuf([P, PACK, PASSES, P], U8, "w2_sc")

        def reorder(copy, dst, src, run):
            copy(
                dst[:].bitcast(U32).rearrange("p t a (g e) -> p t (a g) e", e=run),
                src[:].bitcast(U32).rearrange("p a (g t e) -> p t (a g) e", t=PACK, e=run),
            )

        def weight(u, a, t):
            if u == FIRST:
                cols = slice(t * P, (t + 1) * P)
                return w1_codes[:, a, cols].bitcast(FP8X4), w1_sc[:, a, cols]
            if u == SECOND:
                return w2_codes[:, t, a, :].bitcast(FP4X4), w2_sc[:, t, a, :]
            return w3_codes[:, t, a, :].bitcast(FP8X4), w3_sc[:, t, a, :]

        def one_pass(dst, u, a, t, s, local, start, stop):
            codes, scale = weight(u, a, t)
            nc.tensor.matmul_mx(
                dst,
                lhsT=codes,
                lhsT_scale=scale,
                rhs=v_words[u, a, s][:, local].bitcast(FP8X4),
                rhs_scale=moving_scale(u, a, slice(s * SLICE + local.start, s * SLICE + local.stop)),
                start=start,
                stop=stop,
            )

        d_banks = {}
        d_order = ((SECOND, 0), (FIRST, 0), (SECOND, 1), (FIRST, 1))

        def open_d(s, bank):
            d_banks[s] = [psum.tile([P, 2, SLICE], F32, name=f"bank{bank + m}") for m in range(2)]

        def d_passes(pair, *slices, order=(d_order[0], d_order[-1])):
            for s in slices:
                for t in range(PACK):
                    m, e = divmod(t, 2)
                    first = pair == order[0] and e == 0
                    last = pair == order[1] and e == 1
                    one_pass(d_banks[s][m][:, e, :], *pair, t, s, slice(0, SLICE), first, last)

        def template(s, bank):
            banks = [psum.tile([P, PACK, HALF], F32, name=f"bank{bank + hf}") for hf in range(HALVES)]
            for a in range(PASSES):
                for hf in range(HALVES):
                    for t in range(PACK):
                        local = slice(hf * HALF, (hf + 1) * HALF)
                        first = a == 0 and t == 0
                        last = a == PASSES - 1 and t == PACK - 1
                        one_pass(banks[hf][:, t, :], TEMPLATE, a, t, s, local, first, last)
            return banks

        def root_of(s):
            square = sbuf([P, 2, SLICE, 2], F32, f"square{s}", f"square{s % 2}")
            root = sbuf([P, 2, SLICE, 2], F32, f"root{s}")
            for m in range(2):
                nc.scalar.activation(square[:, m], d_banks[s][m][:].rearrange("p e n -> p n e"), ACT.Square)
            for m in range(2):
                nc.scalar.activation(root[:, m], square[:, m], ACT.Abs_reciprocal_sqrt, bias=1.0)
            return root

        def by_entry(damp, first, count):
            return damp[:, :, first : first + count, :].rearrange("p m n e -> p n m e")

        def product(h, banks, damp, hf):
            nc.vector.tensor_tensor(
                h[:, hf].rearrange("p n (m e) -> p n m e", e=2),
                banks[hf][:].rearrange("p (m e) n -> p n m e", e=2),
                by_entry(damp, hf * HALF, HALF),
                MULT,
            )

        out_view = out.rearrange("(c p) j -> p c j", p=P)
        h_codes = sbuf([P, S], U32, "h_codes")

        def readout(first, width, scale, banks, vector_tiles, by_tile):
            result = sbuf([P, N_TILES, width], F32, f"result{first}")
            for bank in sorted(set(banks), key=banks.index):
                group = [c for c in range(N_TILES) if banks[c] == bank]
                y = psum.tile([P, len(group), width], F32, name=f"bank{bank}")
                for slot, c in enumerate(group):
                    nc.tensor.matmul_mx(
                        y[:, slot, :],
                        lhsT=wo_codes[:, c * P : (c + 1) * P].bitcast(FP8X4),
                        lhsT_scale=wo_sc[:, c * P : (c + 1) * P],
                        rhs=h_codes[:, first : first + width].bitcast(FP8X4),
                        rhs_scale=scale,
                        start=True,
                        stop=True,
                    )
                for slot, c in enumerate(group):
                    if c in vector_tiles:
                        nc.vector.tensor_scalar_add(result[:, c, :], y[:, slot, :], bias[:, c : c + 1])
                    else:
                        nc.scalar.activation(result[:, c, :], y[:, slot, :], ACT.Identity, bias=bias[:, c : c + 1])
                    if by_tile:
                        nc.sync.dma_start(out_view[:, c, first : first + width], result[:, c, :])
            if not by_tile:
                nc.sync.dma_start(out_view[:, :, first : first + width], result[:])

        nc.gpsimd.memset(w2_sc_raw[:], 0)
        nc.gpsimd.memset(second_sc_pass1[:], 0)
        nc.gpsimd.memset(w3_sc_raw[:], 0)
        nc.gpsimd.memset(template_sc[:], 0)
        nc.sync.dma_start(lists[TEMPLATE][:], offs3)
        nc.sync.dma_start(tab_rows[0:32, :], tab_scales.rearrange("a q t -> q a t").bitcast(I32))
        for q in range(QUADRANTS):
            nc.sync.dma_start(tab_sc[32 * q : 32 * q + 2 * LOWER, :], tab_scales[:, 4 * q : 4 * q + 4, :].bitcast(I32))
        nc.sync.dma_start(lists[SECOND][:], offs2)
        load_table_words(0)
        nc.sync.dma_start(lists[FIRST][:], offs)
        nc.sync.dma_start(w2_raw[:], w2_words.rearrange("a p c -> p a c").bitcast(I32))
        load_w1(0)
        load_weight_scales(nc.sync, w2_scales, w2_sc_raw)
        load_w1(1)
        reorder(nc.scalar.copy, w2_codes, w2_raw, 4)
        reorder(nc.gpsimd.tensor_copy, w2_sc, w2_sc_raw, 2)
        round_w1(0)
        round_w1(1)

        nc.vector.tensor_copy(template_rows[:], tab_rows[:].bitcast(U8).indirect(lists[TEMPLATE][:, S // 32 :]))
        gather_scales(SECOND)
        for r in range(ROWS):
            nc.sync.dma_start(second_sc_pass1[r:P:32, :], v_sc[SECOND][LOWER + r : P : 32, :].bitcast(I32))
        load_table_words(1)
        nc.sync.dma_start(w3_raw[:], w3_words.rearrange("a p c i -> p a (c i)").bitcast(I32))
        load_weight_scales(nc.sync, w3_scales, w3_sc_raw)
        wo_rows = wo.rearrange("(g t i) n -> t g i n", t=PACK, i=8)
        for t in range(PACK):
            nc.sync.dma_start(wo_raw[:, t, :], wo_rows[t][:, :, 0 : 2 * P])
        for q in range(QUADRANTS):
            nc.sync.dma_start(
                template_sc[32 * q : 32 * q + ROWS, :, :], template_rows[8 * q : 8 * q + 8, :].bitcast(I32)
            )
        for t in range(PACK):
            nc.sync.dma_start(wo_raw_last[:, t, :], wo_rows[t][:, :, 2 * P : N])
        with nc.allow_non_contiguous_dma(reason="one bias value for each partition and output tile"):
            nc.sync.dma_start(bias[:], b.rearrange("(c p) -> p c", p=P))

        wo_codes = sbuf([P, N], U32, "wo_codes")
        roots = {}
        damp = {}

        def damp_on_scalar(s):
            damp[s] = sbuf([P, 2, SLICE, 2], F32, f"damp{s}")
            for m in range(2):
                nc.scalar.activation(damp[s][:, m], roots[s][:, m], ACT.Square)

        def damp_on_gpsimd(s, tag=None):
            damp[s] = sbuf([P, 2, SLICE, 2], F32, f"damp{s}", tag)
            nc.gpsimd.tensor_tensor(damp[s][:], roots[s][:], roots[s][:], MULT)

        def copy_out(name, banks, halves, offset):
            tile = placed([P, len(halves), HALF, PACK], F32, name, offset)
            for place, hf in enumerate(halves):
                nc.scalar.copy(tile[:, place], banks[hf][:].rearrange("p t n -> p n t"))
            return tile

        def product_on_gpsimd(dst, copied, s, first, count):
            entries = "p f n (m e) -> p (f n) m e"
            nc.gpsimd.tensor_tensor(
                dst.rearrange(entries, e=2), copied[:].rearrange(entries, e=2), by_entry(damp[s], first, count), MULT
            )

        def finish(values, first, width, scale, banks, vector_tiles=(), by_tile=True):
            quantise(h_codes[:, first : first + width], scale, values)
            readout(first, width, scale, banks, vector_tiles, by_tile)

        flat = "p f n t -> p (f n t)"
        gather_words("second0", None, [(SECOND, 0, (0, 1, 2, 3))])
        gather_scales(FIRST)
        gather_words("first0", None, [(FIRST, 0, (0, 1))])
        for a in range(PASSES):
            quantise(w1_codes[:, a, :], w1_sc[:, a, :], w1_bf[a][:])
        reorder(nc.scalar.copy, w3_codes, w3_raw, 8)
        reorder(nc.gpsimd.tensor_copy, w3_sc, w3_sc_raw, 2)
        wo_bf = sbuf([P, 2 * P, PACK], BF16, "wo_bf", "w1_bf1")
        shared = wo_raw[:].rearrange("p t n -> p n t")
        nc.gpsimd.tensor_scalar(wo_bf[:], shared, 1.0, 0.0, MULT, ADD)
        early, late = d_order[:2], d_order[2:]
        for s in range(3):
            open_d(s, 2 * s)
        d_passes(early[0], 0, 1, 2)
        d_passes(early[1], 0, 1)
        gather_words("late_start", "w1_raw0", [(*late[0], (0,))])
        gather_words("late", "w1_raw1", [(*late[1], (0,))] + [(*pair, (1, 2)) for pair in late])
        gather_words("first0_rest", None, [(*early[1], (2, 3))], THIRD_ROOM)
        for s in (0, 1):
            for pair in late:
                d_passes(pair, s)
        for pair in late + early[1:]:
            d_passes(pair, 2, order=(early[0], early[1]))
        template_first = placed([P, S // 2], U8, "template_first", THIRD_ROOM + 2048)
        nc.vector.tensor_copy(template_first[:], tab_sc[:].bitcast(U8).indirect(lists[TEMPLATE][:, 0 : S // 32]))
        wanted = [(TEMPLATE, 0, (0,)), (TEMPLATE, 1, (0,))] + [(*pair, (3,)) for pair in late]
        wanted += [(TEMPLATE, 0, (1, 2, 3)), (TEMPLATE, 1, (1,)), (TEMPLATE, 1, (2, 3))]
        gather_words("middle", None, wanted, THIRD_ROOM + 2560)
        roots[0] = root_of(0)
        roots[1] = root_of(1)
        roots[2] = root_of(2)
        open_d(3, 0)
        for pair in early:
            d_passes(pair, 3)
        damp01 = sbuf([P, 2, 2, SLICE, 2], F32, "damp01", "wo_raw")
        for s in range(2):
            damp[s] = damp01[:, s]
            nc.gpsimd.tensor_tensor(damp[s], roots[s][:], roots[s][:], MULT)
        t0 = template(0, 6)
        t0_sb = copy_out("t0_sb", t0, (0, 1), FIRST_ROOM)
        h01 = sbuf([P, 2, HALVES, HALF, PACK], BF16, "h01")
        product_on_gpsimd(h01[:, 0], t0_sb, 0, 0, SLICE)
        wo_bf_last = sbuf([P, P, PACK], BF16, "wo_bf_last")
        nc.scalar.copy(
            wo_bf_last[:].rearrange("p (c i) t -> p c t i", i=4),
            wo_raw_last[:].rearrange("p t (c i) -> p c t i", i=4),
        )
        damp_on_scalar(2)
        for pair in late:
            d_passes(pair, 3)
        t1 = template(1, 2)
        roots[3] = root_of(3)
        damp_on_scalar(3)
        t2 = template(2, 4)

        for hf in range(HALVES):
            product(h01[:, 1], t1, damp[1], hf)
        t3 = template(3, 2)
        planes = placed([P, N + 2 * SLICE], U8, "planes", FIRST_ROOM)
        wo_sc = planes[:, 0:N]
        for cols, values in ((slice(0, 2 * P), wo_bf), (slice(2 * P, N), wo_bf_last)):
            quantise(wo_codes[:, cols], wo_sc[:, cols], values[:].rearrange("p n t -> p (n t)"))
        finish(h01[:].rearrange("p s f n t -> p (s f n t)"), 0, 2 * SLICE, planes[:, N:], (6, 7, 0))
        h2 = placed([P, HALVES, HALF, PACK], BF16, "h2", FIRST_ROOM + 2048)
        for hf in range(HALVES):
            product(h2, t2, damp[2], hf)
        h3 = sbuf([P, HALVES, HALF, PACK], BF16, "h3")
        late_sc = sbuf([P, 2 * SLICE], U8, "late_sc")
        product(h3, t3, damp[3], 0)
        finish(h2[:].rearrange(flat), 2 * SLICE, SLICE, late_sc[:, 0:SLICE], (1, 1, 4))
        product(h3, t3, damp[3], 1)
        scales = [late_sc[:, SLICE + hf * HALF : SLICE + (hf + 1) * HALF] for hf in range(HALVES)]
        for hf in range(HALVES):
            first = 3 * SLICE + hf * HALF
            quantise(h_codes[:, first : first + HALF], scales[hf], h3[:, hf].rearrange("p n t -> p (n t)"))
        for hf, banks in enumerate(((5, 5, 6), (7, 7, 0))):
            readout(3 * SLICE + hf * HALF, HALF, scales[hf], banks, (2,), False)
